import numpy as np, ml_dtypes
CORES = [10,34,74,98]
N = 4
BF = ml_dtypes.bfloat16
def gentries(a):
    return np.ascontiguousarray(a.reshape(8, 16, -1).transpose(0, 2, 1)).reshape(8, -1)
def gtable(e):
    e = np.asarray(e); return np.ascontiguousarray(e.reshape(8, -1, 16).transpose(0, 2, 1)).reshape(128, -1).astype(np.int32)
def f(rng, *shape):
    return (rng.standard_normal(shape, dtype=np.float32) * np.exp2(rng.integers(-2, 3, shape[:-1] + (1,)))).astype(BF)
def wide(rng, *shape):
    v = f(rng, *shape).astype(np.float32); k = shape[:-2] + (1, shape[-1])
    return (v * np.exp2(rng.integers(-6, 7, k)) * (rng.random(k) > 0.0625)).astype(BF)
W, C, D, B, R, K = 8192, 2048, 5, 2, 8, 37
def ints(x):
    return np.clip(np.rint(x), -32768, 32768).astype(BF)
def cols(fr, ix):
    return np.take_along_axis(fr.reshape(N, 8, 16, W), ix[None, :, None, :], 3).astype(np.float32).astype(np.int64)
def limits(rng, fr):
    m = 512; lim = np.zeros((8, 16, D), np.int64); s = cols(fr, rng.integers(0, W, (8, m)))
    for l in range(D):
        s = s + cols(fr, rng.integers(0, W, (8, m))); en = np.sum(np.abs(s), axis=(0, 2)); o = np.argsort(en, axis=1)
        lim[:, :, l] = np.take_along_axis(np.take_along_axis(en, o, 1), rng.integers(m // 5, 4 * m // 5, (8, 16)), 1)
        s = np.take_along_axis(s, o[:, rng.integers(0, m // 2, m)][None, :, None, :], 3)
    return lim
def parts(rng):
    fr = ints(f(rng, N, 128, W).astype(np.float32) * 1024)
    return fr, rng.integers(0, W, (8, W)), rng.integers(0, W, (8, C))
def pack(fr, first, start, lim):
    return {"frag": fr, "first": np.stack([first.astype(np.int32)] * N), "start": np.stack([gtable(start)] * N), "lim": np.stack([lim.reshape(128, D).astype(np.int32)] * N)}
def setup_inputs(rng):
    fr, first, start = parts(rng)
    return pack(fr, first, start, limits(rng, fr))
def setup_inputs_ties(rng):
    fr, first, start = parts(rng); x = fr.reshape(N, 8, 16, W)
    x[:, ::2] = (4096 * rng.integers(-1, 2, (N, 4, 16, W))).astype(np.float32).astype(BF)
    x[..., 0] = 0; x[..., W - 1] = 0; x[..., 5] = -x[..., 7]
    first[:, 0] = W - 1; first[:, W - 1] = 0; first[:, 5] = 7; start[::2, 15::32] = 0; start[::2, 14::32] = 5
    lim = limits(rng, fr); lim[::2] = np.maximum(lim[::2] - rng.integers(0, 2, (4, 16, D)), 0)
    lim[::2, 15] = 0; lim[::2, 14, 0] = 0
    s = cols(fr, start[:, :16]) + cols(fr, np.take_along_axis(first, start[:, :16], 1)); en = np.sum(np.abs(s), axis=(0, 2))
    lim[1::2, :, 0] = np.maximum(en - (np.arange(16) & 1), 0)[1::2]
    return pack(fr, first, start, lim)
def setup_inputs_walls(rng):
    fr, first, start = parts(rng); lim = limits(rng, fr)
    m = ((np.arange(16)[None, :] + rng.integers(0, 16, (8, 1))) % (D + 1))[:, :, None]; lv = np.arange(D)[None, None, :]
    lim = np.where((lv < m) & (rng.random((8, 16, 1)) < 0.6), 2 ** 24 - 1, lim)
    return pack(fr, first, start, np.where(lv == m, 0, lim))
def setup_inputs_alike(rng):
    fr, first, start = parts(rng); lim = limits(rng, fr)
    start[::2] = rng.choice(np.array([0, W - 1, W // 2, 3]), (4, C))
    first[1] = np.arange(W); first[2] = rng.choice(np.array([0, W - 1, W - K, W - K - 1, W - K + 1]), W)
    first[4] = np.where(rng.random(W) < 0.5, W - K, first[4]); first[5] = W - 1 - rng.integers(0, K, W); start[6, ::2] = W - 1
    return pack(fr, first, start, lim)
def setup_inputs_ends(rng):
    fr, first, start = parts(rng); x = fr.reshape(N, 8, 16, W); lv = np.arange(1, D + 1)[None, :]; odd = (np.arange(16) & 1)[:, None]
    x[:, 3] = (32768 * (2 * rng.integers(0, 2, (N, 16, 1)) - 1) * np.where(rng.random(W) < 0.9, 1, -1)).astype(np.float32).astype(BF)
    x[:, 4::3] = np.where(rng.random((N, 2, 16, W)) < 0.5, rng.integers(-255, 256, (N, 2, 16, W)), rng.choice(np.array([-32768, 32768]), (N, 2, 16, W))).astype(np.float32).astype(BF)
    x[:, 5] = rng.integers(-255, 256, (N, 16, W)).astype(np.float32).astype(BF)
    x[int(rng.integers(0, N)), 5] = (32768 * (2 * rng.integers(0, 2, (16, 1)) - 1)).astype(np.float32).astype(BF)
    lim = limits(rng, fr)
    lim[0] = 0; lim[1] = 2 ** 24 - 1; lim[2] = 2 ** 24 - 1; lim[2, :, D - 1] = 0; lim[7, :2] = 2 ** 24 - 1
    lim[3] = 2 ** 21 * (lv + 1) - odd * (lv >= 4)
    lim[5] = 2 ** 19 * (lv + 1) + 2 ** 17
    lim[5, ::2, 3] = rng.integers(2 ** 21 + 2 ** 17, 5 * 2 ** 19, 8)
    if D > 4: lim[5, 1::2, 4] = rng.integers(2 ** 21 + 2 ** 17, 6 * 2 ** 19, 8)
    s = cols(fr, start) + cols(fr, np.take_along_axis(first, start, 1)); sh = np.sum(np.abs(s[:, 4]), axis=1)
    hi = sh.astype(np.float32).astype(BF).astype(np.float64); lo = (sh - hi).astype(np.float32).astype(BF).astype(np.float64); er = np.sum(hi + lo - sh, axis=0)
    for i in range(16):
        c = i + 16 * int(np.argmin(er[i::16]) if i & 1 else np.argmax(er[i::16]))
        lim[4, i, 0] = np.sum(sh[:, c]) - (i & 1)
    return pack(fr, first, start, lim)
def setup_inputs_spread(rng):
    fr, first, start = parts(rng); fr = ints(wide(rng, N, 128, W).astype(np.float32) * 32)
    return pack(fr, first, start, limits(rng, fr))
def check_inputs(d):
    bad = []; v = np.asarray(d["frag"]).astype(np.float32)
    if not np.all((np.abs(v) <= 32768) & (np.rint(v) == v)): bad.append("frag: whole numbers from -32768 to 32768")
    for k, hi in (("first", W - 1), ("start", W - 1), ("lim", 2 ** 24 - 1)):
        if np.min(d[k]) < 0 or np.max(d[k]) > hi: bad.append("range of " + k)
        if np.any(d[k] != d[k][:1]): bad.append(k + " is not alike on all ranks")
    return bad
def reference(frag, first, start, lim):
    fr = frag.astype(np.float32).astype(np.int32).reshape(N, 8, 16, W).transpose(1, 3, 0, 2).reshape(8, W, 16 * N)
    fi = first[0].astype(np.int64); lm = lim[0].astype(np.int64).reshape(8, 16, D)
    M = 8 * C; a = np.arange(M); g = np.repeat(np.arange(8), C); cl = np.tile(np.arange(C) & 15, 8)
    V = np.zeros((M, D + 1), np.int64); Q = np.zeros((M, D + 1), np.int64); S = np.zeros((M, D + 1, 16 * N), np.int32); d = np.zeros(M, np.int64)
    V[:, 0] = gentries(start[0]).reshape(-1); S[:, 0] = fr[g, V[:, 0]]
    for rnd in range(R):
        v = V[a, d]; b = Q[a, d]; live = d < D
        w = (fi[g, v] + K * b) & (W - 1)
        s = S[a, d] + fr[g, w]; en = np.sum(np.abs(s), axis=1); up = np.minimum(d + 1, D)
        go = live & (b < B) & (en <= lm[g, cl, up - 1]); no = live & (b < B) & ~go
        back = live & (b == B) & (d > 0); anew = live & (b == B) & (d == 0)
        Q[a[no], d[no]] += 1
        Q[a[anew], 0] = 0
        Q[a[back], d[back] - 1] += 1
        V[a[go], up[go]] = w[go]; Q[a[go], up[go]] = 0; S[a[go], up[go]] = s[go]
        d = d + go.astype(np.int64) - back.astype(np.int64)
    y = S[a, d].reshape(8, C, N, 16).transpose(2, 0, 3, 1).reshape(N, 128, C)
    t = np.where(np.arange(D + 1)[None, :] <= d[:, None], 16 * V + Q, -1).reshape(8, C, D + 1).transpose(0, 2, 1).reshape(8, -1)
    return {"y": np.ascontiguousarray(y).astype(np.float32), "stk": np.stack([gtable(t)] * N).astype(np.float32)}

@@ -1,0 +1,651 @@
+from concourse.bass import DstId, RemoteDMATransfer
+from concourse.mybir import AluOpType as A, ActivationFunctionType as F
+
+NR, CH, W, K, NS = 4, 512, 8192, 37, 5
+AO = 48
+f32, bf16, i32, u16 = "float32", "bfloat16", "int32", "uint16"
+
+_SB = {"fr": (8240, bf16), "ax": (8240, bf16), "fi": (512, i32), "hl": (1024, bf16), "sti": (128, i32), "stu": (128, u16),
+       "limi": (8, i32), "limf": (8, f32), "gx": (1280, bf16), "l0": (128, u16), "ls": (1024, u16), "lw": (640, u16),
+       "yu": (128, u16), "sb": (1280, f32), "rv": (1280, f32), "es": (384, f32), "fin": (512, f32), "pi": (8, i32),
+       "ci": (8, i32), "cf": (16, f32), "x144": (144, f32), "x96": (384, f32), "x4": (128, f32), "x16": (32, f32),
+       "bo": (8, f32), "m0": (144, bf16), "m1": (144, bf16), "mk": (4, f32), "rc0": (384, bf16), "rc1": (384, bf16),
+       "lq": (128, f32), "gq": (32, f32), "lr": (160, f32), "lz": (160, f32), "dl": (128, f32), "pre": (64, f32),
+       "ta": (64, f32), "tb": (64, f32), "te": (64, f32), "d1": (192, f32), "d4": (768, f32), "d5": (384, f32),
+       "so": (768, f32), "s4": (768, f32), "s5": (384, f32), "nb": (384, f32), "pb": (160, f32), "v": (3584, f32)}
+SCRATCH = {k: ("sbuf", [128, n], d) for k, (n, d) in _SB.items()}
+SCRATCH.update({"stb": ("sbuf", [128, 6, 128], f32), "lx": ("sbuf", [128, 16, 4, 4], bf16),
+                "pc": ("psum", [128, 512], f32), "pa": ("psum", [128, 512], f32), "pl": ("psum", [128, 512], f32)})
+for _k in range(NR):
+    SCRATCH["xs%d" % _k] = ("sbuf", [128, 11 * CH], f32)
+    SCRATCH["st%d" % _k] = ("sbuf", [128, CH], f32)
+    SCRATCH["ab%d" % _k] = ("sbuf", [128, 2 * CH], f32)
+    SCRATCH["pe%d" % _k] = ("psum", [128, 512], f32)
+
+SEMAPHORES = (["qV", "qS", "qP", "qG", "sent", "dfi", "dst", "dlim", "dfa", "dfb", "dax", "dk0", "dk1", "ini"]
+              + ["dy%d" % k for k in range(NR)] + ["sh%d" % t for t in range(1, 6)]
+              + ["li%d_%d" % (t, k) for t in range(1, 6) for k in range(NR)] + ["ea%d" % k for k in range(NR)])
+
+PLAN = {"cyc": 0.9e-3, "gth": 1.56, "fix": 0.05, "pe": 0.52e-3, "sem": 0.05, "issue": 0.6, "start": 2.3, "rows": 1.0,
+        "dma": 1.9, "bw": 240e3, "first": 2.0, "slack": 0.0, "ev": 0}
+PRI = {"Vd": 2.5, "Vsl": 1, "Vs": -8, "Vrz": -8, "Sd": 8, "Vtb": -0.5}
+
+
+def record(g, r, T, topo):
+    cores = list(T.cores)
+    others = [k for k in range(NR) if k != r]
+    Q = {"V": g.vector, "S": g.scalar, "P": g.tensor, "G": g, "Y": g.sync}
+    V, S, P = g.vector, g.scalar, g.tensor
+    ops, ext = [], {}
+    cyc, GA, H = PLAN["cyc"], PLAN["gth"], CH // 2
+
+    def add(q, fn, rd, wr, cost, sem=None, inc=16, to=None):
+        ops.append({"q": q, "fn": fn, "rd": list(rd), "wr": list(wr), "cost": cost, "sem": sem, "inc": inc, "to": to, "r": r})
+
+    def cost(n, m=1.0):
+        return PLAN["fix"] + max(64, n * m) * cyc
+
+    def tt(o, a, b, op, rd, wr, n=32, m=2.0):
+        add("V", lambda: V.tensor_tensor(o, a, b, op), rd, wr, cost(n, m))
+
+    def ts(o, a, s1, op0, rd, wr, s2=None, op1=None, n=32):
+        if op1 is None:
+            add("V", lambda: V.tensor_scalar(o, a, s1, None, op0), rd, wr, cost(n))
+        else:
+            add("V", lambda: V.tensor_scalar(o, a, s1, s2, op0, op1), rd, wr, cost(n))
+
+    def cp(o, a, rd, wr, n=32, m=1.0):
+        add("V", lambda: V.tensor_copy(o, a), rd, wr, cost(n, m))
+
+    def act(o, a, f, rd, wr, n=32, m=1.0):
+        add("S", lambda: S.activation(o, a, f), rd, wr, cost(n, m))
+
+    def affine(o, a, scale, bias, rd, wr):
+        add("S", lambda: S.activation(o, a, F.Identity, bias=bias, scale=scale), rd, wr, cost(32))
+
+    def mm(o, l, rh, s0, s1, rd, wr, n=64):
+        add("P", lambda: P.matmul(o, l, rh, s0, s1), rd, wr, n * PLAN["pe"])
+
+    def mset(o, c, wr, n=32):
+        add("V", lambda: V.memset(o, c), (), wr, cost(n))
+
+    def scan(o, d0, d1, rd, wr, n=96):
+        add("V", lambda: V.tensor_tensor_scan(o, d0, d1, 0.0, A.mult, A.add), rd, wr, cost(n))
+
+    def dma(q, o, a, sem, rd, wr, size):
+        add(q, lambda: Q[q].dma_start(o, a), rd, wr, 0.3 + size / PLAN["bw"], sem=sem)
+
+    def both(k, ranks):
+        mask = -1
+        for j in ranks:
+            mask &= topo.mask(cores[k], cores[j])
+        return mask
+
+    def nin(k, ranks):
+        return bin(both(k, ranks)).count("1")
+
+    def send(ap_out, ap_in, ranks, sem, rd, more=0.0):
+        mask = both(r, ranks)
+        ad = [topo.addr(cores[k]) for k in ranks]
+        if len(ranks) == 1:
+            fn = lambda: g.remote_dma(ap_out, ap_in, T.sem[sem], T.sem.sent, ad[0][1], ad[0][0], mask)
+        else:
+            fn = lambda: g.remote_dma_fused([RemoteDMATransfer(
+                dst_ids=[DstId(rid=a[0], pnc=a[1]) for a in ad], dma_engine_mask=mask, remote_sem=T.sem[sem],
+                src=ap_in, dsts=[ap_out] * len(ranks))], local_sem=T.sem.sent)
+        add("G", fn, rd, (), PLAN["rows"] + more, sem="sent", inc=nin(r, ranks), to=(ranks, sem))
+
+    rest = lambda k: [j for j in range(NR) if j != k]
+    ring = [(r + i) % NR for i in range(1, NR)]
+    WA = 5 * W // 8
+
+    dma("Y", T.fi[:], T.first[:], "dfi", (), ["fi", "y0"], 2 ** 18)
+    dma("Y", T.sti[:], T.start[:], "dst", (), ["sti", "y0"], 2 ** 16)
+    dma("Y", T.fr[:, 0:WA], T.frag[:, 0:WA], "dfa", (), ["y0"], 256 * WA)
+    dma("Y", T.fr[:, W:W + K], T.frag[:, 0:K], "dfa", (), ["y0", "fra"], 2 ** 14)
+    dma("S", T.limi[:, 0:5], T.lim[:], "dlim", (), ["limi"], 2 ** 12)
+
+    def iota(o, pat, key):
+        add("G", lambda: g.iota(o, pat, 0, 0, allow_small_or_imprecise_dtypes=True), (), [key], 0.5)
+    add("G", lambda: g.iota(T.pi[:, 0:1], [[0, 1]], 0, 1), (), ["ip"], 0.13)
+    iota(T.x144[:], [[1, 144]], "x144")
+    iota(T.x4[:], [[0, 32], [1, 4]], "x4")
+    iota(T.x16[:], [[16, 32]], "x16")
+    iota(T.x96[:], [[0, 4], [1, 96]], "x96")
+
+    mset(T.ax[:, 0:2752], 0.0, ["ax0"], 1376)
+    act(T.ax[:, 2752:5504], T.ax[:, 0:2752], F.Copy, ["ax0"], ["ax1"], 2752)
+    mset(T.ax[:, 5504:8240], 0.0, ["ax2"], 1376)
+    cp(T.hl[:, 0:512], T.fi[:], ["fi"], ["hi"], 512)
+    tt(T.hl[:, 512:1024], T.fi[:], T.hl[:, 0:512], A.subtract, ["fi", "hi"], ["lo"], 512)
+    axk = ["ax0", "ax1", "ax2", "y0"]
+    for h in range(2):
+        key = ["hi", "lo"][h]
+        dma("Y", T.ax[h::16, AO:AO + W], T.hl[:, 512 * h:512 * h + 512], "dax", [key], axk, 2 ** 17)
+        dma("Y", T.ax[2 + h::16, AO - K:AO - K + W], T.hl[:, 512 * h:512 * h + 512], "dax", [key], axk, 2 ** 17)
+        dma("Y", T.ax[2 + h::16, AO - K + W:AO + W], T.hl[0::16, 512 * h:512 * h + K], "dax", [key], axk + ["ax"] * h, 2 ** 10)
+    dma("Y", T.fr[:, WA:W], T.frag[:, WA:W], "dfb", (), ["y0", "frb"], 256 * (W - WA))
+    cp(T.stu[:], T.sti[:], ["sti"], ["stu"], 128)
+
+    p0 = T.pi[:, 0:1]
+    ts(T.ci[:, 0:1], p0, 4, A.arith_shift_right, ["ip"], ["ci0"])
+    ts(T.ci[:, 1:2], p0, 15, A.bitwise_and, ["ip"], ["ci1"])
+    ts(T.ci[:, 2:3], p0, 3, A.bitwise_and, ["ip"], ["ci2"])
+    ts(T.ci[:, 3:4], p0, 2, A.arith_shift_right, ["ip"], ["ci3"])
+    ts(T.ci[:, 4:5], p0, 2, A.arith_shift_right, ["ip"], ["ci4"], 3, A.bitwise_and)
+    ts(T.ci[:, 5:6], p0, 1, A.arith_shift_right, ["ip"], ["ci5"], 7, A.bitwise_and)
+    cp(T.cf[:, 0:6], T.ci[:, 0:6], ["ci%d" % i for i in range(6)], ["cf"])
+    c = lambda i: T.cf[:, i:i + 1]
+    ts(c(6), c(0), 16.0, A.mult, ["cf"], ["c6"], 15.0, A.add)
+    ts(c(7), c(5), 0.0, A.is_equal, ["cf"], ["c7"])
+    ts(c(8), c(5), 1.0, A.is_equal, ["cf"], ["c8"])
+    ts(c(9), c(3), 3.0, A.mult, ["cf"], ["c9"], 1.0, A.add)
+    ts(c(10), c(3), 3.0, A.mult, ["cf"], ["c10"], 2.0, A.add)
+    ts(c(11), c(0), 4.0, A.mult, ["cf"], ["c11"], c(2), A.add)
+    ts(T.m0[:], T.x144[:], c(6), A.is_equal, ["x144", "c6", "c7"], ["m0"], c(7), A.mult, 144)
+    ts(T.m1[:], T.x144[:], c(6), A.is_equal, ["x144", "c6", "c8"], ["m1"], c(8), A.mult, 144)
+    ts(T.bo[:], T.x144[:, 0:8], c(0), A.is_equal, ["x144", "cf"], ["bo"])
+    ts(T.mk[:], T.x144[:, 0:4], c(2), A.is_equal, ["x144", "cf"], ["mk"])
+    ts(T.gq[:], T.x144[:, 0:32], c(11), A.is_equal, ["x144", "c11"], ["gq"])
+    ts(T.lq[:], T.x4[:], c(4), A.is_equal, ["x4", "cf"], ["lq"], n=128)
+    cp(T.limf[:, 0:5], T.limi[:, 0:5], ["limi"], ["limf"])
+    for l in range(5):
+        ts(T.lr[:, 32 * l:32 * l + 32], T.gq[:], T.limf[:, l:l + 1], A.mult, ["gq", "limf"], ["lr%d" % l])
+    mm(T.pl[:, 0:160], T.lq[:], T.lr[:], True, True, ["lq"] + ["lr%d" % l for l in range(5)], ["pl"], 640)
+    ts(T.rc0[:], T.x96[:], c(10), A.is_equal, ["x96", "c10"], ["rc0"], n=384)
+    ts(T.rc1[:], T.x96[:], c(9), A.is_equal, ["x96", "c9"], ["rc1"], n=384)
+    cp(T.lz[:], T.pl[:, 0:160], (), ["pl", "lz"], 160)
+    ts(T.x16[:], T.x16[:], c(1), A.add, ["x16", "cf"], ["x16"])
+    tt(T.dl[:], T.lz[:, 0:128], T.lz[:, 32:160], A.subtract, ["lz"], ["dl"], 128)
+    mset(T.d1[:, 96:192:3], -2.0 * CH, ["d1s"])
+    mset(T.d1[:, 97:192:3], 1.0 * CH, ["d1s"])
+    ts(T.d1[:, 98:192:3], T.x16[:], 1.0 * CH, A.add, ["x16"], ["d1s"])
+    mset(T.pb[:, 0:32], 0.0, ["b0"])
+
+    axw = T.ax[:, AO:AO + W]
+    frw = T.fr[:, 0:W + K]
+
+    def extract(n0, n, col, m, key, rd):
+        for i in range(16):
+            mm(T.pa[:, col:col + n // 16], m[:, 15 - i:143 - i], T.gx[:, n0 + i:n0 + n:16], i == 0, i == 15, rd + [key], ["pa"])
+
+    pc0 = 64 + 16 * r
+    cp(T.gx[:, 1024:1280], axw.indirect(T.stu[:, pc0:pc0 + 16]), ["ax", "stu"], ["gxc"], 256, GA)
+    act(T.gx[:, 0:512], axw.indirect(T.stu[:, 0:32]), F.Copy, ["ax", "stu"], ["gxa"], CH, GA)
+    cp(T.gx[:, 512:1024], axw.indirect(T.stu[:, 32:64]), ["ax", "stu"], ["gxb"], CH, GA)
+    extract(1024, 256, 64, T.m0, "m0", ["gxc"])
+    cp(T.l0[:, pc0:pc0 + 16], T.pa[:, 64:80], (), ["pa", "l0own"])
+    send(T.l0[:, pc0:pc0 + 16], T.l0[:, pc0:pc0 + 16], ring, "ini", ["l0own"])
+    extract(0, 1024, 0, T.m0, "m0", ["gxa", "gxb"])
+    cp(T.l0[:, 0:64], T.pa[:, 0:64], (), ["pa", "l0a"])
+    ext["l0in"] = ("ini", sum(nin(k, rest(k)) for k in others))
+    for t in range(1, NS + 1):
+        ext["rv%d" % t] = ("sh%d" % t, sum(nin(k, [r]) for k in others))
+        for k in others:
+            ext["ls%d_%d" % (t, k)] = ("li%d_%d" % (t, k), nin(k, rest(k)))
+    for k in others:
+        ext["es%d" % k] = ("ea%d" % k, nin(k, rest(k)))
+
+    place = {}
+
+    def vv(name, n=1, a=0, b=None):
+        if name not in place:
+            place[name] = sum(x[1] for x in place.values()), n
+        o = place[name][0]
+        return T.v[:, 32 * (o + a):32 * (o + (n if b is None else b))]
+
+    def wl(t, k, a, b):
+        if t == 1:
+            return T.l0[:, 32 * k + a:32 * k + b], (["l0a"] if k < 2 else ["l0own", "l0in"])
+        o = ((t - 2) * 4 + k) * 64
+        return T.ls[:, o + a:o + b], ["ls%d_%d" % (t - 1, k)]
+
+    def bulk(t, k):
+        xs, st, ab, pe = T["xs%d" % k], T["st%d" % k], T["ab%d" % k], T["pe%d" % k]
+        o1, x0, fk = ((t - 1) * 4 + k) * 32, (2 * t - 1) * CH, ["fra", "frb"]
+        xk = lambda s, h: "x%d_%d_%d" % (k, s, h)
+        top = lambda h: (xs[:, h * H:h * H + H], [xk(0, h)]) if t == 1 else (st[:, h * H:h * H + H], ["st%d_%d" % (k, h)])
+
+        def red(v, rd):
+            for q in range(4):
+                mm(pe[:, 32 * v + q:32 * v + 32:4], ab[:, v * CH + q:v * CH + CH:4], T.bo[:], True, True, rd + ["bo"], ["pe%d" % k], 256)
+        for h in range(2):
+            if t == 1:
+                act(top(h)[0], frw.indirect(T.stu[:, 32 * k + 16 * h:32 * k + 16 * h + 16]), F.Copy, fk + ["stu"], top(h)[1] + ["os"], H, GA)
+            else:
+                li, lk = wl(t, k, 32 + 16 * h, 48 + 16 * h)
+                act(top(h)[0], xs[:, (2 * t - 4) * CH:(2 * t - 1) * CH].indirect(li), F.Copy,
+                    lk + [xk(s, i) for s in range(2 * t - 4, 2 * t - 1) for i in range(2)], top(h)[1] + ["os"], H, GA)
+        li, lk = wl(t, k, 0, 32)
+        ts(T.lw[:, o1:o1 + 32], li, float(K), A.add, lk, ["lw%d_%d" % (t, k)])
+        for h in range(2):
+            li, lk = wl(t, k, 16 * h, 16 * h + 16)
+            tt(xs[:, x0 + h * H:x0 + h * H + H], frw.indirect(li), top(h)[0], A.add, fk + lk + top(h)[1], [xk(2 * t - 1, h), "ov"], H, GA)
+        act(ab[:, 0:CH], xs[:, x0:x0 + CH], F.Abs, [xk(2 * t - 1, 0), xk(2 * t - 1, 1)], ["a%d_0" % k], CH)
+        red(0, ["a%d_0" % k])
+        for h in range(2):
+            a = x0 + CH + h * H
+            tt(xs[:, a:a + H], frw.indirect(T.lw[:, o1 + 16 * h:o1 + 16 * h + 16]), top(h)[0], A.add,
+               fk + ["lw%d_%d" % (t, k)] + top(h)[1], [xk(2 * t, h), "ov"], H, GA)
+            act(ab[:, CH + h * H:CH + h * H + H], xs[:, a:a + H], F.Abs, [xk(2 * t, h)], ["a%d_1%d" % (k, h)], H)
+        red(1, ["a%d_10" % k, "a%d_11" % k])
+        if k != r:
+            o, o2, key = ((t - 1) * 4 + k) * 64, ((t - 1) * 4 + r) * 64, "sb%d_%d" % (t, k)
+            if PLAN["ev"]:
+                cp(T.sb[:, o:o + 64], pe[:, 0:64], (), ["pe%d" % k, key])
+            else:
+                act(T.sb[:, o:o + 64], pe[:, 0:64], F.Copy, (), ["pe%d" % k, key])
+            send(T.rv[:, o2:o2 + 64], T.sb[:, o:o + 64], [k], "sh%d" % t, [key])
+        else:
+            lim, lk = (T.lz[:, 32 * (t - 1):32 * t], ["lz"]) if t < 3 else (vv("tn"), ["tn"])
+            for v in range(2):
+                tt(T.pre[:, 32 * v:32 * v + 32], pe[:, 32 * v:32 * v + 32], lim, A.subtract, lk, ["pe%d" % k, "pre%d" % v])
+
+    def look(t):
+        li, lk = wl(t, r, 0, 32)
+        act(T.gx[:, 0:CH], axw.indirect(li), F.Copy, ["ax"] + lk, ["gxa"], CH, GA)
+        extract(0, CH, 0, T.m0, "m0", ["gxa"])
+        extract(0, CH, 32, T.m1, "m1", ["gxa"])
+        act(T.d1[:, 2:96:3], T.pa[:, 0:32], F.Copy, (), ["pa", "d1a"])
+        act(T.pb[:, 32 * t:32 * t + 32], T.pa[:, 32:64], F.Copy, (), ["pa", "b%d" % t])
+        tt(T.d1[:, 0:96:3], T.pb[:, 32 * (t - 1):32 * t], T.pb[:, 32 * t:32 * t + 32], A.subtract, ["b%d" % (t - 1), "b%d" % t], ["d1c"])
+        tt(T.d1[:, 1:96:3], T.pb[:, 32 * t:32 * t + 32], T.d1[:, 2:96:3], A.subtract, ["d1a", "b%d" % t], ["d1b"])
+
+    def decide(t):
+        o = [((t - 1) * 4 + k) * 64 for k in others]
+        rk = ["rv%d" % t]
+        tt(T.ta[:], T.rv[:, o[0]:o[0] + 64], T.rv[:, o[1]:o[1] + 64], A.add, rk, ["ta"], 64)
+        tt(T.tb[:], T.rv[:, o[2]:o[2] + 64], T.pre[:], A.add, rk + ["pre0", "pre1"], ["tb"], 64)
+        tt(T.te[:], T.ta[:], T.tb[:], A.add, ["ta", "tb"], ["te"], 64)
+        for a in range(4):
+            ts(T.lx[:, :, a, :], T.te[:], 0.0, A.is_gt, ["te", "mk"], ["lx%d" % a], T.mk[:, a:a + 1], A.mult)
+        n = 192 if t < NS else 384
+        lk, key = ["lx%d" % a for a in range(4)], "ls%d_%d" % (t, r)
+        mm(T.pc[:, 0:n], T.lx[:, 0:8], T.rc0[:, 0:n], True, False, lk + ["rc0"], ["pc"], n)
+        mm(T.pc[:, 0:n], T.lx[:, 8:16], T.rc1[:, 0:n], False, True, lk + ["rc1"], ["pc"], n)
+        if t < NS:
+            o, ol = (t - 1) * 192, ((t - 1) * 4 + r) * 64
+            scan(T.so[:, o:o + 192], T.pc[:, 0:192], T.d1[:], ["d1a", "d1b", "d1c", "d1s"], ["pc", "so%d" % t], 192)
+            cp(T.ls[:, ol:ol + 64], T.so[:, o + 2:o + 192:3], ["so%d" % t], [key])
+            send(T.ls[:, ol:ol + 64], T.ls[:, ol:ol + 64], ring, "li%d_%d" % (t, r), [key])
+        else:
+            scan(T.s5[:], T.pc[:, 0:384], T.d5[:], ["d5_%d" % i for i in range(12)], ["pc", "s5"], 384)
+            cp(T.fin[:, 128 * r:128 * r + 128], T.s5[:, 2:384:3], ["s5"], [key], 128)
+            send(T.fin[:, 128 * r:128 * r + 128], T.fin[:, 128 * r:128 * r + 128], ring, "li5_%d" % r, [key], 0.5)
+
+    def books(t):
+        val = lambda x: (vv(x), [x]) if isinstance(x, str) else x
+
+        def b2(o, a, b, op):
+            (oa, ok), (aa, ak), (ba, bk) = val(o), val(a), val(b)
+            tt(oa, aa, ba, op, ak + bk, ok)
+
+        def b1(o, a, s1, op0, s2=None, op1=None):
+            (oa, ok), (aa, ak) = val(o), val(a)
+            if op0 in (A.mult, A.add) and op1 in (None, A.add) and "sti" not in ak:
+                affine(oa, aa, s1 if op0 == A.mult else 1.0, s1 if op0 == A.add else s2 or 0.0, ak, ok)
+            else:
+                ts(oa, aa, s1, op0, ak, ok, s2, op1)
+
+        n0 = lambda s: (T.nb[:, (s - 1) * 96 + 2:s * 96:3], ["nb%d" % s])
+        n1 = lambda s: (T.nb[:, (s - 1) * 96 + 1:s * 96:3], ["nb%d" % s])
+        wv = lambda s: "w1" if s == 1 else (T.so[:, (s - 2) * 192 + 2:(s - 2) * 192 + 96:3], ["so%d" % (s - 1)])
+        d4 = lambda l, j: (T.d4[:, 96 * l + j:96 * l + 96:3], ["d4_%d" % (3 * l + j)])
+        d5 = lambda l, j: (T.d5[:, 96 * l + j:96 * l + 96:3], ["d5_%d" % (3 * l + j)])
+        s4 = lambda l, n=1: (T.s4[:, 96 * l + 2:96 * (l + n):3], ["s4_%d" % i for i in range(l, l + n)])
+        es = lambda l: (T.es[:, 96 * r + 32 * l:96 * r + 32 * l + 32], ["eo%d" % l])
+        part = lambda name, n, a, key: (vv(name, n, a, a + 1), [key])
+        x16 = (T.x16[:], ["x16"])
+        sub, mul, plus = A.subtract, A.mult, A.add
+
+        def wrap16(name, wk, ck):
+            a, b = (vv(name, 2), [name]), (vv(name + "t", 2), [name + "t"])
+            b1(a, ck, float(K), mul)
+            b2(a, a, wk, plus)
+            b1(b, a, float(W), A.is_ge, float(W), mul)
+            b2(a, a, b, sub)
+            b1(a, a, 16.0, mul, 1.0, plus)
+
+        act(T.nb[:, (t - 1) * 96:t * 96], T.pc[:, 0:96], F.Copy, (), ["pc", "nb%d" % t], 96)
+        if t >= 2:
+            b2("mx" if t == 2 else "mn", (T.te[:, 0:32], ["te"]), (T.te[:, 32:64], ["te"]), A.min)
+            if t > 2:
+                b2("mx", "mx", "mn", A.max)
+            b1("rz", "mx", 0.0, A.is_gt)
+            b2("rz", "rz", (T.dl[:, 32 * (t - 1):32 * t], ["dl"]), mul)
+            b2("tn", "rz", (T.lz[:, 32 * t:32 * t + 32], ["lz"]), plus)
+        if t < 4:
+            b2("z%d" % t, n0(t), n1(t), mul)
+        b2("ns%d" % t, n0(t), n1(t), A.max)
+        if t == 1:
+            li, lk = wl(1, r, 0, 32)
+            cp(vv("w1"), li, lk, ["w1"])
+            b1("v0", (T.sti[:, 32 * r:32 * r + 32], ["sti"]), 16.0, mul, 2.0, plus)
+        if t == 2:
+            b2("r2", "z2", "ns1", A.is_gt)
+            b2("a", n0(1), n0(2), plus)
+            b2("dd2", "z2", "r2", sub)
+            b2("k1", "ns1", "r2", plus)
+            b2("c1", n0(1), "r2", A.max)
+            b2("wd", wv(3), wv(2), sub)
+            b2("D2", "dd2", "z1", A.is_gt)
+            b2("dd2", "dd2", "z1", plus)
+            b2("wd", "wd", "r2", mul)
+            b1("aa", "a", 0.0, A.is_equal, 1.0, plus)
+            b1("ka", "a", 0.0, A.is_equal)
+            b1("ne", "a", 1.0, A.not_equal)
+            b2("b1", "D2", n0(1), A.is_gt)
+            b1(part("ws12", 2, 0, "ws1"), "w1", 0.0, plus)
+            b2(part("ws12", 2, 1, "ws2"), "wd", wv(2), plus)
+            b1("sl2", "r2", 2.0, mul, 3.0, plus)
+        if t == 3:
+            cc1, cc2 = part("c12", 2, 0, "cc1"), part("c12", 2, 1, "cc2")
+            b2("r3", "z3", "ns2", A.is_gt)
+            b2("o", "a", n0(3), plus)
+            b2("q1", n0(3), n0(2), sub)
+            b2("wd", wv(4), wv(3), sub)
+            b2("dd3", "z3", "r3", sub)
+            b2("rho", "r2", "r3", plus)
+            b2("D3", "dd3", "dd2", A.is_gt)
+            b2("dd3", "dd3", "dd2", plus)
+            b2("o", "o", "rho", plus)
+            b2("q1", "q1", "rho", mul)
+            b2("wd", "wd", "rho", mul)
+            b2("F3", "D3", "k1", A.is_gt)
+            b1("al3", "dd3", 0.0, A.is_equal)
+            b2("o", "o", "rho", plus)
+            b2(cc2, "q1", n0(2), plus)
+            b2(part("ws34", 2, 0, "ws3"), "wd", wv(3), plus)
+            b1(part("ws34", 2, 1, "ws4"), wv(4), 0.0, plus)
+            b2(cc1, "c1", "F3", A.max)
+            b2("ge1", "D2", "F3", plus)
+            b1("t1", "o", 4.0, A.is_equal)
+            b1("t3", "o", 2.0, A.is_le)
+            b1("nr", "o", 1.0, A.is_gt)
+            b2("ge1", "ge1", "al3", plus)
+            wrap16("V12", (vv("ws12", 2), ["ws1", "ws2"]), (vv("c12", 2), ["cc1", "cc2"]))
+            b2("nr", "nr", "ns3", A.max)
+            b1("q2", cc1, -2.0, plus)
+            b2("u1", "al3", cc2, mul)
+            b2("nt3", "nr", "t3", mul)
+            b2("q2", "q2", "ge1", mul)
+            b2("b1", "b1", "u1", plus)
+            b2("dr", "nt3", "aa", mul)
+            b2(es(0), "v0", "q2", plus)
+            b2("b1", "b1", part("V12", 2, 0, "V12"), plus)
+            b2("b1", "b1", "ge1", mul)
+            b1("u2", "rho", -1.0, mul, 4.0, plus)
+            b2(d4(0, 2), "u2", "al3", mul)
+            b2("at1", "al3", "t1", mul)
+            b2("u3", "t1", "dr", sub)
+            b1(d4(0, 1), "at1", -1.0, mul)
+            b1("u3", "u3", -1.0, plus)
+            b2(d4(0, 0), "u3", "al3", mul)
+            b2("q3", "t3", "ne", mul)
+            b2("q3", "q3", "t1", plus)
+            b1("q3", "q3", -1.0, mul, 2.0, plus)
+            b2("q3", "q3", "nr", mul)
+            for l in (1, 2):
+                mset(d4(l, 2)[0], 0.0, d4(l, 2)[1])
+                b1(d4(l, 1), "t1", 0.0, plus)
+                b2(d4(l, 0), "q3", "t1", sub)
+            b1("rr", "nr", -1.0, mul, 1.0, plus)
+            b2(d4(3, 2), n0(3), "rho", A.is_gt)
+            b1(d4(3, 1), "rho", 0.0, plus)
+            b2("q4", "rr", n0(3), A.is_gt)
+            b2(d4(3, 0), "q4", "rho", A.is_gt)
+            for j in range(3):
+                mset(d4(4, j)[0], float(j == 1), d4(4, j)[1])
+            b1("u4", "o", -1.0, mul, 4.0, plus)
+            b2(d4(5, 2), "u4", "al3", mul)
+            b2(d4(5, 1), "at1", "al3", sub)
+            b1("u5", "o", -1.0, mul, 1.0, plus)
+            b2("tb5", d4(5, 2), d4(5, 1), plus)
+            b2("u5", "u5", "rr", mul)
+            b2("u5", "u5", "al3", mul)
+            b2(d4(5, 0), "u5", "tb5", sub)
+            b1(d4(6, 2), "rho", 0.0, plus)
+            mset(d4(6, 1)[0], 0.0, d4(6, 1)[1])
+            b1(d4(6, 0), "rr", 0.0, plus)
+            b2("cur", (T.so[:, 482:576:3], ["so3"]), x16, sub)
+            b1("sl1", cc1, 1.0, plus)
+            b1("cur", "cur", 1.0 / CH, mul, 4.0, plus)
+            b2("yp", "sl1", "ge1", mul)
+            b2("sl2", "sl2", cc2, plus)
+            b1("u6", "yp", -1.0, mul, 7.0, plus)
+            b1("q5", "cur", -8.0, plus)
+            b2("s3", "sl1", "sl2", sub)
+            b2("u6", "u6", "al3", mul)
+            b2("q5", "q5", "t1", mul)
+            b2(d4(7, 2), "u6", "yp", plus)
+            b1("u7", "q5", 1.0, plus)
+            b2("s3", "s3", "ka", mul)
+            b2(d4(7, 1), "u7", "al3", mul)
+            b2("s3", "s3", "sl2", plus)
+            b1("u8", "cur", -1.0, mul, 6.0, plus)
+            b2("s3", "s3", "cur", sub)
+            b2("u8", "u8", "rr", mul)
+            b2("s3", "s3", "nt3", mul)
+            b2("u8", "u8", "cur", plus)
+            b2("s3", "s3", "q5", sub)
+            b2("u8", "u8", "s3", plus)
+            b1("u8", "u8", -8.0, plus)
+            b2(d4(7, 0), "u8", "al3", mul)
+            b1("sib", wv(4), float(W - K), A.is_ge, float(W), mul)
+            b2("sib", wv(4), "sib", sub)
+            b1("sib", "sib", 16.0, mul, 16.0 * K + 1.0, plus)
+            b1("yc", "cur", -1.0 * CH, mul, 8.0 * CH, plus)
+        if t == 4:
+            for l in range(8):
+                scan(T.s4[:, 96 * l:96 * l + 96], T.nb[:, 288:384], T.d4[:, 96 * l:96 * l + 96],
+                     ["nb4"] + ["d4_%d" % (3 * l + j) for j in range(3)], ["s4_%d" % l])
+            ge = lambda i, n=1: (vv("ge", 3, i, i + n), ["ge_%d" % j for j in range(i, i + n)])
+            for i in range(3):
+                b1(ge(i), s4(0), 2.0 + i, A.is_ge)
+            for i, x in enumerate(["al", "g2", "g3", "g4"]):
+                b1(x, s4(5), 1.0 + i, A.is_ge)
+            b1("p1", s4(0), 1.0, A.is_equal, -1.0, plus)
+            bb = (vv("bb", 2), ["bb"])
+            b2(bb, s4(3, 2), s4(1, 2), sub)
+            b2(es(1), "b1", "p1", plus)
+            wrap16("V34", (vv("ws34", 2), ["ws3", "ws4"]), s4(3, 2))
+            b2(bb, bb, ge(1, 2), mul)
+            b2("e1", "al", s4(6), mul)
+            b2("gs", "g4", "ns4", A.is_gt)
+            b1("wa", wv(5), 16.0, mul, 1.0, plus)
+            b1("wb", wv(5), float(W - K), A.is_ge, float(W), mul)
+            b2(bb, bb, s4(1, 2), plus)
+            b2("e0", "al", "e1", sub)
+            b2("wb", wv(5), "wb", sub)
+            b2("p2", part("bb", 2, 0, "bb"), part("V12", 2, 1, "V12"), plus)
+            b2("p3", part("bb", 2, 1, "bb"), part("V34", 2, 0, "V34"), plus)
+            b2("k4", part("V34", 2, 1, "V34"), ge(2), mul)
+            b1("wb", "wb", 16.0, mul, 16.0 * K + 1.0, plus)
+            b2("p2", "p2", ge(0), mul)
+            b2("p3", "p3", ge(1), mul)
+            b2("x1", "e1", "wa", mul)
+            b2("x0", "e0", "wa", mul)
+            b1(es(2), "p2", -1.0, plus)
+            send(T.es[:, 96 * r:96 * r + 96], T.es[:, 96 * r:96 * r + 96], ring, "ea%d" % r, ["eo0", "eo1", "eo2"], 0.4)
+            b1(d5(1, 2), "p3", -1.0, plus)
+            b1(d5(1, 1), "e1", 0.0, plus)
+            b2("p4", "g3", "g4", plus)
+            b2(d5(1, 0), "p4", "gs", sub)
+            b2("wb", "wb", "g2", mul)
+            b1(d5(3, 2), "x0", -1.0, plus)
+            b2(d5(3, 1), "wb", "x0", sub)
+            b1(d5(3, 0), "wb", -1.0, mul)
+            b2("p5", "k4", "x1", plus)
+            b1(d5(2, 2), "p5", -1.0, plus)
+            b2(d5(2, 1), "e0", "x1", sub)
+            b1("k5", "k4", 2.0, plus)
+            b2("sib", "sib", "gs", mul)
+            b2("k5", "k5", "g3", mul)
+            b2("sib", "sib", "g2", plus)
+            b2(d5(2, 0), "sib", "k5", sub)
+            b1("ya", s4(7), -1.0 * CH, mul, 9.0 * CH, plus)
+            b1("yb", s4(7), -1.0 * CH, mul, 10.0 * CH, plus)
+            b1("y0", s4(7), 1.0 * CH, mul)
+            b2("ya", "ya", "al", mul)
+            b2("yb", "yb", "g2", mul)
+            b2("p6", "cur", s4(7), sub)
+            b2("yc", "yc", "gs", mul)
+            b2("p6", "p6", "g3", mul)
+            b2(d5(0, 1), "yb", "ya", sub)
+            b2("y0", "y0", "ya", plus)
+            b1("p6", "p6", 1.0 * CH, mul)
+            b2("yc", "yc", "yb", sub)
+            b2(d5(0, 2), "y0", x16, plus)
+            b2(d5(0, 0), "p6", "yc", plus)
+
+    look(1)
+    for t in range(1, NS + 1):
+        for k in range(NR):
+            bulk(t, k)
+        decide(t)
+        if t < NS:
+            books(t)
+        if t < NS - 1:
+            look(t + 1)
+
+    for k in range(NR):
+        act(T.stb[:, 0:3, 32 * k:32 * k + 32], T.es[:, 96 * k:96 * k + 96], F.Copy,
+            ["eo0", "eo1", "eo2"] if k == r else ["es%d" % k], ["se%d" % k], 96)
+    dma("Y", T.stk[:, 0:384], T.stb[:, 0:3, :], "dk0", ["se%d" % j for j in range(NR)], (), 196608)
+    for k in range(NR):
+        xs, st = T["xs%d" % k], T["st%d" % k]
+        rd = ["yu%d" % k] + ["x%d_%d_%d" % (k, s, h) for s in range(11) for h in range(2)]
+        cp(T.yu[:, 32 * k:32 * k + 32], T.fin[:, 128 * k:128 * k + 32], ["ls5_%d" % k], ["yu%d" % k])
+        act(st[:, 0:H], xs[:].indirect(T.yu[:, 32 * k:32 * k + 16]), F.Copy, rd, ["st%d_0" % k], H, GA)
+        cp(st[:, H:CH], xs[:].indirect(T.yu[:, 32 * k + 16:32 * k + 32]), rd, ["st%d_1" % k], H, GA)
+        dma("Y", T.y[:, CH * k:CH * k + CH], st[:], "dy%d" % k, ["st%d_0" % k, "st%d_1" % k], (), 2 ** 18)
+        cp(T.stb[:, 3:6, 32 * k:32 * k + 32], T.fin[:, 128 * k + 32:128 * k + 128], ["ls5_%d" % k], ["sl%d" % k], 96)
+    dma("S", T.stk[:, 384:768], T.stb[:, 3:6, :], "dk1", ["sl%d" % j for j in range(NR)], (), 196608)
+    return ops, ext, Q
+
+
+def links(ops):
+    lastw, readers, out = {}, {}, []
+    for n, op in enumerate(ops):
+        d = {lastw[k]: True for k in op["rd"] if k in lastw}
+        for k in op["wr"]:
+            for m in ([lastw[k]] if k in lastw else []) + readers.get(k, []):
+                d[m] = d.get(m, False) or ops[m]["q"] != op["q"]
+        if op["q"] == "P":
+            d = {m: w and ops[m]["q"] != "P" for m, w in d.items()}
+        out.append(d)
+        for k in op["rd"]:
+            readers.setdefault(k, []).append(n)
+        for k in op["wr"]:
+            lastw[k] = n
+            readers[k] = []
+    return out
+
+
+def plan(recs):
+    ops, deps, sends = [], [], {}
+    for rops, _, _ in recs:
+        base = len(ops)
+        deps += [{m + base: w for m, w in d.items()} for d in links(rops)]
+        ops += rops
+    for n, op in enumerate(ops):
+        for i, k in enumerate(op["to"][0] if op["to"] else []):
+            sends.setdefault((k, op["to"][1]), []).append((n, i))
+    far = [[x for k in op["rd"] if k in recs[op["r"]][1] for x in sends[(op["r"], recs[op["r"]][1][k][0])]] for op in ops]
+    succ, left = [[] for _ in ops], []
+    for n in range(len(ops)):
+        pre = set(deps[n]) | {m for m, _ in far[n]}
+        left.append(len(pre))
+        for m in pre:
+            succ[m].append(n)
+    order, todo, cnt = [], [n for n in range(len(ops)) if not left[n]], list(left)
+    while todo:
+        order.append(todo.pop())
+        for m in succ[order[-1]]:
+            cnt[m] -= 1
+            if not cnt[m]:
+                todo.append(m)
+    prio = [0.0] * len(ops)
+    for n in reversed(order):
+        op = ops[n]
+        more = PLAN["sem"] if op["sem"] is None else PLAN["issue"] + PLAN["start"] + op["cost"] if op["to"] else PLAN["dma"]
+        prio[n] = op["cost"] + more + max([prio[m] for m in succ[n]] + [0.0])
+    for n, op in enumerate(ops):
+        name = (op["wr"] + [op["to"][1] if op["to"] else op["sem"]])[0]
+        prio[n] += PRI.get(op["q"] + "".join(x for x in name if x.isalpha()), 0.0)
+    start, end, land, free, ready = {}, {}, {}, {}, {}
+    rings, first, out = [0.0] * NR, [PLAN["first"]] * NR, [[] for _ in recs]
+
+    def release(n):
+        t = max([0.0] + [end[m] if w else start[m] for m, w in deps[n].items()] + [land[x] for x in far[n]])
+        ready.setdefault((ops[n]["r"], ops[n]["q"]), []).append((t, n))
+    for n in range(len(ops)):
+        if not left[n]:
+            release(n)
+    for _ in range(len(ops)):
+        t, key = min((max(free.get(key, 0.0), min(l)[0]), key) for key, l in ready.items() if l)
+        x = max([x for x in ready[key] if x[0] <= t + PLAN["slack"]], key=lambda x: (prio[x[1]], -x[1]))
+        ready[key].remove(x)
+        n, op = x[1], ops[x[1]]
+        t, r = max(t, x[0]), op["r"]
+        start[n] = t
+        if op["to"]:
+            free[key] = t + PLAN["issue"]
+            e = max(t + PLAN["issue"] + PLAN["start"] + first[r], rings[r])
+            first[r] = 0.0
+            for i in range(len(op["to"][0])):
+                e += op["cost"]
+                land[(n, i)] = e
+            rings[r] = end[n] = e
+        elif op["sem"]:
+            free[key] = t + 0.1
+            rings[r] = max(t + PLAN["dma"], rings[r]) + op["cost"]
+            end[n] = rings[r] + 0.3
+        else:
+            free[key] = t + op["cost"]
+            end[n] = t + op["cost"] + PLAN["sem"]
+        out[r].append(op)
+        for m in succ[n]:
+            left[m] -= 1
+            if not left[m]:
+                release(m)
+    return out
+
+
+def rank_program(g, core, T, topo):
+    r = T.rank_of(core)
+    if r is None:
+        return
+    recs = [record(g, k, T, topo) for k in range(NR)]
+    ops, ext, Q = plan(recs)[r], recs[r][1], recs[r][2]
+    known, count, tok, waits, need = {q: {} for q in Q}, {}, [], [], set()
+    for n, (op, d) in enumerate(zip(ops, links(ops))):
+        q, w = op["q"], {}
+        for t in [tok[m] for m in d if d[m]] + [ext[k] + ({}, None) for k in op["rd"] if k in ext]:
+            if known[q].get(t[0], 0) < t[1] and w.get(t[0], (0, 0))[1] < t[1]:
+                w[t[0]] = t
+        for t in w.values():
+            for s, c in list(t[2].items()) + [t[:2]]:
+                known[q][s] = max(known[q].get(s, 0), c)
+            need.add(t[3])
+        waits.append(list(w.values()))
+        s = op["sem"] or q
+        count[s] = count.get(s, 0) + (op["inc"] if op["sem"] else 1)
+        tok.append((s, count[s], dict(known[q]), None if op["sem"] else n))
+    num, at = {}, {}
+    for n, op in enumerate(ops):
+        q = op["q"]
+        for t in waits[n]:
+            if t[3] is None:
+                Q[q].wait_ge(T.sem[t[0]], t[1])
+            else:
+                Q[q].wait_ge(T.sem["q" + t[0]], at[t[3]])
+        ins = op["fn"]()
+        if op["sem"] is None:
+            if n in need:
+                num[q] = at[n] = num.get(q, 0) + 1
+                ins.then_inc(T.sem["q" + q], 1)
+        elif not op["to"]:
+            ins.then_inc(T.sem[op["sem"]], op["inc"])
+    for s in ["dk0", "dk1", "sent"] + ["dy%d" % k for k in range(NR)]:
+        g.wait_ge(T.sem[s], count[s])

@@ -1,3 +1,4 @@
+import numpy as np
 from concourse.bass import DstId, RemoteDMATransfer
 from concourse.mybir import AluOpType as A, ActivationFunctionType as F
 
@@ -5,75 +6,136 @@ NR, CH, W, K, NS = 4, 512, 8192, 37, 5
 AO = 48
 f32, bf16, i32, u16 = "float32", "bfloat16", "int32", "uint16"
 
-_SB = {"fr": (8240, bf16), "ax": (8240, bf16), "fi": (512, i32), "hl": (1024, bf16), "sti": (128, i32), "stu": (128, u16),
-       "limi": (8, i32), "limf": (8, f32), "gx": (1280, bf16), "l0": (128, u16), "ls": (1024, u16), "lw": (640, u16),
-       "yu": (128, u16), "sb": (1280, f32), "rv": (1280, f32), "es": (384, f32), "fin": (512, f32), "pi": (8, i32),
-       "ci": (8, i32), "cf": (16, f32), "x144": (144, f32), "x96": (384, f32), "x4": (128, f32), "x16": (32, f32),
-       "bo": (8, f32), "m0": (144, bf16), "m1": (144, bf16), "mk": (4, f32), "rc0": (384, bf16), "rc1": (384, bf16),
-       "lq": (128, f32), "gq": (32, f32), "lr": (160, f32), "lz": (160, f32), "dl": (128, f32), "pre": (64, f32),
-       "ta": (64, f32), "tb": (64, f32), "te": (64, f32), "d1": (192, f32), "d4": (768, f32), "d5": (384, f32),
-       "so": (768, f32), "s4": (768, f32), "s5": (384, f32), "nb": (384, f32), "pb": (160, f32), "v": (3584, f32)}
-SCRATCH = {k: ("sbuf", [128, n], d) for k, (n, d) in _SB.items()}
-SCRATCH.update({"stb": ("sbuf", [128, 6, 128], f32), "lx": ("sbuf", [128, 16, 4, 4], bf16),
-                "pc": ("psum", [128, 512], f32), "pa": ("psum", [128, 512], f32), "pl": ("psum", [128, 512], f32)})
+_SB = {"fr": ([8240], bf16), "ax": ([8240], bf16), "fi": ([512], i32), "hl": ([1024], bf16), "sti": ([128], i32),
+       "stu": ([128], u16), "limi": ([8], i32), "limf": ([8], f32), "la": ([2, 8], f32), "lb": ([2, 8], f32),
+       "gx": ([2048], bf16), "gl": ([1024], bf16), "l0": ([512], u16), "ls": ([1024], u16), "lw": ([512], u16),
+       "x64": ([128], f32), "r0": ([320], bf16), "r1": ([320], bf16), "r2": ([320], bf16), "pm": ([128], bf16),
+       "pn": ([128], bf16), "lz": ([192], f32), "cb": ([320], bf16), "da": ([320], f32), "db": ([320], f32), "sa": ([320], f32),
+       "sc": ([320], f32), "y0": ([160], bf16), "y1": ([160], f32), "fp": ([384], f32),
+       "sb": ([1536], f32), "rv": ([1536], f32), "fin": ([896], u16), "ci2": ([384], i32), "stb": ([6, 128], f32),
+       "pi": ([8], i32), "ci": ([8], i32), "cf": ([24], f32), "x144": ([144], f32), "x32": ([64], f32),
+       "x16": ([32], f32), "bo": ([8], f32), "m0": ([144], bf16), "m1": ([144], bf16), "idf": ([128], f32), "idb": ([128], bf16),
+       "idn": ([128], bf16), "gq": ([64], f32), "rc": ([384], bf16), "de": ([64], bf16), "dn": ([64], bf16), "dd": ([64], bf16),
+       "one": ([64], bf16), "rk": ([32, 9, 3], bf16), "ra": ([32, 2], bf16), "rb": ([32, 2], bf16),
+       "lx": ([9, 8, 2, 8], bf16), "ll": ([5, 64, 2], f32), "jj": ([5, 64], bf16),
+       "d1": ([384], f32), "d5": ([384], f32), "so": ([384], f32), "wv": ([160], f32), "s5": ([384], f32), "pb": ([160], f32),
+       "sq": ([640], bf16), "rs": ([640], bf16), "ro": ([640], bf16), "h0": ([160], bf16), "h1": ([320], bf16),
+       "ho": ([320], bf16), "xg": ([128], bf16), "c0": ([256], bf16), "co": ([256], bf16), "v0": ([384], bf16),
+       "v1": ([384], f32), "vo": ([384], f32), "f0": ([800], bf16), "f1": ([800], f32), "fo": ([800], f32),
+       "lvl": ([160], f32), "slc": ([128], bf16), "u": ([512], bf16), "v": ([1120], f32)}
 for _k in range(NR):
-    SCRATCH["xs%d" % _k] = ("sbuf", [128, 11 * CH], f32)
-    SCRATCH["st%d" % _k] = ("sbuf", [128, CH], f32)
-    SCRATCH["ab%d" % _k] = ("sbuf", [128, 2 * CH], f32)
-    SCRATCH["pe%d" % _k] = ("psum", [128, 512], f32)
+    _SB.update({"xs%d" % _k: ([(13 if _k < 2 else 11) * CH], f32), "ab%d" % (_k % 2): ([4 * CH], f32)})
+SCRATCH = {k: ("sbuf", [128] + n, d) for k, (n, d) in _SB.items()}
+BANKS = ["pe0", "pe1", "pq", "pc", "pa", "px", "py", "pz"]
+SCRATCH.update({k: ("psum", [128, 512], f32) for k in BANKS})
 
-SEMAPHORES = (["qV", "qS", "qP", "qG", "sent", "dfi", "dst", "dlim", "dfa", "dfb", "dax", "dk0", "dk1", "ini"]
-              + ["dy%d" % k for k in range(NR)] + ["sh%d" % t for t in range(1, 6)]
+SEMAPHORES = (["qV", "qS", "qP", "qG", "sent", "dfi", "dst", "dlim", "dfa", "dfb", "dax", "day", "dk0", "dk1"] + ["fi%d" % k for k in range(NR)]
+              + ["dy%d" % k for k in range(NR)] + ["sh%d_%d" % (t, k) for t in range(1, 6) for k in range(NR)]
               + ["li%d_%d" % (t, k) for t in range(1, 6) for k in range(NR)] + ["ea%d" % k for k in range(NR)])
 
-PLAN = {"cyc": 0.9e-3, "gth": 1.56, "fix": 0.05, "pe": 0.52e-3, "sem": 0.05, "issue": 0.6, "start": 2.3, "rows": 1.0,
-        "dma": 1.9, "bw": 240e3, "first": 2.0, "slack": 0.0, "ev": 0}
-PRI = {"Vd": 2.5, "Vsl": 1, "Vs": -8, "Vrz": -8, "Sd": 8, "Vtb": -0.5}
+PLAN = {"cyc": 0.9e-3, "gth": 1.2, "fix": 0.0, "pe": 0.45e-3, "sem": 0.3, "issue": 0.2, "start": 0.9, "rows": 0.5,
+        "wake": 0.4, "dma": 1.3, "bw": 350e3, "first": 2.0, "hold": 1.5, "passes": 0, "keep": 1.2}
+OPT = {"look": "VS", "WA": 5, "cut": 2, "dec": 4.0, "lk": 0.0, "bk": 1.0, "lcut": 2, "pcut": 0, "fin": 24.0,
+       "mrg": 3, "pre": 0.8, "ev": 0.4, "ew": 0.7, "dl": (0.55, 0.55, 0.55, 0.55), "order": "VSPG",
+       "ring": (2, 1, 3), "rev": -1, "xz": "SV", "lk2": "SS", "pra": 0.5, "half": ((0, 0), (2, 1)), "ea_": 0.3,
+       "d1": (5.0, 5.7), "d2": (10.3, 11.7, 12.6, 13.55), "txz": (3.95, 4.15), "tl2": (4.6, 5.0), "e3": 0.2, "e1": 0.12, "gap": 0.3,
+       "sw": 0.7, "g1": 0.16, "g2": 0.0, "ea": 23.5}
+WIDE = (0, 1)
+ORDER = [(1, 2, 2), (1, 3, 3), (2, 0, 4), (2, 1, 5), (2, 2, 10), (2, 3, 11)] + [(t, k, 4 * t + k) for t in (3, 4, 5) for k in range(NR)]
+_cols = {}
+
+
+def columns(name, ix):
+    key = (name, repr(ix))
+    if key not in _cols:
+        shape = SCRATCH[name][1][1:]
+        m = np.zeros(shape, bool)
+        m[ix[1:]] = True
+        _cols[key] = int.from_bytes(np.packbits(m.reshape(-1), bitorder="little").tobytes(), "little"), int(m.sum())
+    return _cols[key]
 
 
 def record(g, r, T, topo):
     cores = list(T.cores)
     others = [k for k in range(NR) if k != r]
+    ring = [(r + i) % NR for i in OPT["ring"]]
+    rest = lambda k: [j for j in range(NR) if j != k]
     Q = {"V": g.vector, "S": g.scalar, "P": g.tensor, "G": g, "Y": g.sync}
     V, S, P = g.vector, g.scalar, g.tensor
-    ops, ext = [], {}
-    cyc, GA, H = PLAN["cyc"], PLAN["gth"], CH // 2
+    ops, turn = [], [99, 0]
+    cyc, GA, H, sl = PLAN["cyc"], PLAN["gth"], CH // 2, slice
+
+    def view(name, *ix, part=sl(None)):
+        ix = (part,) + ix
+        bits, n = columns(name, ix)
+        return T[name][ix if len(ix) > 1 else part], [(name, bits)], n, False
+
+    def at(name, a=None, b=None, c=None):
+        return view(name, sl(a, b, c)) if len(SCRATCH[name][1]) == 2 else view(name)
+
+    def nth(name, n, i, a, b):
+        return at(name, 32 * n * a + i, 32 * n * b, n)
+
+    def gather(win, off):
+        return win[0].indirect(off[0]), win[1] + off[1], 16 * off[2], True
 
     def add(q, fn, rd, wr, cost, sem=None, inc=16, to=None):
-        ops.append({"q": q, "fn": fn, "rd": list(rd), "wr": list(wr), "cost": cost, "sem": sem, "inc": inc, "to": to, "r": r})
+        rd = [x for a in rd if isinstance(a, tuple) for x in a[1]]
+        wr = [x for a in wr for x in a[1]] + [x for x in rd if x[0] in BANKS]
+        wr = [(n, 1) if n in BANKS else (n, m) for n, m in wr]
+        ops.append({"q": q, "fn": fn, "rd": [x for x in rd if x[0] not in BANKS], "wr": wr, "cost": cost, "sem": sem,
+                    "inc": inc, "to": to, "r": r, "turn": turn[0], "rush": turn[1], "tau": None})
 
-    def cost(n, m=1.0):
-        return PLAN["fix"] + max(64, n * m) * cyc
+    def cost(o, a, m=1.0):
+        return 0.06 + o[2] * GA * cyc if a[3] else PLAN["fix"] + max(64, o[2] * m) * cyc
 
-    def tt(o, a, b, op, rd, wr, n=32, m=2.0):
-        add("V", lambda: V.tensor_tensor(o, a, b, op), rd, wr, cost(n, m))
+    def narrow(*x):
+        return 0.5 if all(SCRATCH[a[1][0][0]][2] in (bf16, u16) for a in x) else 1.0
 
-    def ts(o, a, s1, op0, rd, wr, s2=None, op1=None, n=32):
+    ap = lambda x: x[0] if isinstance(x, tuple) else x
+
+    def tt(o, a, b, op):
+        m = 1.0 if a[1][0][0] in BANKS or b[1][0][0] in BANKS else 2.0
+        add("V", lambda: V.tensor_tensor(o[0], a[0], b[0], op), [a, b], [o], cost(o, a, m))
+
+    def ts(o, a, s1, op0, s2=None, op1=None):
         if op1 is None:
-            add("V", lambda: V.tensor_scalar(o, a, s1, None, op0), rd, wr, cost(n))
+            add("V", lambda: V.tensor_scalar(o[0], a[0], ap(s1), None, op0), [a, s1], [o], cost(o, a, narrow(o, a)))
         else:
-            add("V", lambda: V.tensor_scalar(o, a, s1, s2, op0, op1), rd, wr, cost(n))
+            add("V", lambda: V.tensor_scalar(o[0], a[0], ap(s1), ap(s2), op0, op1), [a, s1, s2], [o], cost(o, a, narrow(o, a)))
 
-    def cp(o, a, rd, wr, n=32, m=1.0):
-        add("V", lambda: V.tensor_copy(o, a), rd, wr, cost(n, m))
+    def cp(o, a):
+        add("V", lambda: V.tensor_copy(o[0], a[0]), [a], [o], cost(o, a, narrow(o, a)))
 
-    def act(o, a, f, rd, wr, n=32, m=1.0):
-        add("S", lambda: S.activation(o, a, f), rd, wr, cost(n, m))
+    def act(o, a, f=F.Copy, scale=1.0, bias=0.0):
+        if f == F.Copy and (scale, bias) == (1.0, 0.0):
+            add("S", lambda: S.activation(o[0], a[0], f), [a], [o], cost(o, a))
+        else:
+            f = F.Identity if f == F.Copy else f
+            add("S", lambda: S.activation(o[0], a[0], f, bias=ap(bias), scale=ap(scale)), [a, scale, bias], [o], cost(o, a))
 
-    def affine(o, a, scale, bias, rd, wr):
-        add("S", lambda: S.activation(o, a, F.Identity, bias=bias, scale=scale), rd, wr, cost(32))
+    def move(q, o, a):
+        (cp if q == "V" else act)(o, a)
 
-    def mm(o, l, rh, s0, s1, rd, wr, n=64):
-        add("P", lambda: P.matmul(o, l, rh, s0, s1), rd, wr, n * PLAN["pe"])
+    def mm(o, terms):
+        for i, (l, rh) in enumerate(terms):
+            c = max(min(64, l[2]), rh[2]) * (4 if SCRATCH[l[1][0][0]][2] == f32 else 1) * PLAN["pe"]
+            add("P", lambda l=l, rh=rh, i=i: P.matmul(o[0], l[0], rh[0], i == 0, i == len(terms) - 1), [l, rh], [o], c)
 
-    def mset(o, c, wr, n=32):
-        add("V", lambda: V.memset(o, c), (), wr, cost(n))
+    def mset(o, c):
+        add("V", lambda: V.memset(o[0], c), (), [o], cost(o, o, narrow(o)))
 
-    def scan(o, d0, d1, rd, wr, n=96):
-        add("V", lambda: V.tensor_tensor_scan(o, d0, d1, 0.0, A.mult, A.add), rd, wr, cost(n))
+    def scan(o, d0, d1):
+        add("V", lambda: V.tensor_tensor_scan(o[0], d0[0], d1[0], 0.0, A.mult, A.add), [d0, d1], [o], cost(o, o, narrow(o, d0, d1)))
 
-    def dma(q, o, a, sem, rd, wr, size):
-        add(q, lambda: Q[q].dma_start(o, a), rd, wr, 0.3 + size / PLAN["bw"], sem=sem)
+    def iota(o, pat, base=0, cm=0):
+        add("G", lambda: g.iota(o[0], pat, base, cm, allow_small_or_imprecise_dtypes=True), (), [o], 0.13 + 2 * o[2] * cyc)
+
+    hbm = lambda x: (x, [], 0, False)
+    line = (None, [("line", 1)], 0, False)
+
+    def dma(q, o, a, sem, size, more=()):
+        add(q, lambda: Q[q].dma_start(o[0], a[0]), [a], [o] + list(more), 0.3 + size / PLAN["bw"], sem=sem)
 
     def both(k, ranks):
         mask = -1
@@ -84,474 +146,589 @@ def record(g, r, T, topo):
     def nin(k, ranks):
         return bin(both(k, ranks)).count("1")
 
-    def send(ap_out, ap_in, ranks, sem, rd, more=0.0):
+    def send(o, a, ranks, sem, more=0.0):
         mask = both(r, ranks)
         ad = [topo.addr(cores[k]) for k in ranks]
         if len(ranks) == 1:
-            fn = lambda: g.remote_dma(ap_out, ap_in, T.sem[sem], T.sem.sent, ad[0][1], ad[0][0], mask)
+            fn = lambda: g.remote_dma(o[0], a[0], T.sem[sem], T.sem.sent, ad[0][1], ad[0][0], mask)
         else:
             fn = lambda: g.remote_dma_fused([RemoteDMATransfer(
-                dst_ids=[DstId(rid=a[0], pnc=a[1]) for a in ad], dma_engine_mask=mask, remote_sem=T.sem[sem],
-                src=ap_in, dsts=[ap_out] * len(ranks))], local_sem=T.sem.sent)
-        add("G", fn, rd, (), PLAN["rows"] + more, sem="sent", inc=nin(r, ranks), to=(ranks, sem))
+                dst_ids=[DstId(rid=x[0], pnc=x[1]) for x in ad], dma_engine_mask=mask, remote_sem=T.sem[sem],
+                src=a[0], dsts=[o[0]] * len(ranks))], local_sem=T.sem.sent)
+        add("G", fn, [a], (), PLAN["rows"] + more, sem="sent", inc=nin(r, ranks), to=(ranks, sem))
 
-    rest = lambda k: [j for j in range(NR) if j != k]
-    ring = [(r + i) % NR for i in range(1, NR)]
-    WA = 5 * W // 8
+    arrivals = []
 
-    dma("Y", T.fi[:], T.first[:], "dfi", (), ["fi", "y0"], 2 ** 18)
-    dma("Y", T.sti[:], T.start[:], "dst", (), ["sti", "y0"], 2 ** 16)
-    dma("Y", T.fr[:, 0:WA], T.frag[:, 0:WA], "dfa", (), ["y0"], 256 * WA)
-    dma("Y", T.fr[:, W:W + K], T.frag[:, 0:K], "dfa", (), ["y0", "fra"], 2 ** 14)
-    dma("S", T.limi[:, 0:5], T.lim[:], "dlim", (), ["limi"], 2 ** 12)
+    def landed(t, j, k):
+        o, n = (192 * j, 192) if t == 2 and k in WIDE else (64 * (4 * (t - 1 if t < 3 else t) + j), 64)
+        return at("rv", o, o + n)
 
-    def iota(o, pat, key):
-        add("G", lambda: g.iota(o, pat, 0, 0, allow_small_or_imprecise_dtypes=True), (), [key], 0.5)
-    add("G", lambda: g.iota(T.pi[:, 0:1], [[0, 1]], 0, 1), (), ["ip"], 0.13)
-    iota(T.x144[:], [[1, 144]], "x144")
-    iota(T.x4[:], [[0, 32], [1, 4]], "x4")
-    iota(T.x16[:], [[16, 32]], "x16")
-    iota(T.x96[:], [[0, 4], [1, 96]], "x96")
+    def leaving(t, k):
+        o, n = (192 * k, 192) if t == 2 and k in WIDE else (128 * k + 64 * t + 64 if t < 3 else 64 * (4 * t + k), 64)
+        return at("sb", o, o + n)
 
-    mset(T.ax[:, 0:2752], 0.0, ["ax0"], 1376)
-    act(T.ax[:, 2752:5504], T.ax[:, 0:2752], F.Copy, ["ax0"], ["ax1"], 2752)
-    mset(T.ax[:, 5504:8240], 0.0, ["ax2"], 1376)
-    cp(T.hl[:, 0:512], T.fi[:], ["fi"], ["hi"], 512)
-    tt(T.hl[:, 512:1024], T.fi[:], T.hl[:, 0:512], A.subtract, ["fi", "hi"], ["lo"], 512)
-    axk = ["ax0", "ax1", "ax2", "y0"]
-    for h in range(2):
-        key = ["hi", "lo"][h]
-        dma("Y", T.ax[h::16, AO:AO + W], T.hl[:, 512 * h:512 * h + 512], "dax", [key], axk, 2 ** 17)
-        dma("Y", T.ax[2 + h::16, AO - K:AO - K + W], T.hl[:, 512 * h:512 * h + 512], "dax", [key], axk, 2 ** 17)
-        dma("Y", T.ax[2 + h::16, AO - K + W:AO + W], T.hl[0::16, 512 * h:512 * h + K], "dax", [key], axk + ["ax"] * h, 2 ** 10)
-    dma("Y", T.fr[:, WA:W], T.frag[:, WA:W], "dfb", (), ["y0", "frb"], 256 * (W - WA))
-    cp(T.stu[:], T.sti[:], ["sti"], ["stu"], 128)
-
-    p0 = T.pi[:, 0:1]
-    ts(T.ci[:, 0:1], p0, 4, A.arith_shift_right, ["ip"], ["ci0"])
-    ts(T.ci[:, 1:2], p0, 15, A.bitwise_and, ["ip"], ["ci1"])
-    ts(T.ci[:, 2:3], p0, 3, A.bitwise_and, ["ip"], ["ci2"])
-    ts(T.ci[:, 3:4], p0, 2, A.arith_shift_right, ["ip"], ["ci3"])
-    ts(T.ci[:, 4:5], p0, 2, A.arith_shift_right, ["ip"], ["ci4"], 3, A.bitwise_and)
-    ts(T.ci[:, 5:6], p0, 1, A.arith_shift_right, ["ip"], ["ci5"], 7, A.bitwise_and)
-    cp(T.cf[:, 0:6], T.ci[:, 0:6], ["ci%d" % i for i in range(6)], ["cf"])
-    c = lambda i: T.cf[:, i:i + 1]
-    ts(c(6), c(0), 16.0, A.mult, ["cf"], ["c6"], 15.0, A.add)
-    ts(c(7), c(5), 0.0, A.is_equal, ["cf"], ["c7"])
-    ts(c(8), c(5), 1.0, A.is_equal, ["cf"], ["c8"])
-    ts(c(9), c(3), 3.0, A.mult, ["cf"], ["c9"], 1.0, A.add)
-    ts(c(10), c(3), 3.0, A.mult, ["cf"], ["c10"], 2.0, A.add)
-    ts(c(11), c(0), 4.0, A.mult, ["cf"], ["c11"], c(2), A.add)
-    ts(T.m0[:], T.x144[:], c(6), A.is_equal, ["x144", "c6", "c7"], ["m0"], c(7), A.mult, 144)
-    ts(T.m1[:], T.x144[:], c(6), A.is_equal, ["x144", "c6", "c8"], ["m1"], c(8), A.mult, 144)
-    ts(T.bo[:], T.x144[:, 0:8], c(0), A.is_equal, ["x144", "cf"], ["bo"])
-    ts(T.mk[:], T.x144[:, 0:4], c(2), A.is_equal, ["x144", "cf"], ["mk"])
-    ts(T.gq[:], T.x144[:, 0:32], c(11), A.is_equal, ["x144", "c11"], ["gq"])
-    ts(T.lq[:], T.x4[:], c(4), A.is_equal, ["x4", "cf"], ["lq"], n=128)
-    cp(T.limf[:, 0:5], T.limi[:, 0:5], ["limi"], ["limf"])
-    for l in range(5):
-        ts(T.lr[:, 32 * l:32 * l + 32], T.gq[:], T.limf[:, l:l + 1], A.mult, ["gq", "limf"], ["lr%d" % l])
-    mm(T.pl[:, 0:160], T.lq[:], T.lr[:], True, True, ["lq"] + ["lr%d" % l for l in range(5)], ["pl"], 640)
-    ts(T.rc0[:], T.x96[:], c(10), A.is_equal, ["x96", "c10"], ["rc0"], n=384)
-    ts(T.rc1[:], T.x96[:], c(9), A.is_equal, ["x96", "c9"], ["rc1"], n=384)
-    cp(T.lz[:], T.pl[:, 0:160], (), ["pl", "lz"], 160)
-    ts(T.x16[:], T.x16[:], c(1), A.add, ["x16", "cf"], ["x16"])
-    tt(T.dl[:], T.lz[:, 0:128], T.lz[:, 32:160], A.subtract, ["lz"], ["dl"], 128)
-    mset(T.d1[:, 96:192:3], -2.0 * CH, ["d1s"])
-    mset(T.d1[:, 97:192:3], 1.0 * CH, ["d1s"])
-    ts(T.d1[:, 98:192:3], T.x16[:], 1.0 * CH, A.add, ["x16"], ["d1s"])
-    mset(T.pb[:, 0:32], 0.0, ["b0"])
-
-    axw = T.ax[:, AO:AO + W]
-    frw = T.fr[:, 0:W + K]
-
-    def extract(n0, n, col, m, key, rd):
-        for i in range(16):
-            mm(T.pa[:, col:col + n // 16], m[:, 15 - i:143 - i], T.gx[:, n0 + i:n0 + n:16], i == 0, i == 15, rd + [key], ["pa"])
-
-    pc0 = 64 + 16 * r
-    cp(T.gx[:, 1024:1280], axw.indirect(T.stu[:, pc0:pc0 + 16]), ["ax", "stu"], ["gxc"], 256, GA)
-    act(T.gx[:, 0:512], axw.indirect(T.stu[:, 0:32]), F.Copy, ["ax", "stu"], ["gxa"], CH, GA)
-    cp(T.gx[:, 512:1024], axw.indirect(T.stu[:, 32:64]), ["ax", "stu"], ["gxb"], CH, GA)
-    extract(1024, 256, 64, T.m0, "m0", ["gxc"])
-    cp(T.l0[:, pc0:pc0 + 16], T.pa[:, 64:80], (), ["pa", "l0own"])
-    send(T.l0[:, pc0:pc0 + 16], T.l0[:, pc0:pc0 + 16], ring, "ini", ["l0own"])
-    extract(0, 1024, 0, T.m0, "m0", ["gxa", "gxb"])
-    cp(T.l0[:, 0:64], T.pa[:, 0:64], (), ["pa", "l0a"])
-    ext["l0in"] = ("ini", sum(nin(k, rest(k)) for k in others))
-    for t in range(1, NS + 1):
-        ext["rv%d" % t] = ("sh%d" % t, sum(nin(k, [r]) for k in others))
-        for k in others:
-            ext["ls%d_%d" % (t, k)] = ("li%d_%d" % (t, k), nin(k, rest(k)))
+    def ends(k):
+        o = 224 * k + (128 if k >= OPT["mrg"] else 32)
+        return at("fin", 224 * k, 224 * k + 32), at("fin", o, 224 * k + 224), at("fp", 96 * k, 96 * k + 96)
+    for t, k, _ in ORDER:
+        o = ((t - 1) * 4 + k) * 64
+        if k == r:
+            arrivals += [(landed(t, j, r), "sh%d_%d" % (t, j), nin(j, [r])) for j in others]
+        else:
+            arrivals.append((at("ls", o, o + 64) if t < NS else ends(k)[0], "li%d_%d" % (t, k), nin(k, rest(k))))
     for k in others:
-        ext["es%d" % k] = ("ea%d" % k, nin(k, rest(k)))
+        arrivals.append((ends(k)[1], "fi%d" % k, nin(k, rest(k))))
+        arrivals += [(ends(k)[2], "ea%d" % k, nin(k, rest(k)))] * (k >= OPT["mrg"])
+
+    WA = OPT["WA"] * W // 8
+    dma("Y", at("fi"), hbm(T.first[:]), "dfi", 2 ** 18, [line])
+    dma("Y", at("sti"), hbm(T.start[:]), "dst", 2 ** 16, [line])
+    dma("Y", at("fr", 0, WA), hbm(T.frag[:, 0:WA]), "dfa", 256 * WA, [line])
+    dma("Y", at("fr", W, W + K), hbm(T.frag[:, 0:K]), "dfa", 2 ** 14, [line, at("fr", 0, 1)])
+    dma("S", at("limi", 0, 5), hbm(T.lim[:]), "dlim", 2 ** 12)
+    add("G", lambda: g.iota(T.pi[:, 0:1], [[0, 1]], 0, 1), (), [at("pi", 0, 1)], 0.13)
+    iota(at("x144"), [[1, 144]])
+    iota(at("x32"), [[0, 2], [1, 32]])
+    iota(at("x16"), [[16, 32]])
+    iota(at("s5"), [[0, 4], [1, 96]])
+    iota(at("lvl"), [[-1, 5], [0, 32]], 4)
+
+    mset(at("ax", 0, 2752), 0.0)
+    act(at("ax", 2752, 5504), at("ax", 0, 2752))
+    mset(at("ax", 5504, 8240), 0.0)
+    cp(at("hl", 0, 512), at("fi"))
+    tt(at("hl", 512, 1024), at("fi"), at("hl", 0, 512), A.subtract)
+    for h in range(2):
+        dma("Y", view("ax", sl(AO, AO + W), part=sl(h, None, 16)), at("hl", 512 * h, 512 * h + 512), "dax", 2 ** 17, [line, at("ax")])
+    dma("Y", at("fr", WA, W), hbm(T.frag[:, WA:W]), "dfb", 256 * (W - WA), [line])
+    cp(at("stu"), at("sti"))
+
+    p0 = at("pi", 0, 1)
+    for i, (sh, msk) in enumerate([(4, 7), (0, 15), (1, 7), (0, 1), (1, 31), (6, 1), (3, 1), (0, 7)]):
+        ts(at("ci", i, i + 1), p0, sh, A.arith_shift_right, msk, A.bitwise_and)
+    cp(at("cf", 0, 8), at("ci"))
+    c = lambda i: at("cf", i, i + 1)
+    cg, ci_, cpair, ch, cj, ce, ck, cq = [c(i) for i in range(8)]
+    cp(c(8), p0)
+    ts(c(9), cg, 16.0, A.mult, 15.0, A.add)
+    ts(c(10), cpair, 0.0, A.is_equal)
+    ts(c(11), cpair, 1.0, A.is_equal)
+    ts(c(12), ch, -1.0, A.mult, 1.0, A.add)
+    ts(c(13), ck, -1.0, A.mult, 1.0, A.add)
+    ts(c(14), cg, 8.0, A.mult, cq, A.add)
+    ts(c(15), cj, 3.0, A.mult, 2.0, A.add)
+    ts(c(15), c(15), ce, A.subtract)
+    ts(c(16), ce, 2.0, A.mult, -1.0, A.add)
+    ts(c(17), ce, -1.0, A.add)
+    mk, mk2 = [c(12), ch], [c(13), ck]
+    ts(at("m0"), at("x144"), c(9), A.is_equal, c(10), A.mult)
+    ts(at("m1"), at("x144"), c(9), A.is_equal, c(11), A.mult)
+    ts(at("bo"), at("x144", 0, 8), cg, A.is_equal)
+    ts(at("idf"), at("x144", 0, 128), c(8), A.is_equal)
+    act(at("idb"), at("idf"))
+    act(at("idn"), at("idf"), scale=-1.0)
+    ts(at("gq"), at("x144", 0, 64), c(14), A.is_equal)
+    ts(at("rc"), at("s5"), c(15), A.is_equal)
+    ts(at("de"), at("x32"), cj, A.is_equal)
+    de = at("de", 0, 32)
+    act(at("dn"), at("de"), scale=-1.0)
+    act(at("dd", 0, 32), de, scale=c(16))
+    act(at("dd", 32, 64), at("dd", 0, 32), scale=-1.0)
+    mset(at("one"), 1.0)
+    mset(at("rk"), 0.0)
+    mset(at("rb"), 0.0)
+    act(view("ra", sl(None), 0), de, scale=c(17))
+    act(view("ra", sl(None), 1), view("ra", sl(None), 0), scale=-1.0)
+    act(view("rb", sl(None), 0), view("ra", sl(None), 1))
+    for u, k, x in [(4, 0, 1.0), (4, 1, 10.0), (5, 0, -1.0), (5, 1, 5.0)]:
+        act(view("rk", sl(None), u, k), de, scale=x)
+    act(view("rk", sl(None), 4, 2), view("ra", sl(None), 1), scale=0.5)
+    cp(at("limf", 1, 6), at("limi", 0, 5))
+    mset(at("limf", 0, 1), 0.0)
+    for h in range(2):
+        ts(view("lb", h, sl(0, 6)), at("limf", 0, 6), -1.0, A.mult, mk2[h], A.mult)
+        tt(view("la", h, sl(1, 6)), view("lb", h, sl(0, 5)), view("lb", h, sl(1, 6)), A.subtract)
+    ts(at("x16"), at("x16"), ci_, A.add)
+    wide = r in WIDE
+    tri = lambda t, a=0, b=192, c=None: at(["da", "db", "d1", "d1"][t - 1], a + 192 * (t == 4), b + 192 * (t == 4), c)
+    out = lambda t, a=0, b=192, c=None: at(["sa", "sc", "so", "so"][t - 1], a + 192 * (t == 4), b + 192 * (t == 4), c)
+    for t in range(3 if wide else 1, NS):
+        if t != 3 or not wide:
+            mset(tri(t, 96, 192, 3), -2.0 * CH)
+        mset(tri(t, 97, 192, 3), 1.0 * CH)
+        ts(tri(t, 98, 192, 3), at("x16"), 3.0 * CH if t == 3 and wide else 1.0 * CH, A.add)
+    for l, x in enumerate([1.0, 2.0, 2.0 + 2 * wide, 2.0]):
+        mset(at("slc", 32 * l, 32 * l + 32), x)
+    mset(nth("y0", 5, 0, 0, 1), 0.0)
+    if wide:
+        for i, x in enumerate([1.0, 3.0, -2.0, 1.0]):
+            mset(nth("da", 5, i, 1, 2), x * CH)
+        ts(nth("da", 5, 4, 1, 2), at("x16"), 1.0 * CH, A.add)
+        mset(at("db"), 0.0)
+        iota(at("sc"), [[0, 2], [1, 160]])
+        iota(at("x64"), [[0, 2], [1, 64]])
+        ts(c(18), cj, -5.0, A.mult, -3.0, A.add)
+        ts(c(19), cj, 5.0, A.mult, 4.0, A.add)
+        ts(c(19), c(19), ce, A.subtract)
+        ts(c(20), cj, 5.0, A.mult, 1.0, A.add)
+        ts(c(21), ce, -1.0, A.mult, 1.0, A.add)
+        ts(at("r1"), at("sc"), c(19), A.is_equal)
+        ts(at("r2"), at("sc"), c(20), A.is_equal, c(21), A.mult)
+        act(at("sa"), at("sc"), F.Abs, bias=c(18))
+        ts(at("r0"), at("sa"), 1.0, A.is_le, c(21), A.mult)
+        ts(at("pm"), at("x64"), c(8), A.is_equal)
+        act(at("pn"), at("pm"), scale=-1.0)
+    else:
+        mset(tri(1, 0, 96, 3), 0.0)
+    mset(view("jj", sl(0, 2)), 0.0)
+    mset(view("lx", 0), 0.25)
+    mset(at("sq", 0, 640, 4), 0.5)
+    mset(at("sq", 0, 640, 20), -0.25)
+    mset(at("rs"), 1.0)
+    mset(at("rs", 0, 640, 20), 0.0)
+    for name in ("h1", "xg", "c0", "v0"):
+        mset(at(name), 0.0)
+    mset(nth("h1", 5, 0, 0, 1), 2.0)
+    mset(nth("v0", 3, 2, 0, 4), 1.0)
+    mset(nth("v1", 3, 0, 0, 4), 0.0)
+    mset(at("f0"), 1.0)
+    mset(nth("f0", 5, 0, 0, 5), 0.0)
+    mset(nth("f1", 5, 2, 0, 1), 0.0)
+    mset(nth("f1", 5, 3, 4, 5), 0.0)
+    mset(nth("f1", 5, 4, 0, 3), 0.0)
+    mset(nth("f1", 5, 4, 3, 5), -1.0 * (r >= OPT["mrg"]))
+
+    axw = at("ax", AO, AO + W)
+    frw = at("fr", 0, W + K)
+
+    def extract(o, src, n0, n, m):
+        mm(o, [(at(m, 15 - i, 143 - i), at(src, n0 + i, n0 + n, 16)) for i in range(16)])
+
+    for k in (2, 3, 0, 1):
+        move("SV"[k % 2], at("gx", CH * k, CH * k + CH), gather(axw, at("stu", 32 * k, 32 * k + 32)))
+        if k % 2:
+            extract(at("pa", 0, 64), "gx", CH * (k - 1), 2 * CH, "m0")
+            cp(at("l0", 32 * k - 32, 32 * k + 32), at("pa", 0, 64))
+            ts(at("l0", 96 + 32 * k, 160 + 32 * k), at("pa", 0, 64), float(K), A.add)
+    for h in range(2):
+        dma("Y", view("ax", sl(AO - K, AO - K + W), part=sl(2 + h, None, 16)), at("hl", 512 * h, 512 * h + 512), "day", 2 ** 17, [line, at("ax")])
+        dma("Y", view("ax", sl(AO - K + W, AO + W), part=sl(2 + h, None, 16)),
+            view("hl", sl(512 * h, 512 * h + K), part=sl(0, None, 16)), "day", 2 ** 10, [line, at("ax")])
+    for k in WIDE:
+        move(OPT["xz"][k], at("gx", CH * k, CH * k + CH), gather(axw, at("l0", 32 * k, 32 * k + 32)))
+        ops[-1]["tau"] = OPT["txz"][k]
+    extract(at("px", 0, 64), "gx", 0, 2 * CH, "m0")
+    extract(at("px", 64, 128), "gx", 0, 2 * CH, "m1")
+    cp(at("l0", 256, 384), at("px", 0, 128))
+    ts(at("l0", 384, 512), at("px", 0, 128), float(K), A.add)
+
+    def first(p, e, k, a=0, b=32):
+        o = 128 * e + 32 * k if p == 0 else 256 + 128 * e + 64 * (p - 1) + 32 * k
+        return at("l0", o + a, o + b)
 
     place = {}
 
-    def vv(name, n=1, a=0, b=None):
+    def vv(name, n=1, a=0, b=None, buf="v"):
         if name not in place:
-            place[name] = sum(x[1] for x in place.values()), n
-        o = place[name][0]
-        return T.v[:, 32 * (o + a):32 * (o + (n if b is None else b))]
+            place[name] = sum(x[1] for x in place.values() if x[2] == buf), n, buf
+        o, n, buf = place[name]
+        return at(buf, 32 * (o + a), 32 * (o + (n if b is None else b)))
+
+    uu = lambda name, n=1, a=0, b=None: vv(name, n, a, b, "u")
 
     def wl(t, k, a, b):
-        if t == 1:
-            return T.l0[:, 32 * k + a:32 * k + b], (["l0a"] if k < 2 else ["l0own", "l0in"])
         o = ((t - 2) * 4 + k) * 64
-        return T.ls[:, o + a:o + b], ["ls%d_%d" % (t - 1, k)]
+        return at("ls", o + a, o + b) if t > 1 else first(0, 0, k, a, b)
+
+    def limit(t):
+        for h in range(2):
+            act(view("ll", t - 1, sl(None), h), view("jj", t - 1), scale=view("la", h, sl(t, t + 1)), bias=view("lb", h, sl(t, t + 1)))
+
+    def due(x, n=1):
+        for op in ops[-n:]:
+            op["tau"] = turn[0] + x
+
+    picked = lambda k, a, b: at("ab%d" % (k % 2), (2 + k // 2) * CH + a, (2 + k // 2) * CH + b)
 
     def bulk(t, k):
-        xs, st, ab, pe = T["xs%d" % k], T["st%d" % k], T["ab%d" % k], T["pe%d" % k]
-        o1, x0, fk = ((t - 1) * 4 + k) * 32, (2 * t - 1) * CH, ["fra", "frb"]
-        xk = lambda s, h: "x%d_%d_%d" % (k, s, h)
-        top = lambda h: (xs[:, h * H:h * H + H], [xk(0, h)]) if t == 1 else (st[:, h * H:h * H + H], ["st%d_%d" % (k, h)])
-
-        def red(v, rd):
-            for q in range(4):
-                mm(pe[:, 32 * v + q:32 * v + 32:4], ab[:, v * CH + q:v * CH + CH:4], T.bo[:], True, True, rd + ["bo"], ["pe%d" % k], 256)
-        for h in range(2):
+        xs, ab, pe = "xs%d" % k, "ab%d" % (k % 2), "pe%d" % (k % 2)
+        o1, x0 = ((t - 2) * 4 + k) * 32, (2 * t + (1 if k in WIDE else -1)) * CH
+        n = OPT["cut"]
+        w, lw = CH // n, 32 // n
+        top = lambda h: picked(k, h * w, h * w + w) if t > 1 else at(xs, h * w, h * w + w)
+        for h in range(n):
             if t == 1:
-                act(top(h)[0], frw.indirect(T.stu[:, 32 * k + 16 * h:32 * k + 16 * h + 16]), F.Copy, fk + ["stu"], top(h)[1] + ["os"], H, GA)
+                act(top(h), gather(frw, at("stu", 32 * k + lw * h, 32 * k + lw * h + lw)))
             else:
-                li, lk = wl(t, k, 32 + 16 * h, 48 + 16 * h)
-                act(top(h)[0], xs[:, (2 * t - 4) * CH:(2 * t - 1) * CH].indirect(li), F.Copy,
-                    lk + [xk(s, i) for s in range(2 * t - 4, 2 * t - 1) for i in range(2)], top(h)[1] + ["os"], H, GA)
-        li, lk = wl(t, k, 0, 32)
-        ts(T.lw[:, o1:o1 + 32], li, float(K), A.add, lk, ["lw%d_%d" % (t, k)])
-        for h in range(2):
-            li, lk = wl(t, k, 16 * h, 16 * h + 16)
-            tt(xs[:, x0 + h * H:x0 + h * H + H], frw.indirect(li), top(h)[0], A.add, fk + lk + top(h)[1], [xk(2 * t - 1, h), "ov"], H, GA)
-        act(ab[:, 0:CH], xs[:, x0:x0 + CH], F.Abs, [xk(2 * t - 1, 0), xk(2 * t - 1, 1)], ["a%d_0" % k], CH)
-        red(0, ["a%d_0" % k])
-        for h in range(2):
-            a = x0 + CH + h * H
-            tt(xs[:, a:a + H], frw.indirect(T.lw[:, o1 + 16 * h:o1 + 16 * h + 16]), top(h)[0], A.add,
-               fk + ["lw%d_%d" % (t, k)] + top(h)[1], [xk(2 * t, h), "ov"], H, GA)
-            act(ab[:, CH + h * H:CH + h * H + H], xs[:, a:a + H], F.Abs, [xk(2 * t, h)], ["a%d_1%d" % (k, h)], H)
-        red(1, ["a%d_10" % k, "a%d_11" % k])
+                act(top(h), gather(at(xs, x0 - (5 if k in WIDE and t < NS else 3) * CH, x0), wl(t, k, 32 + lw * h, 32 + lw * h + lw)))
+            due(0.16 * h - (OPT["pre"] if (k == r or t == 1) and (t, k) != (2, 2) else 0.0))
+        if t > 1:
+            ts(at("lw", o1, o1 + 32), wl(t, k, 0, 32), float(K), A.add)
+            due(0.01)
+        for e in range(2):
+            for h in range(n):
+                li = wl(t, k, lw * h, lw * h + lw)
+                if e:
+                    li = at("lw", o1 + lw * h, o1 + lw * h + lw) if t > 1 else first(0, 1, k, lw * h, lw * h + lw)
+                x = at(xs, x0 + e * CH + h * w, x0 + e * CH + h * w + w)
+                tt(x, gather(frw, li), top(h), A.add)
+                due(0.18 + 0.16 * (2 * e + h))
+                act(at(ab, e * CH + h * w, e * CH + h * w + w), x, F.Abs)
+                due(0.34 + 0.16 * (2 * e + h))
+        for a, b in ([(0, 96), (96, 128)] if OPT["pcut"] else [(0, 128)]):
+            for q in range(8):
+                mm(view(pe, sl(q, 64, 8), part=sl(a, b)), [(at(ab, 8 * a + q, 8 * b, 8), at("bo"))])
+                due(0.9 if b == 128 else 0.75)
+        hand(t, k, 64, 1 + OPT["e1" if (t, k) == (1, 3) else "ew" if k == r or (k + 1) % NR == r or t == 1 else "ev"])
+
+    def hand(t, k, n, when):
+        act(leaving(t, k) if k != r else landed(t, r, r), at("pe%d" % (k % 2), 0, n))
+        due(when)
         if k != r:
-            o, o2, key = ((t - 1) * 4 + k) * 64, ((t - 1) * 4 + r) * 64, "sb%d_%d" % (t, k)
-            if PLAN["ev"]:
-                cp(T.sb[:, o:o + 64], pe[:, 0:64], (), ["pe%d" % k, key])
-            else:
-                act(T.sb[:, o:o + 64], pe[:, 0:64], F.Copy, (), ["pe%d" % k, key])
-            send(T.rv[:, o2:o2 + 64], T.sb[:, o:o + 64], [k], "sh%d" % t, [key])
-        else:
-            lim, lk = (T.lz[:, 32 * (t - 1):32 * t], ["lz"]) if t < 3 else (vv("tn"), ["tn"])
-            for v in range(2):
-                tt(T.pre[:, 32 * v:32 * v + 32], pe[:, 32 * v:32 * v + 32], lim, A.subtract, lk, ["pe%d" % k, "pre%d" % v])
+            send(landed(t, r, k), leaving(t, k), [k], "sh%d_%d" % (t, r), 0.5 * (n > 64))
+            due(when + 0.01)
+
+    def opening(k):
+        xs, ab, pe = "xs%d" % k, "ab%d" % (k % 2), "pe%d" % (k % 2)
+        for h in range(2):
+            act(at(xs, h * H, h * H + H), gather(frw, at("stu", 32 * k + 16 * h, 32 * k + 16 * h + 16)))
+            due(0.08 * h - OPT["pra"] - OPT["sw"] * k)
+        for p in range(3):
+            lead = OPT["sw"] * (-k if p == 0 else (1 - k) * 0.4)
+            for e in range(2):
+                n = 2 if (p, e) in OPT["half"] else 1
+                for h in range(n):
+                    a, b, a0 = CH // n * h, CH // n * (h + 1), 2 * CH * (p % 2) + CH * e
+                    x = at(xs, (2 * p + e + 1) * CH + a, (2 * p + e + 1) * CH + b)
+                    tt(x, gather(frw, first(p, e, k, a // 16, b // 16)), at(xs, p * CH + a, p * CH + b), A.add)
+                    due(lead + 0.1 + 0.15 * (2 * p + e) + 0.07 * h)
+                    act(at(ab, a0 + a, a0 + b), x, F.Abs)
+                    due(lead + 0.2 + 0.15 * (2 * p + e) + 0.07 * h)
+            for q in range(8):
+                mm(at(pe, 64 * p + q, 64 * p + 64, 8), [(at(ab, 2 * CH * (p % 2) + q, 2 * CH * (p % 2 + 1), 8), at("bo"))])
+                due(lead + 0.45 + 0.3 * p)
+        hand(2, k, 192, lead + 1 + OPT["ea_"] if k < 1 else 5 + OPT["e3"])
 
     def look(t):
-        li, lk = wl(t, r, 0, 32)
-        act(T.gx[:, 0:CH], axw.indirect(li), F.Copy, ["ax"] + lk, ["gxa"], CH, GA)
-        extract(0, CH, 0, T.m0, "m0", ["gxa"])
-        extract(0, CH, 32, T.m1, "m1", ["gxa"])
-        act(T.d1[:, 2:96:3], T.pa[:, 0:32], F.Copy, (), ["pa", "d1a"])
-        act(T.pb[:, 32 * t:32 * t + 32], T.pa[:, 32:64], F.Copy, (), ["pa", "b%d" % t])
-        tt(T.d1[:, 0:96:3], T.pb[:, 32 * (t - 1):32 * t], T.pb[:, 32 * t:32 * t + 32], A.subtract, ["b%d" % (t - 1), "b%d" % t], ["d1c"])
-        tt(T.d1[:, 1:96:3], T.pb[:, 32 * t:32 * t + 32], T.d1[:, 2:96:3], A.subtract, ["d1a", "b%d" % t], ["d1b"])
+        n = OPT["lcut"]
+        for h in range(n):
+            move(OPT["look"][h % len(OPT["look"])], at("gl", CH // n * h, CH // n * (h + 1)), gather(axw, wl(t, r, 32 // n * h, 32 // n * (h + 1))))
+        extract(at("pa", 0, 32), "gl", 0, CH, "m0")
+        extract(at("pa", 32, 64), "gl", 0, CH, "m1")
+        act(tri(t, 2, 96, 3), at("pa", 0, 32))
+        act(at("pb", 32 * t, 32 * t + 32), at("pa", 32, 64))
+        if t > 1:
+            tt(tri(t, 0, 96, 3), nth("sc", 5, 4, 0, 1) if t == 3 and wide else at("pb", 32 * (t - 1), 32 * t), at("pb", 32 * t, 32 * t + 32), A.subtract)
+        tt(tri(t, 1, 96, 3), at("pb", 32 * t, 32 * t + 32), tri(t, 2, 96, 3), A.subtract)
+
+    def look2():
+        for p in (1, 2):
+            move(OPT["lk2"][p - 1], at("gl", CH * p - CH, CH * p), gather(axw, first(p, 0, r)))
+            ops[-1]["tau"] = OPT["tl2"][r] + 0.3 * p
+        extract(at("pa", 0, 64), "gl", 0, 2 * CH, "m0")
+        extract(at("pa", 64, 128), "gl", 0, 2 * CH, "m1")
+        a1, a2, b1, b2 = [at("pa", 32 * i, 32 * i + 32) for i in range(4)]
+        da, db = (lambda i: nth("da", 5, i, 0, 1)), (lambda l, i: nth("db", 5, i, l, l + 1))
+        cp(db(1, 4), first(1, 0, r))
+        cp(vv("z"), first(2, 0, r))
+        tt(db(1, 1), vv("z"), db(1, 4), A.subtract)
+        act(da(4), a1)
+        act(vv("a2"), a2)
+        act(db(0, 4), b1)
+        tt(da(3), b1, da(4), A.subtract)
+        tt(da(0), b2, vv("a2"), A.subtract)
+        tt(db(0, 1), b2, db(0, 4), A.subtract)
+        tt(da(2), vv("z"), db(0, 4), A.subtract)
+        tt(da(1), vv("a2"), vv("z"), A.subtract)
+
+    def decide2():
+        for p in range(3):
+            mm(at("pz", 64 * p, 64 * p + 64), [(view("ll", min(p, 1)), at("gq"))])
+        act(at("lz"), at("pz", 0, 192))
+        mm(at("pq", 0, 192), [(at("idf"), at("lz"))] + [(at("idf"), landed(2, k, r)) for k in [r] + ring[::OPT["rev"]]])
+        d = 0
+        due(d, 3)
+        for h in range(2):
+            ts(view("lx", sl(1, 4), sl(None), h), at("pq", 0, 192), 0.0, A.is_gt, mk[h], A.mult)
+        mm(at("pc", 0, 320), [(view("lx", 1 + p), at("r%d" % p)) for p in range(3)])
+        ts(at("cb"), at("pc", 0, 320), 1.0, A.min)
+        scan(at("sa"), at("cb"), at("da"))
+        cp(wl(3, r, 0, 64), nth("sa", 5, 4, 0, 2))
+        send(wl(3, r, 0, 64), wl(3, r, 0, 64), ring, "li2_%d" % r)
+        due(d, 9)
+        due(d + OPT["gap"], 4)
+        turn[:] = 99, 0
+        scan(at("sc"), at("cb"), at("db"))
+        act(at("wv", 32, 64), nth("sc", 5, 4, 1, 2))
+        act(at("wv", 64, 96), nth("sa", 5, 4, 0, 1))
+        act(at("d1", 96, 192, 3), nth("cb", 5, 2, 0, 1), scale=2.0 * CH, bias=-4.0 * CH)
+        mm(at("py", 0, 128), [(at("idb"), view("lx", 2)), (at("pn"), view("lx", 1))])
+        mm(at("py", 128, 256), [(at("idb"), view("lx", 3)), (at("pm"), view("lx", 1))])
+        act(view("lx", 4), at("py", 0, 128), F.Relu)
+        act(view("lx", 5), at("py", 128, 256), F.Relu, bias=-1.0)
+        lost(2)
+
+    bits = lambda s: [view("lx", 4), view("lx", 5)] if s == 2 and wide else [view("lx", s + 3 * (s > 2))]
+
+    def lost(t):
+        mm(at("pz", 0, 64), [(at("idn"), at("one"))] + [(x, at("de")) for x in bits(t)])
+        tt(view("jj", t), at("pz", 0, 64), view("jj", t - 1), A.max)
+        limit(t + 1)
 
     def decide(t):
-        o = [((t - 1) * 4 + k) * 64 for k in others]
-        rk = ["rv%d" % t]
-        tt(T.ta[:], T.rv[:, o[0]:o[0] + 64], T.rv[:, o[1]:o[1] + 64], A.add, rk, ["ta"], 64)
-        tt(T.tb[:], T.rv[:, o[2]:o[2] + 64], T.pre[:], A.add, rk + ["pre0", "pre1"], ["tb"], 64)
-        tt(T.te[:], T.ta[:], T.tb[:], A.add, ["ta", "tb"], ["te"], 64)
-        for a in range(4):
-            ts(T.lx[:, :, a, :], T.te[:], 0.0, A.is_gt, ["te", "mk"], ["lx%d" % a], T.mk[:, a:a + 1], A.mult)
+        mm(at("pq", 0, 64), [(view("ll", t - 1), at("gq"))] + [(at("idf"), landed(t, k, r)) for k in [r] + ring[::OPT["rev"]]])
+        due(0, 3)
+        for h in range(2):
+            ts(view("lx", t + 3 * (t > 2), sl(None), h), at("pq", 0, 64), 0.0, A.is_gt, mk[h], A.mult)
         n = 192 if t < NS else 384
-        lk, key = ["lx%d" % a for a in range(4)], "ls%d_%d" % (t, r)
-        mm(T.pc[:, 0:n], T.lx[:, 0:8], T.rc0[:, 0:n], True, False, lk + ["rc0"], ["pc"], n)
-        mm(T.pc[:, 0:n], T.lx[:, 8:16], T.rc1[:, 0:n], False, True, lk + ["rc1"], ["pc"], n)
+        mm(at("pc", 0, n), [(bits(t)[0], at("rc", 0, n))])
         if t < NS:
-            o, ol = (t - 1) * 192, ((t - 1) * 4 + r) * 64
-            scan(T.so[:, o:o + 192], T.pc[:, 0:192], T.d1[:], ["d1a", "d1b", "d1c", "d1s"], ["pc", "so%d" % t], 192)
-            cp(T.ls[:, ol:ol + 64], T.so[:, o + 2:o + 192:3], ["so%d" % t], [key])
-            send(T.ls[:, ol:ol + 64], T.ls[:, ol:ol + 64], ring, "li%d_%d" % (t, r), [key])
+            scan(out(t), at("pc", 0, 192), tri(t))
+            cp(wl(t + 1, r, 0, 64), out(t, 2, 192, 3))
+            send(wl(t + 1, r, 0, 64), wl(t + 1, r, 0, 64), ring, "li%d_%d" % (t, r))
+            due(0, 6)
+            due(OPT["g1"], 3)
+            due(OPT["g2"], 2)
         else:
-            scan(T.s5[:], T.pc[:, 0:384], T.d5[:], ["d5_%d" % i for i in range(12)], ["pc", "s5"], 384)
-            cp(T.fin[:, 128 * r:128 * r + 128], T.s5[:, 2:384:3], ["s5"], [key], 128)
-            send(T.fin[:, 128 * r:128 * r + 128], T.fin[:, 128 * r:128 * r + 128], ring, "li5_%d" % r, [key], 0.5)
-
-    def books(t):
-        val = lambda x: (vv(x), [x]) if isinstance(x, str) else x
-
-        def b2(o, a, b, op):
-            (oa, ok), (aa, ak), (ba, bk) = val(o), val(a), val(b)
-            tt(oa, aa, ba, op, ak + bk, ok)
-
-        def b1(o, a, s1, op0, s2=None, op1=None):
-            (oa, ok), (aa, ak) = val(o), val(a)
-            if op0 in (A.mult, A.add) and op1 in (None, A.add) and "sti" not in ak:
-                affine(oa, aa, s1 if op0 == A.mult else 1.0, s1 if op0 == A.add else s2 or 0.0, ak, ok)
+            m = 3 * ends(r)[0][2]
+            scan(at("s5", 0, m), at("pc", 0, m), at("d5", 0, m))
+            cp(ends(r)[0], at("s5", 2, m, 3))
+            send(ends(r)[0], ends(r)[0], ring, "li5_%d" % r, m / 1500 - 0.15)
+            due(0, 6)
+            due(OPT["g1"], 3)
+            due(OPT["g2"], 2)
+            turn[:] = OPT["fin"], 0
+            scan(at("s5", m, 384), at("pc", m, 384), at("d5", m, 384))
+            if r >= OPT["mrg"]:
+                act(ends(r)[2], at("s5", m + 2, 384, 3))
+                send(ends(r)[2], ends(r)[2], ring, "ea%d" % r, 0.3)
             else:
-                ts(oa, aa, s1, op0, ak, ok, s2, op1)
-
-        n0 = lambda s: (T.nb[:, (s - 1) * 96 + 2:s * 96:3], ["nb%d" % s])
-        n1 = lambda s: (T.nb[:, (s - 1) * 96 + 1:s * 96:3], ["nb%d" % s])
-        wv = lambda s: "w1" if s == 1 else (T.so[:, (s - 2) * 192 + 2:(s - 2) * 192 + 96:3], ["so%d" % (s - 1)])
-        d4 = lambda l, j: (T.d4[:, 96 * l + j:96 * l + 96:3], ["d4_%d" % (3 * l + j)])
-        d5 = lambda l, j: (T.d5[:, 96 * l + j:96 * l + 96:3], ["d5_%d" % (3 * l + j)])
-        s4 = lambda l, n=1: (T.s4[:, 96 * l + 2:96 * (l + n):3], ["s4_%d" % i for i in range(l, l + n)])
-        es = lambda l: (T.es[:, 96 * r + 32 * l:96 * r + 32 * l + 32], ["eo%d" % l])
-        part = lambda name, n, a, key: (vv(name, n, a, a + 1), [key])
-        x16 = (T.x16[:], ["x16"])
-        sub, mul, plus = A.subtract, A.mult, A.add
-
-        def wrap16(name, wk, ck):
-            a, b = (vv(name, 2), [name]), (vv(name + "t", 2), [name + "t"])
-            b1(a, ck, float(K), mul)
-            b2(a, a, wk, plus)
-            b1(b, a, float(W), A.is_ge, float(W), mul)
-            b2(a, a, b, sub)
-            b1(a, a, 16.0, mul, 1.0, plus)
-
-        act(T.nb[:, (t - 1) * 96:t * 96], T.pc[:, 0:96], F.Copy, (), ["pc", "nb%d" % t], 96)
-        if t >= 2:
-            b2("mx" if t == 2 else "mn", (T.te[:, 0:32], ["te"]), (T.te[:, 32:64], ["te"]), A.min)
-            if t > 2:
-                b2("mx", "mx", "mn", A.max)
-            b1("rz", "mx", 0.0, A.is_gt)
-            b2("rz", "rz", (T.dl[:, 32 * (t - 1):32 * t], ["dl"]), mul)
-            b2("tn", "rz", (T.lz[:, 32 * t:32 * t + 32], ["lz"]), plus)
-        if t < 4:
-            b2("z%d" % t, n0(t), n1(t), mul)
-        b2("ns%d" % t, n0(t), n1(t), A.max)
-        if t == 1:
-            li, lk = wl(1, r, 0, 32)
-            cp(vv("w1"), li, lk, ["w1"])
-            b1("v0", (T.sti[:, 32 * r:32 * r + 32], ["sti"]), 16.0, mul, 2.0, plus)
-        if t == 2:
-            b2("r2", "z2", "ns1", A.is_gt)
-            b2("a", n0(1), n0(2), plus)
-            b2("dd2", "z2", "r2", sub)
-            b2("k1", "ns1", "r2", plus)
-            b2("c1", n0(1), "r2", A.max)
-            b2("wd", wv(3), wv(2), sub)
-            b2("D2", "dd2", "z1", A.is_gt)
-            b2("dd2", "dd2", "z1", plus)
-            b2("wd", "wd", "r2", mul)
-            b1("aa", "a", 0.0, A.is_equal, 1.0, plus)
-            b1("ka", "a", 0.0, A.is_equal)
-            b1("ne", "a", 1.0, A.not_equal)
-            b2("b1", "D2", n0(1), A.is_gt)
-            b1(part("ws12", 2, 0, "ws1"), "w1", 0.0, plus)
-            b2(part("ws12", 2, 1, "ws2"), "wd", wv(2), plus)
-            b1("sl2", "r2", 2.0, mul, 3.0, plus)
-        if t == 3:
-            cc1, cc2 = part("c12", 2, 0, "cc1"), part("c12", 2, 1, "cc2")
-            b2("r3", "z3", "ns2", A.is_gt)
-            b2("o", "a", n0(3), plus)
-            b2("q1", n0(3), n0(2), sub)
-            b2("wd", wv(4), wv(3), sub)
-            b2("dd3", "z3", "r3", sub)
-            b2("rho", "r2", "r3", plus)
-            b2("D3", "dd3", "dd2", A.is_gt)
-            b2("dd3", "dd3", "dd2", plus)
-            b2("o", "o", "rho", plus)
-            b2("q1", "q1", "rho", mul)
-            b2("wd", "wd", "rho", mul)
-            b2("F3", "D3", "k1", A.is_gt)
-            b1("al3", "dd3", 0.0, A.is_equal)
-            b2("o", "o", "rho", plus)
-            b2(cc2, "q1", n0(2), plus)
-            b2(part("ws34", 2, 0, "ws3"), "wd", wv(3), plus)
-            b1(part("ws34", 2, 1, "ws4"), wv(4), 0.0, plus)
-            b2(cc1, "c1", "F3", A.max)
-            b2("ge1", "D2", "F3", plus)
-            b1("t1", "o", 4.0, A.is_equal)
-            b1("t3", "o", 2.0, A.is_le)
-            b1("nr", "o", 1.0, A.is_gt)
-            b2("ge1", "ge1", "al3", plus)
-            wrap16("V12", (vv("ws12", 2), ["ws1", "ws2"]), (vv("c12", 2), ["cc1", "cc2"]))
-            b2("nr", "nr", "ns3", A.max)
-            b1("q2", cc1, -2.0, plus)
-            b2("u1", "al3", cc2, mul)
-            b2("nt3", "nr", "t3", mul)
-            b2("q2", "q2", "ge1", mul)
-            b2("b1", "b1", "u1", plus)
-            b2("dr", "nt3", "aa", mul)
-            b2(es(0), "v0", "q2", plus)
-            b2("b1", "b1", part("V12", 2, 0, "V12"), plus)
-            b2("b1", "b1", "ge1", mul)
-            b1("u2", "rho", -1.0, mul, 4.0, plus)
-            b2(d4(0, 2), "u2", "al3", mul)
-            b2("at1", "al3", "t1", mul)
-            b2("u3", "t1", "dr", sub)
-            b1(d4(0, 1), "at1", -1.0, mul)
-            b1("u3", "u3", -1.0, plus)
-            b2(d4(0, 0), "u3", "al3", mul)
-            b2("q3", "t3", "ne", mul)
-            b2("q3", "q3", "t1", plus)
-            b1("q3", "q3", -1.0, mul, 2.0, plus)
-            b2("q3", "q3", "nr", mul)
-            for l in (1, 2):
-                mset(d4(l, 2)[0], 0.0, d4(l, 2)[1])
-                b1(d4(l, 1), "t1", 0.0, plus)
-                b2(d4(l, 0), "q3", "t1", sub)
-            b1("rr", "nr", -1.0, mul, 1.0, plus)
-            b2(d4(3, 2), n0(3), "rho", A.is_gt)
-            b1(d4(3, 1), "rho", 0.0, plus)
-            b2("q4", "rr", n0(3), A.is_gt)
-            b2(d4(3, 0), "q4", "rho", A.is_gt)
-            for j in range(3):
-                mset(d4(4, j)[0], float(j == 1), d4(4, j)[1])
-            b1("u4", "o", -1.0, mul, 4.0, plus)
-            b2(d4(5, 2), "u4", "al3", mul)
-            b2(d4(5, 1), "at1", "al3", sub)
-            b1("u5", "o", -1.0, mul, 1.0, plus)
-            b2("tb5", d4(5, 2), d4(5, 1), plus)
-            b2("u5", "u5", "rr", mul)
-            b2("u5", "u5", "al3", mul)
-            b2(d4(5, 0), "u5", "tb5", sub)
-            b1(d4(6, 2), "rho", 0.0, plus)
-            mset(d4(6, 1)[0], 0.0, d4(6, 1)[1])
-            b1(d4(6, 0), "rr", 0.0, plus)
-            b2("cur", (T.so[:, 482:576:3], ["so3"]), x16, sub)
-            b1("sl1", cc1, 1.0, plus)
-            b1("cur", "cur", 1.0 / CH, mul, 4.0, plus)
-            b2("yp", "sl1", "ge1", mul)
-            b2("sl2", "sl2", cc2, plus)
-            b1("u6", "yp", -1.0, mul, 7.0, plus)
-            b1("q5", "cur", -8.0, plus)
-            b2("s3", "sl1", "sl2", sub)
-            b2("u6", "u6", "al3", mul)
-            b2("q5", "q5", "t1", mul)
-            b2(d4(7, 2), "u6", "yp", plus)
-            b1("u7", "q5", 1.0, plus)
-            b2("s3", "s3", "ka", mul)
-            b2(d4(7, 1), "u7", "al3", mul)
-            b2("s3", "s3", "sl2", plus)
-            b1("u8", "cur", -1.0, mul, 6.0, plus)
-            b2("s3", "s3", "cur", sub)
-            b2("u8", "u8", "rr", mul)
-            b2("s3", "s3", "nt3", mul)
-            b2("u8", "u8", "cur", plus)
-            b2("s3", "s3", "q5", sub)
-            b2("u8", "u8", "s3", plus)
-            b1("u8", "u8", -8.0, plus)
-            b2(d4(7, 0), "u8", "al3", mul)
-            b1("sib", wv(4), float(W - K), A.is_ge, float(W), mul)
-            b2("sib", wv(4), "sib", sub)
-            b1("sib", "sib", 16.0, mul, 16.0 * K + 1.0, plus)
-            b1("yc", "cur", -1.0 * CH, mul, 8.0 * CH, plus)
-        if t == 4:
-            for l in range(8):
-                scan(T.s4[:, 96 * l:96 * l + 96], T.nb[:, 288:384], T.d4[:, 96 * l:96 * l + 96],
-                     ["nb4"] + ["d4_%d" % (3 * l + j) for j in range(3)], ["s4_%d" % l])
-            ge = lambda i, n=1: (vv("ge", 3, i, i + n), ["ge_%d" % j for j in range(i, i + n)])
-            for i in range(3):
-                b1(ge(i), s4(0), 2.0 + i, A.is_ge)
-            for i, x in enumerate(["al", "g2", "g3", "g4"]):
-                b1(x, s4(5), 1.0 + i, A.is_ge)
-            b1("p1", s4(0), 1.0, A.is_equal, -1.0, plus)
-            bb = (vv("bb", 2), ["bb"])
-            b2(bb, s4(3, 2), s4(1, 2), sub)
-            b2(es(1), "b1", "p1", plus)
-            wrap16("V34", (vv("ws34", 2), ["ws3", "ws4"]), s4(3, 2))
-            b2(bb, bb, ge(1, 2), mul)
-            b2("e1", "al", s4(6), mul)
-            b2("gs", "g4", "ns4", A.is_gt)
-            b1("wa", wv(5), 16.0, mul, 1.0, plus)
-            b1("wb", wv(5), float(W - K), A.is_ge, float(W), mul)
-            b2(bb, bb, s4(1, 2), plus)
-            b2("e0", "al", "e1", sub)
-            b2("wb", wv(5), "wb", sub)
-            b2("p2", part("bb", 2, 0, "bb"), part("V12", 2, 1, "V12"), plus)
-            b2("p3", part("bb", 2, 1, "bb"), part("V34", 2, 0, "V34"), plus)
-            b2("k4", part("V34", 2, 1, "V34"), ge(2), mul)
-            b1("wb", "wb", 16.0, mul, 16.0 * K + 1.0, plus)
-            b2("p2", "p2", ge(0), mul)
-            b2("p3", "p3", ge(1), mul)
-            b2("x1", "e1", "wa", mul)
-            b2("x0", "e0", "wa", mul)
-            b1(es(2), "p2", -1.0, plus)
-            send(T.es[:, 96 * r:96 * r + 96], T.es[:, 96 * r:96 * r + 96], ring, "ea%d" % r, ["eo0", "eo1", "eo2"], 0.4)
-            b1(d5(1, 2), "p3", -1.0, plus)
-            b1(d5(1, 1), "e1", 0.0, plus)
-            b2("p4", "g3", "g4", plus)
-            b2(d5(1, 0), "p4", "gs", sub)
-            b2("wb", "wb", "g2", mul)
-            b1(d5(3, 2), "x0", -1.0, plus)
-            b2(d5(3, 1), "wb", "x0", sub)
-            b1(d5(3, 0), "wb", -1.0, mul)
-            b2("p5", "k4", "x1", plus)
-            b1(d5(2, 2), "p5", -1.0, plus)
-            b2(d5(2, 1), "e0", "x1", sub)
-            b1("k5", "k4", 2.0, plus)
-            b2("sib", "sib", "gs", mul)
-            b2("k5", "k5", "g3", mul)
-            b2("sib", "sib", "g2", plus)
-            b2(d5(2, 0), "sib", "k5", sub)
-            b1("ya", s4(7), -1.0 * CH, mul, 9.0 * CH, plus)
-            b1("yb", s4(7), -1.0 * CH, mul, 10.0 * CH, plus)
-            b1("y0", s4(7), 1.0 * CH, mul)
-            b2("ya", "ya", "al", mul)
-            b2("yb", "yb", "g2", mul)
-            b2("p6", "cur", s4(7), sub)
-            b2("yc", "yc", "gs", mul)
-            b2("p6", "p6", "g3", mul)
-            b2(d5(0, 1), "yb", "ya", sub)
-            b2("y0", "y0", "ya", plus)
-            b1("p6", "p6", 1.0 * CH, mul)
-            b2("yc", "yc", "yb", sub)
-            b2(d5(0, 2), "y0", x16, plus)
-            b2(d5(0, 0), "p6", "yc", plus)
-
-    look(1)
-    for t in range(1, NS + 1):
-        for k in range(NR):
-            bulk(t, k)
-        decide(t)
+                cp(at("fin", 224 * r + 32, 224 * r + 128), at("s5", m + 2, 384, 3))
+                send(ends(r)[1], ends(r)[1], ring, "fi%d" % r, 0.3)
+        turn[:] = 99, 0
         if t < NS:
-            books(t)
+            act(at("wv", 32 * t, 32 * t + 32), out(t, 2, 96, 3))
+        if 1 < t < NS:
+            lost(t)
+
+    def books():
+        al_, I, N = sl(None), at("idb"), at("idn")
+        by = lambda s, x: [(b, x) for b in bits(s)]
+        sub, mul, plus = A.subtract, A.mult, A.add
+        mm(at("px", 0, 480), [x for s in range(5) for x in by(s, view("rk", al_, sl(4 - s, 9 - s)))])
+        for k, b in enumerate([-1.0, -20.0, 0.0]):
+            act(at("sq", 1 + k, 640, 4), at("px", k, 480, 3), F.Relu, bias=b)
+        scan(at("ro"), at("rs"), at("sq"))
+        ts(at("h0"), at("ro", 3, 640, 4), 4.0, A.is_gt)
+        nc = lambda s: nth("h0", 5, s, 0, 1)
+        rr = lambda s: nth("sq", 20, 4 * s + 1, 0, 1)
+        for i, s, b in [(0, 1, 2.0), (0, 2, 8.0), (0, 3, 8.0), (1, 2, 6.0), (1, 3, 6.0)]:
+            act(nth("h1", 5, s, i, i + 1), nth("ro", 20, 4 * s + 3 - i, 0, 1), F.Relu, scale=-2.0, bias=b)
+        for i in range(2):
+            scan(at("ho", 160 * i, 160 * i + 160), at("h0"), at("h1", 160 * i, 160 * i + 160))
+        ts(uu("ge", 2), nth("ho", 5, 4, 0, 2), 3.0, A.is_ge)
+        ts(uu("eq", 2), nth("ho", 5, 4, 0, 2), 3.0, A.is_equal)
+        act(uu("mn"), nth("ho", 5, 4, 0, 1), F.Relu, scale=-1.0, bias=2.0)
+        mm(at("pz", 0, 64), by(3, at("de")) + by(2, at("dd")) + by(1, at("dn")))
+        act(nth("xg", 2, 1, 0, 2), at("pz", 0, 64), F.Relu, bias=-2.0)
+        xa, xb = nth("xg", 2, 1, 0, 1), nth("xg", 2, 1, 1, 2)
+        jc = lambda l: nth("c0", 2, 1, l - 1, l)
+        act(jc(1), rr(2))
+        tt(uu("r3"), rr(3), nc(3), A.is_gt)
+        tt(jc(2), rr(2), rr(3), plus)
+        tt(uu("r4"), rr(4), nc(4), A.is_gt)
+        tt(jc(3), uu("r4"), jc(2), plus)
+        tt(jc(4), uu("r4"), jc(2), plus)
+        act(nth("v0", 3, 1, 1, 3), nth("c0", 2, 1, 0, 2))
+        g3, g5 = uu("ge", 2, 0, 1), uu("ge", 2, 1, 2)
+        mm(at("pz", 0, 32), [(N, xa), (N, xb), (I, rr(2))] + [(I, nc(s)) for s in range(1, 5)]
+           + [(I, uu("r3")), (I, uu("r4")), (I, g3), (I, g5)])
+        for l in range(1, 5):
+            ts(nth("y0", 5, 5 - l, 0, 1), at("pz", 0, 32), 4.0 - l, A.is_le)
+        for l in range(1, 5):
+            mm(at("py", 64 * l - 64, 64 * l), by(l, at("ra")) + by(l + 1, at("rb")) * (l < 4)
+               + [(I, at("xg", 0, 64)), (I, at("xg", 64, 128))] * (l == 1))
+        scan(at("co"), at("c0"), at("py", 0, 256))
+        cl = nth("co", 2, 1, 0, 4)
+        slot = lambda l: [nth("co", 2, 1, l - 1, l)] + [jc(l - 1)] * 2 * (l in (2, 3)) + [jc(1), nth("cb", 5, 2, 0, 1)] * 2 * (l == 2 and wide)
+        for l in range(4, 0, -1):
+            mm(at("py", 260 - l, 416, 5), [(I, at("slc", 32 * l - 32, 32 * l))] + [(I, x) for x in slot(l)] + [(N, x) for x in slot(l - 1) if l > 1])
+        mm(at("py", 260, 416, 5), [(I, nth("xg", 2, 0, 0, 1))])
+        scan(at("y1"), at("y0"), at("py", 256, 416))
+        for i in range(4):
+            ts(vv("gg", 4, i, i + 1), nth("ro", 20, 19, 0, 1), 3.5 - 0.5 * i, A.is_le)
+        al, g2, g3, g4 = [vv("gg", 4, i, i + 1) for i in range(4)]
+        d5 = lambda l, j: nth("d5", 3, j, l, l + 1)
+        gs, ka = vv("gs"), 9.0 + 2 * wide
+        tt(gs, g4, at("pc", 1, 96, 3), A.is_gt)
+        act(vv("m2"), al, scale=-1.0 * CH, bias=1.0 * CH)
+        act(vv("n2"), al, scale=ka * CH)
+        act(vv("n1"), g2, scale=(ka + 1) * CH)
+        act(vv("g6"), gs, scale=3.0 * CH)
+        act(vv("c3"), nth("co", 2, 1, 2, 3), scale=1.0 * CH, bias=(ka - 4) * CH)
+        act(vv("gc", 3), vv("gg", 4, 0, 3), scale=1.0 * CH)
+        tt(vv("m0", 2), vv("gc", 3, 0, 2), vv("gc", 3, 1, 3), sub)
+        tt(vv("c3"), vv("c3"), g3, mul)
+        tt(vv("g6"), vv("g6"), vv("n1"), sub)
+        tt(vv("n1"), vv("n1"), vv("n2"), sub)
+        tt(vv("n2"), vv("n2"), at("x16"), plus)
+        tt(vv("c3"), vv("c3"), vv("g6"), plus)
+        for j, m, n in [(0, vv("m0", 2, 1, 2), "c3"), (1, vv("m0", 2, 0, 1), "n1"), (2, vv("m2"), "n2")]:
+            tt(vv("t%d" % j), m, nth("y1", 5, 4, 0, 1), mul)
+            tt(d5(0, j), vv("t%d" % j), vv(n), plus)
+        g3u = uu("ge", 2, 0, 1)
+        mm(at("pz", 32, 64), [(N, uu("mn")), (N, uu("eq", 2, 0, 1)), (N, uu("eq", 2, 1, 2)), (N, nc(4)), (I, g3u)]
+           + [(N, xa)] * 2 + [(N, xb)] * 3)
+        act(uu("db", 2), at("pz", 0, 64))
+        for l in range(5):
+            mm(at("pz", 32 * l, 32 * l + 32), [(I, uu("db", 2, 0, 1))])
+            mm(at("pz", 160 + 32 * l, 192 + 32 * l), [(I, uu("db", 2, 1, 2))])
+        tt(nth("f0", 5, 1, 0, 5), at("pz", 0, 160), at("lvl"), A.is_equal)
+        tt(nth("f0", 5, 4, 0, 5), at("pz", 0, 160), at("lvl"), A.is_le)
+        act(nth("f1", 5, 0, 0, 5), at("pz", 160, 320), bias=2.0)
+        plain = r >= OPT["mrg"]
+        unit = 16.0 if plain else 4.0
+        act(nth("f1", 5, 3, 0, 4), cl)
+        act(nth("v1", 3, 2, 0, 4), cl, scale=float(K))
+        ws = lambda a, b: at("wv", 32 * a - 32, 32 * b - 32)
+        cp(ws(1, 2), first(0, 0, r))
+        act(nth("v1", 3, 1, 0, 4), ws(1, 5))
+        tt(nth("v1", 3, 0, 1, 3), ws(3, 5), ws(2, 4), sub)
+        scan(at("vo"), at("v0"), at("v1"))
+        for a, b, x in [(1, 3, 4.0), (3, 5, unit)] if plain else [(1, 5, 4.0)]:
+            ts(nth("f1", 5, 2, a, b), nth("vo", 3, 2, a - 1, b - 1), float(W), A.is_ge, -x * W, mul)
+            act(nth("f1", 5, 1, a, b), nth("vo", 3, 2, a - 1, b - 1), scale=x, bias=1.0)
+        ts(nth("f1", 5, 1, 0, 1), at("sti", 32 * r, 32 * r + 32), 4.0, mul, 1.0, plus)
+        scan(at("fo"), at("f0"), at("f1"))
+        cp(at("fin", 224 * r + 128, 224 * r + 224), nth("fo", 5, 4, 0, 3))
+        if plain:
+            turn[0] = OPT["ea"]
+            send(ends(r)[1], ends(r)[1], ring, "fi%d" % r, 0.05)
+            turn[0] = 99
+        s3, s4 = nth("fo", 5, 4, 3, 4), nth("fo", 5, 4, 4, 5)
+        e0, e1 = vv("e0"), d5(1, 1)
+        tt(e1, al, jc(3), mul)
+        tt(e0, al, e1, sub)
+        act(vv("wa"), ws(5, 6), scale=unit, bias=1.0)
+        act(vv("wb", 2), ws(4, 6), scale=unit, bias=unit * K + 1.0)
+        ts(vv("wt", 2), ws(4, 6), float(W - K), A.is_ge, unit * W, mul)
+        tt(vv("wb", 2), vv("wb", 2), vv("wt", 2), sub)
+        act(d5(1, 2), s3)
+        tt(vv("p4"), g3, g4, plus)
+        tt(d5(1, 0), vv("p4"), gs, sub)
+        tt(vv("x0"), e0, vv("wa"), mul)
+        tt(vv("xb"), g2, vv("wb", 2, 1, 2), mul)
+        act(d5(3, 2), vv("x0"), bias=-1.0 * plain)
+        tt(d5(3, 1), vv("xb"), vv("x0"), sub)
+        act(d5(3, 0), vv("xb"), scale=-1.0)
+        tt(vv("x1"), e1, vv("wa"), mul)
+        tt(d5(2, 2), s4, vv("x1"), plus)
+        tt(d5(2, 1), e0, vv("x1"), sub)
+        act(vv("k5"), s4, bias=2.0 + plain)
+        tt(vv("k5"), vv("k5"), g3, mul)
+        tt(vv("sb"), vv("wb", 2, 0, 1), gs, mul)
+        tt(vv("sb"), vv("sb"), g2, plus)
+        tt(d5(2, 0), vv("sb"), vv("k5"), sub)
+
+    limit(1)
+    limit(2)
+    (look2 if wide else look)(*[1][wide:])
+    calls = [(x, t, k) for t, k, x in ORDER]
+    for t, k, x in ORDER:
+        if k == r:
+            calls.append((OPT["d1"][r - 2] if t == 1 else OPT["d2"][r] if t == 2 else x + 2 + OPT["dl"][r], t, None))
+    for x, t, k in sorted(calls, key=lambda c: c[0] if c[2] is None else c[0] + 0.8):
+        turn[:] = x, 0
+        if k is not None:
+            (opening if t == 2 and k in WIDE else bulk)(*[t, k][t == 2 and k in WIDE:])
+            continue
+        turn[1] = OPT["dec"]
+        (decide2 if t == 2 and wide else decide)(*[t][t == 2 and wide:])
+        turn[:] = 99, OPT["lk"]
         if t < NS - 1:
             look(t + 1)
+        turn[1] = OPT["bk"]
+        if t == NS - 1:
+            books()
+    turn[:] = 99, 0
 
+    def levels(k, h):
+        o = 192 * (k % 2) + 96 * h
+        a, b, d = at("fi", o, o + 96), at("ci2", o, o + 96), at("vo", o, o + 96)
+        cp(a, at("fin", 224 * k + 128 - 96 * h, 224 * k + 224 - 96 * h))
+        ts(b, a, 2, A.arith_shift_right)
+        ts(d, b, 12.0, A.mult, -1.0, A.add)
+        tt(view("stb", sl(3 * h, 3 * h + 3), sl(32 * k, 32 * k + 32)), d, a, A.add)
     for k in range(NR):
-        act(T.stb[:, 0:3, 32 * k:32 * k + 32], T.es[:, 96 * k:96 * k + 96], F.Copy,
-            ["eo0", "eo1", "eo2"] if k == r else ["es%d" % k], ["se%d" % k], 96)
-    dma("Y", T.stk[:, 0:384], T.stb[:, 0:3, :], "dk0", ["se%d" % j for j in range(NR)], (), 196608)
+        levels(k, 0)
+    dma("Y", hbm(T.stk[:, 0:384]), view("stb", sl(0, 3)), "dk0", 196608)
     for k in range(NR):
-        xs, st = T["xs%d" % k], T["st%d" % k]
-        rd = ["yu%d" % k] + ["x%d_%d_%d" % (k, s, h) for s in range(11) for h in range(2)]
-        cp(T.yu[:, 32 * k:32 * k + 32], T.fin[:, 128 * k:128 * k + 32], ["ls5_%d" % k], ["yu%d" % k])
-        act(st[:, 0:H], xs[:].indirect(T.yu[:, 32 * k:32 * k + 16]), F.Copy, rd, ["st%d_0" % k], H, GA)
-        cp(st[:, H:CH], xs[:].indirect(T.yu[:, 32 * k + 16:32 * k + 32]), rd, ["st%d_1" % k], H, GA)
-        dma("Y", T.y[:, CH * k:CH * k + CH], st[:], "dy%d" % k, ["st%d_0" % k, "st%d_1" % k], (), 2 ** 18)
-        cp(T.stb[:, 3:6, 32 * k:32 * k + 32], T.fin[:, 128 * k + 32:128 * k + 128], ["ls5_%d" % k], ["sl%d" % k], 96)
-    dma("S", T.stk[:, 384:768], T.stb[:, 3:6, :], "dk1", ["sl%d" % j for j in range(NR)], (), 196608)
-    return ops, ext, Q
+        xs = at("xs%d" % k)
+        act(picked(k, 0, H), gather(xs, at("fin", 224 * k, 224 * k + 16)))
+        cp(picked(k, H, CH), gather(xs, at("fin", 224 * k + 16, 224 * k + 32)))
+        turn[0] = 24 + k
+        due(0, 2)
+        turn[0] = 99
+        dma("Y", hbm(T.y[:, CH * k:CH * k + CH]), picked(k, 0, CH), "dy%d" % k, 2 ** 18)
+        if k >= OPT["mrg"]:
+            act(view("stb", sl(3, 6), sl(32 * k, 32 * k + 32)), ends(k)[2])
+        else:
+            levels(k, 1)
+    dma("S", hbm(T.stk[:, 384:768]), view("stb", sl(3, 6)), "dk1", 196608)
+    return ops, arrivals, Q
 
 
-def links(ops):
-    lastw, readers, out = {}, {}, []
+def links(ops, arrivals):
+    seen, out, far = {}, [], []
+    for a, sem, cnt in arrivals:
+        seen.setdefault(a[1][0][0], []).append([a[1][0][1], (sem, cnt), True])
     for n, op in enumerate(ops):
-        d = {lastw[k]: True for k in op["rd"] if k in lastw}
-        for k in op["wr"]:
-            for m in ([lastw[k]] if k in lastw else []) + readers.get(k, []):
-                d[m] = d.get(m, False) or ops[m]["q"] != op["q"]
+        d, f = {}, set()
+        for name, bits in op["rd"]:
+            for m, who, wrote in seen.get(name, []):
+                if wrote and m & bits:
+                    if isinstance(who, tuple):
+                        f.add(who)
+                    else:
+                        d[who] = True
+        for name, bits in op["wr"]:
+            for m, who, wrote in seen.get(name, []):
+                if m & bits:
+                    d[who] = d.get(who, False) or ops[who]["q"] != op["q"] or (name in _SB and op["q"] in "VS")
         if op["q"] == "P":
             d = {m: w and ops[m]["q"] != "P" for m, w in d.items()}
         out.append(d)
-        for k in op["rd"]:
-            readers.setdefault(k, []).append(n)
-        for k in op["wr"]:
-            lastw[k] = n
-            readers[k] = []
-    return out
+        far.append(f)
+        for name, bits in op["rd"]:
+            seen.setdefault(name, []).append([bits, n, False])
+        for name, bits in op["wr"]:
+            seen[name] = [[m & ~bits, who, wrote] for m, who, wrote in seen.get(name, []) if m & ~bits] + [[bits, n, True]]
+    return out, far
 
 
 def plan(recs):
-    ops, deps, sends = [], [], {}
-    for rops, _, _ in recs:
+    ops, deps, sends, waits = [], [], {}, []
+    for rops, arrivals, _ in recs:
         base = len(ops)
-        deps += [{m + base: w for m, w in d.items()} for d in links(rops)]
+        d, f = links(rops, arrivals)
+        deps += [{m + base: w for m, w in x.items()} for x in d]
+        waits += f
         ops += rops
     for n, op in enumerate(ops):
         for i, k in enumerate(op["to"][0] if op["to"] else []):
             sends.setdefault((k, op["to"][1]), []).append((n, i))
-    far = [[x for k in op["rd"] if k in recs[op["r"]][1] for x in sends[(op["r"], recs[op["r"]][1][k][0])]] for op in ops]
+    far = [[x for s, _ in f for x in sends[(op["r"], s)]] for op, f in zip(ops, waits)]
+    tau, behind = {}, {}
+    while len(tau) < len(ops):
+        for n in range(len(ops)):
+            pre = list(deps[n]) + [x for x, _ in far[n]]
+            if n not in tau and all(m in tau for m in pre):
+                tau[n] = max([ops[n]["tau"] or 0.0] + [tau[m] + 1e-5 for m in pre])
+    for n in sorted([n for n in range(len(ops)) if ops[n]["tau"] and ops[n]["q"] in OPT["order"]], key=lambda n: (tau[n], n)):
+        key = ops[n]["r"], ops[n]["q"]
+        if key in behind:
+            deps[n].setdefault(behind[key], False)
+        behind[key] = n
     succ, left = [[] for _ in ops], []
     for n in range(len(ops)):
         pre = set(deps[n]) | {m for m, _ in far[n]}
@@ -570,46 +747,83 @@ def plan(recs):
         op = ops[n]
         more = PLAN["sem"] if op["sem"] is None else PLAN["issue"] + PLAN["start"] + op["cost"] if op["to"] else PLAN["dma"]
         prio[n] = op["cost"] + more + max([prio[m] for m in succ[n]] + [0.0])
-    for n, op in enumerate(ops):
-        name = (op["wr"] + [op["to"][1] if op["to"] else op["sem"]])[0]
-        prio[n] += PRI.get(op["q"] + "".join(x for x in name if x.isalpha()), 0.0)
-    start, end, land, free, ready = {}, {}, {}, {}, {}
-    rings, first, out = [0.0] * NR, [PLAN["first"]] * NR, [[] for _ in recs]
+    turn = [op["turn"] for op in ops]
+    for n in reversed(order):
+        turn[n] = min([turn[n]] + [turn[m] for m in succ[n] if ops[m]["r"] == ops[n]["r"]])
+    prio = [(ops[n]["rush"] - turn[n], prio[n]) for n in range(len(ops))]
 
-    def release(n):
-        t = max([0.0] + [end[m] if w else start[m] for m, w in deps[n].items()] + [land[x] for x in far[n]])
-        ready.setdefault((ops[n]["r"], ops[n]["q"]), []).append((t, n))
-    for n in range(len(ops)):
-        if not left[n]:
-            release(n)
-    for _ in range(len(ops)):
-        t, key = min((max(free.get(key, 0.0), min(l)[0]), key) for key, l in ready.items() if l)
-        x = max([x for x in ready[key] if x[0] <= t + PLAN["slack"]], key=lambda x: (prio[x[1]], -x[1]))
-        ready[key].remove(x)
-        n, op = x[1], ops[x[1]]
-        t, r = max(t, x[0]), op["r"]
-        start[n] = t
-        if op["to"]:
-            free[key] = t + PLAN["issue"]
-            e = max(t + PLAN["issue"] + PLAN["start"] + first[r], rings[r])
-            first[r] = 0.0
-            for i in range(len(op["to"][0])):
-                e += op["cost"]
-                land[(n, i)] = e
-            rings[r] = end[n] = e
-        elif op["sem"]:
-            free[key] = t + 0.1
-            rings[r] = max(t + PLAN["dma"], rings[r]) + op["cost"]
-            end[n] = rings[r] + 0.3
-        else:
-            free[key] = t + op["cost"]
-            end[n] = t + op["cost"] + PLAN["sem"]
-        out[r].append(op)
-        for m in succ[n]:
-            left[m] -= 1
-            if not left[m]:
-                release(m)
-    return out
+    def once(due):
+        start, end, land, free, ready, became = {}, {}, {}, {}, {}, {}
+        rings, first, out, wait = [0.0] * NR, [PLAN["first"]] * NR, [[] for _ in recs], list(left)
+        coming = {}
+        for n in sorted(due, key=due.get):
+            coming.setdefault((ops[n]["r"], ops[n]["q"]), []).append(n)
+
+        urgent = {}
+        for n in sorted(range(len(ops)), key=tau.get):
+            if ops[n]["tau"]:
+                urgent.setdefault((ops[n]["r"], ops[n]["q"]), []).append(n)
+
+        def guess(n, depth):
+            if n in became:
+                return became[n]
+            if not depth or any(x not in land for x in far[n]):
+                return 1e9
+            return max([land[x] for x in far[n]] + [(end[m] if w else start[m]) if m in start else guess(m, depth - 1) + w * (ops[m]["cost"] + PLAN["sem"])
+                                                    for m, w in deps[n].items()])
+
+        def release(n):
+            became[n] = max([0.0] + [end[m] if w else start[m] for m, w in deps[n].items()] + [land[x] for x in far[n]])
+            ready.setdefault((ops[n]["r"], ops[n]["q"]), []).append((became[n], n))
+        for n in range(len(ops)):
+            if not wait[n]:
+                release(n)
+        while len(start) < len(ops):
+            t, key = min((max(free.get(key, 0.0), min(l)[0]), key) for key, l in ready.items() if l)
+            x = max([x for x in ready[key] if x[0] <= t], key=lambda x: (prio[x[1]], -x[1]))
+            n, op = x[1], ops[x[1]]
+            span = op["cost"] * len(op["to"][0] if op["to"] else [0]) + max(0.0, rings[key[0]] - t - PLAN["start"])
+            soon = [max(t, became.get(m, due[m])) for m in coming.get((key[0], "G"), []) if op["sem"] and turn[n] == 99
+                    and ops[m]["to"] and m not in start and turn[m] < 99 and became.get(m, due[m]) < t + PLAN["hold"] * span]
+            if soon:
+                ready[key].remove(x)
+                ready[key].append((min(soon) + 0.1, n))
+                continue
+            line = urgent[key] = [m for m in urgent.get(key, []) if m not in start]
+            soon = [e for e in [guess(m, 4) for m in line[:1] if prio[m][0] > prio[n][0]] if t < e < t + PLAN["keep"] * op["cost"]]
+            if soon and not op["sem"]:
+                free[key] = min(soon)
+                continue
+            ready[key].remove(x)
+            r = op["r"]
+            start[n] = t
+            if op["to"]:
+                free[key] = t + PLAN["issue"]
+                e = max(t + PLAN["issue"] + PLAN["start"] + first[r], rings[r])
+                first[r] = 0.0
+                for i in range(len(op["to"][0])):
+                    e += op["cost"]
+                    land[(n, i)] = e + PLAN["wake"]
+                rings[r] = end[n] = e
+            elif op["sem"]:
+                free[key] = t + 0.1
+                rings[r] = max(t + PLAN["dma"], rings[r]) + op["cost"]
+                end[n] = rings[r] + 0.3
+            else:
+                free[key] = t + op["cost"]
+                end[n] = t + op["cost"] + PLAN["sem"]
+            out[r].append(op)
+            for m in succ[n]:
+                wait[m] -= 1
+                if not wait[m]:
+                    release(m)
+        return max(end.values()), out, became
+
+    best = last = once({})
+    for _ in range(PLAN["passes"]):
+        last = once(last[2])
+        best = min(best, last, key=lambda x: x[0])
+    return best[1]
 
 
 def rank_program(g, core, T, topo):
@@ -617,11 +831,11 @@ def rank_program(g, core, T, topo):
     if r is None:
         return
     recs = [record(g, k, T, topo) for k in range(NR)]
-    ops, ext, Q = plan(recs)[r], recs[r][1], recs[r][2]
+    ops, Q = plan(recs)[r], recs[r][2]
     known, count, tok, waits, need = {q: {} for q in Q}, {}, [], [], set()
-    for n, (op, d) in enumerate(zip(ops, links(ops))):
+    for n, (op, d, f) in enumerate(zip(ops, *links(ops, recs[r][1]))):
         q, w = op["q"], {}
-        for t in [tok[m] for m in d if d[m]] + [ext[k] + ({}, None) for k in op["rd"] if k in ext]:
+        for t in [tok[m] for m in d if d[m]] + [x + ({}, None) for x in f]:
             if known[q].get(t[0], 0) < t[1] and w.get(t[0], (0, 0))[1] < t[1]:
                 w[t[0]] = t
         for t in w.values():

@@ -8,15 +8,15 @@ f32, bf16, i32, u16 = "float32", "bfloat16", "int32", "uint16"
 
 _SB = {"fr": ([8240], bf16), "ax": ([8240], bf16), "fi": ([512], i32), "hl": ([1024], bf16), "sti": ([128], i32),
        "stu": ([128], u16), "limi": ([8], i32), "limf": ([8], f32), "la": ([2, 8], f32), "lb": ([2, 8], f32),
-       "gx": ([2048], bf16), "gl": ([1024], bf16), "l0": ([512], u16), "ls": ([1024], u16), "lw": ([512], u16),
+       "gx": ([2048], bf16), "gl": ([512], bf16), "l0": ([768], u16), "ls": ([1024], u16), "lw": ([512], u16),
        "x64": ([128], f32), "r0": ([320], bf16), "r1": ([320], bf16), "r2": ([320], bf16), "pm": ([128], bf16),
        "pn": ([128], bf16), "lz": ([192], f32), "cb": ([320], bf16), "da": ([320], f32), "db": ([320], f32), "sa": ([320], f32),
        "sc": ([320], f32), "y0": ([160], bf16), "y1": ([160], f32), "fp": ([384], f32),
-       "sb": ([1536], f32), "rv": ([1536], f32), "fin": ([896], u16), "ci2": ([384], i32), "stb": ([6, 128], f32),
+       "sb": ([1536], f32), "rv": ([1536], f32), "fin": ([896], u16), "ci1": ([768], i32), "ci2": ([768], i32), "stb": ([6, 128], f32),
        "pi": ([8], i32), "ci": ([8], i32), "cf": ([24], f32), "x144": ([144], f32), "x32": ([64], f32),
        "x16": ([32], f32), "bo": ([8], f32), "m0": ([144], bf16), "m1": ([144], bf16), "idf": ([128], f32), "idb": ([128], bf16),
        "idn": ([128], bf16), "gq": ([64], f32), "rc": ([384], bf16), "de": ([64], bf16), "dn": ([64], bf16), "dd": ([64], bf16),
-       "one": ([64], bf16), "rk": ([32, 9, 3], bf16), "ra": ([32, 2], bf16), "rb": ([32, 2], bf16),
+       "one": ([64], bf16), "big": ([384], bf16), "rk": ([32, 9, 3], bf16), "ra": ([32, 2], bf16), "rb": ([32, 2], bf16),
        "lx": ([9, 8, 2, 8], bf16), "ll": ([5, 64, 2], f32), "jj": ([5, 64], bf16),
        "d1": ([384], f32), "d5": ([384], f32), "so": ([384], f32), "wv": ([160], f32), "s5": ([384], f32), "pb": ([160], f32),
        "sq": ([640], bf16), "rs": ([640], bf16), "ro": ([640], bf16), "h0": ([160], bf16), "h1": ([320], bf16),
@@ -33,15 +33,17 @@ SEMAPHORES = (["qV", "qS", "qP", "qG", "sent", "dfi", "dst", "dlim", "dfa", "dfb
               + ["dy%d" % k for k in range(NR)] + ["sh%d_%d" % (t, k) for t in range(1, 6) for k in range(NR)]
               + ["li%d_%d" % (t, k) for t in range(1, 6) for k in range(NR)] + ["ea%d" % k for k in range(NR)])
 
-PLAN = {"cyc": 0.9e-3, "gth": 1.2, "fix": 0.0, "pe": 0.45e-3, "sem": 0.3, "issue": 0.2, "start": 0.9, "rows": 0.5,
-        "wake": 0.4, "dma": 1.3, "bw": 350e3, "first": 2.0, "hold": 1.5, "passes": 0, "keep": 1.2}
-OPT = {"look": "VS", "WA": 5, "cut": 2, "dec": 4.0, "lk": 0.0, "bk": 1.0, "lcut": 2, "pcut": 0, "fin": 24.0,
-       "mrg": 3, "pre": 0.8, "ev": 0.4, "ew": 0.7, "dl": (0.55, 0.55, 0.55, 0.55), "order": "VSPG",
-       "ring": (2, 1, 3), "rev": -1, "xz": "SV", "lk2": "SS", "pra": 0.5, "half": ((0, 0), (2, 1)), "ea_": 0.3,
-       "d1": (5.0, 5.7), "d2": (10.3, 11.7, 12.6, 13.55), "txz": (3.95, 4.15), "tl2": (4.6, 5.0), "e3": 0.2, "e1": 0.12, "gap": 0.3,
-       "sw": 0.7, "g1": 0.16, "g2": 0.0, "ea": 23.5}
-WIDE = (0, 1)
-ORDER = [(1, 2, 2), (1, 3, 3), (2, 0, 4), (2, 1, 5), (2, 2, 10), (2, 3, 11)] + [(t, k, 4 * t + k) for t in (3, 4, 5) for k in range(NR)]
+PLAN = {"cyc": 0.9e-3, "gth": 1.2, "fix": 0.0, "pe": 0.45e-3, "sem": 0.35, "issue": 0.2, "start": 0.9, "rows": 0.5,
+        "wake": 0.4, "dma": 1.3, "bw": 420e3, "first": 2.0, "hold": 1.5, "passes": 0, "keep": 1.2, "late": 28.0}
+OPT = {"look": "SV", "WA": 5, "cut": 2, "dec": 4.0, "lk": 0.0, "bk": 0.5, "lcut": 2, "pcut": 0, "fin": 24,
+       "kind": "LLPP", "pre": 0.8, "ev": 0.2, "ew": 0.7, "dl": (0.4, 0.4, 0.4, 0.4), "order": "VSP",
+       "ring": (2, 1, 3), "rev": -1, "xz": "SVSS", "lk2": "SS", "pra": 1.1, "half": ((0, 0), (2, 1)), "ea_": 0.7,
+       "d1": (7.4, 8.4), "d2": (10.4, 11.4, 12.2, 13.4), "txz": (3.95, 4.3), "tl2": (6.0, 7.0), "e1": 0.7, "e3": 0.2, "gap": 0.3,
+       "lag": 0.0, "tw": 2.7, "tl1": 3.9, "g1": (0.32,) * 5, "g2": 0.14, "rd": 0.9, "h0": (0, 0, 0, 0), "el": 0.35, "th": 0.2, "t1": 0.6, "t2": 0.2, "lt": 0, "tv": (26.2, 26.2, 26.3, 26.6), "yw": 1, "a4": 1, "tk0": 2, "tk": (3.9, 5.05, 5.5, 5.9, 6.05), "tll": 4.7, "eo": 0.7, "tc": (26.6, 27.05), "t0": 0.0, "free": (), "fev": (), "lw": (2, 2), "gp2": 0.0, "dir": 0, "ea": 21.5}
+WIDE = [0, 1]
+TURNS = ([(1, 2), (1, 3), (0, 0), (0, 1), (-1, 0), (-2, 0), (-1, 1), (-2, 1), (2, 2), (2, 3)]
+         + [(t, k) for t in (3, 4, 5) for k in range(NR)])
+ORDER = [(1, 2), (1, 3)] + [(2, k) for k in range(NR)] + TURNS[-12:]
 _cols = {}
 
 
@@ -132,6 +134,7 @@ def record(g, r, T, topo):
         add("G", lambda: g.iota(o[0], pat, base, cm, allow_small_or_imprecise_dtypes=True), (), [o], 0.13 + 2 * o[2] * cyc)
 
     hbm = lambda x: (x, [], 0, False)
+    lineb = (None, [("lineb", 1)], 0, False)
     line = (None, [("line", 1)], 0, False)
 
     def dma(q, o, a, sem, size, more=()):
@@ -168,9 +171,11 @@ def record(g, r, T, topo):
         return at("sb", o, o + n)
 
     def ends(k):
-        o = 224 * k + (128 if k >= OPT["mrg"] else 32)
-        return at("fin", 224 * k, 224 * k + 32), at("fin", o, 224 * k + 224), at("fp", 96 * k, 96 * k + 96)
-    for t, k, _ in ORDER:
+        if OPT["kind"][k] != "P":
+            o = 224 * k + (32 if OPT["kind"][k] == "L" else 128)
+            return at("fin", 224 * k, o), at("fin", o, 224 * k + 224)
+        return at("fin", 224 * k, 224 * k + 32), at("fp", 192 * k - 384, 192 * k - 288), at("fp", 192 * k - 288, 192 * k - 192)
+    for t, k in ORDER:
         o = ((t - 1) * 4 + k) * 64
         if k == r:
             arrivals += [(landed(t, j, r), "sh%d_%d" % (t, j), nin(j, [r])) for j in others]
@@ -178,7 +183,7 @@ def record(g, r, T, topo):
             arrivals.append((at("ls", o, o + 64) if t < NS else ends(k)[0], "li%d_%d" % (t, k), nin(k, rest(k))))
     for k in others:
         arrivals.append((ends(k)[1], "fi%d" % k, nin(k, rest(k))))
-        arrivals += [(ends(k)[2], "ea%d" % k, nin(k, rest(k)))] * (k >= OPT["mrg"])
+        arrivals += [(x, "ea%d" % k, nin(k, rest(k))) for x in ends(k)[2:]]
 
     WA = OPT["WA"] * W // 8
     dma("Y", at("fi"), hbm(T.first[:]), "dfi", 2 ** 18, [line])
@@ -224,10 +229,13 @@ def record(g, r, T, topo):
     ts(at("m0"), at("x144"), c(9), A.is_equal, c(10), A.mult)
     ts(at("m1"), at("x144"), c(9), A.is_equal, c(11), A.mult)
     ts(at("bo"), at("x144", 0, 8), cg, A.is_equal)
-    ts(at("idf"), at("x144", 0, 128), c(8), A.is_equal)
-    act(at("idb"), at("idf"))
-    act(at("idn"), at("idf"), scale=-1.0)
-    ts(at("gq"), at("x144", 0, 64), c(14), A.is_equal)
+    ts(at("idf"), at("x144", 0, 128), c(8), A.is_equal, -1.0, A.mult)
+    act(at("idb"), at("idf"), scale=-1.0)
+    act(at("idn"), at("idf"))
+    ts(at("gq"), at("x144", 0, 64), c(14), A.is_equal, -1.0, A.mult)
+    mset(at("big"), 2.0 ** 26)
+    for h in range(2):
+        ts(at("big", 192 * h, 192 * h + 192), at("big", 192 * h, 192 * h + 192), mk[1 - h], A.mult)
     ts(at("rc"), at("s5"), c(15), A.is_equal)
     ts(at("de"), at("x32"), cj, A.is_equal)
     de = at("de", 0, 32)
@@ -295,8 +303,7 @@ def record(g, r, T, topo):
     mset(nth("f0", 5, 0, 0, 5), 0.0)
     mset(nth("f1", 5, 2, 0, 1), 0.0)
     mset(nth("f1", 5, 3, 4, 5), 0.0)
-    mset(nth("f1", 5, 4, 0, 3), 0.0)
-    mset(nth("f1", 5, 4, 3, 5), -1.0 * (r >= OPT["mrg"]))
+    mset(nth("f1", 5, 4, 0, 5), -1.0 * (OPT["kind"][r] == "P"))
 
     axw = at("ax", AO, AO + W)
     frw = at("fr", 0, W + K)
@@ -304,26 +311,31 @@ def record(g, r, T, topo):
     def extract(o, src, n0, n, m):
         mm(o, [(at(m, 15 - i, 143 - i), at(src, n0 + i, n0 + n, 16)) for i in range(16)])
 
-    for k in (2, 3, 0, 1):
+    for k in [(TURNS[0][1] + i) % NR for i in range(NR)]:
         move("SV"[k % 2], at("gx", CH * k, CH * k + CH), gather(axw, at("stu", 32 * k, 32 * k + 32)))
+        ops[-1]["tau"] = 1.0
         if k % 2:
             extract(at("pa", 0, 64), "gx", CH * (k - 1), 2 * CH, "m0")
             cp(at("l0", 32 * k - 32, 32 * k + 32), at("pa", 0, 64))
             ts(at("l0", 96 + 32 * k, 160 + 32 * k), at("pa", 0, 64), float(K), A.add)
+            for op in ops[-2:]:
+                op["tau"] = 2.0 if k == 3 else 9 + OPT["tw"]
     for h in range(2):
         dma("Y", view("ax", sl(AO - K, AO - K + W), part=sl(2 + h, None, 16)), at("hl", 512 * h, 512 * h + 512), "day", 2 ** 17, [line, at("ax")])
         dma("Y", view("ax", sl(AO - K + W, AO + W), part=sl(2 + h, None, 16)),
             view("hl", sl(512 * h, 512 * h + K), part=sl(0, None, 16)), "day", 2 ** 10, [line, at("ax")])
     for k in WIDE:
         move(OPT["xz"][k], at("gx", CH * k, CH * k + CH), gather(axw, at("l0", 32 * k, 32 * k + 32)))
-        ops[-1]["tau"] = OPT["txz"][k]
-    extract(at("px", 0, 64), "gx", 0, 2 * CH, "m0")
-    extract(at("px", 64, 128), "gx", 0, 2 * CH, "m1")
-    cp(at("l0", 256, 384), at("px", 0, 128))
-    ts(at("l0", 384, 512), at("px", 0, 128), float(K), A.add)
+        ops[-1]["tau"] = 9 + OPT["txz"][k]
+        if k % 2:
+            o = 128 + 128 * k
+            extract(at("px", 0, 64), "gx", CH * (k - 1), 2 * CH, "m0")
+            extract(at("px", 64, 128), "gx", CH * (k - 1), 2 * CH, "m1")
+            cp(at("l0", o, o + 128), at("px", 0, 128))
+            ts(at("l0", o + 128, o + 256), at("px", 0, 128), float(K), A.add)
 
     def first(p, e, k, a=0, b=32):
-        o = 128 * e + 32 * k if p == 0 else 256 + 128 * e + 64 * (p - 1) + 32 * k
+        o = 128 * e + 32 * k if p == 0 else 256 + 256 * (k // 2) + 128 * e + 64 * (p - 1) + 32 * (k % 2)
         return at("l0", o + a, o + b)
 
     place = {}
@@ -346,7 +358,7 @@ def record(g, r, T, topo):
 
     def due(x, n=1):
         for op in ops[-n:]:
-            op["tau"] = turn[0] + x
+            op["tau"] = 9 + turn[0] + x
 
     picked = lambda k, a, b: at("ab%d" % (k % 2), (2 + k // 2) * CH + a, (2 + k // 2) * CH + b)
 
@@ -361,7 +373,7 @@ def record(g, r, T, topo):
                 act(top(h), gather(frw, at("stu", 32 * k + lw * h, 32 * k + lw * h + lw)))
             else:
                 act(top(h), gather(at(xs, x0 - (5 if k in WIDE and t < NS else 3) * CH, x0), wl(t, k, 32 + lw * h, 32 + lw * h + lw)))
-            due(0.16 * h - (OPT["pre"] if (k == r or t == 1) and (t, k) != (2, 2) else 0.0))
+            due(0.16 * h - (OPT["pre"] if (k == r or t == 1) and (t, k) != (2, 2) else OPT["h0"][(k - r) % NR] * (h == 0 and t > 2)))
         if t > 1:
             ts(at("lw", o1, o1 + 32), wl(t, k, 0, 32), float(K), A.add)
             due(0.01)
@@ -378,41 +390,46 @@ def record(g, r, T, topo):
         for a, b in ([(0, 96), (96, 128)] if OPT["pcut"] else [(0, 128)]):
             for q in range(8):
                 mm(view(pe, sl(q, 64, 8), part=sl(a, b)), [(at(ab, 8 * a + q, 8 * b, 8), at("bo"))])
-                due(0.9 if b == 128 else 0.75)
-        hand(t, k, 64, 1 + OPT["e1" if (t, k) == (1, 3) else "ew" if k == r or (k + 1) % NR == r or t == 1 else "ev"])
+                due(OPT["rd"] if b == 128 else 0.75)
+        hand(t, k, 64, 1 + (OPT["el"] if k == (r + 2) % NR and t > 2 else
+                            OPT["e1" if (t, k) == (1, 3) else "eo" if k == r or t < 3 and (t == 1 or (k + 1) % NR == r) else "ew" if (k + 1) % NR == r else "ev"]))
 
     def hand(t, k, n, when):
-        act(leaving(t, k) if k != r else landed(t, r, r), at("pe%d" % (k % 2), 0, n))
+        o = 64 + 192 * (k // 2) if n > 64 else 0
+        act(leaving(t, k) if k != r else landed(t, r, r), at("pe%d" % (k % 2), o, o + n))
         due(when)
+        if (t, k) in OPT["fev"]:
+            ops[-1].update(tau=None, rush=4)
         if k != r:
             send(landed(t, r, k), leaving(t, k), [k], "sh%d_%d" % (t, r), 0.5 * (n > 64))
             due(when + 0.01)
 
-    def opening(k):
-        xs, ab, pe = "xs%d" % k, "ab%d" % (k % 2), "pe%d" % (k % 2)
-        for h in range(2):
+    def opening(p, k):
+        xs, ab, pe, o = "xs%d" % k, "ab%d" % (turn[0] % 2), "pe%d" % (k % 2), 64 + 192 * (k // 2) + 64 * p
+        a0 = 2 * CH * ((turn[0] // 2 + OPT["a4"]) % 2) * (OPT["a4"] < 2)
+        for h in range(2 * (p == 0)):
             act(at(xs, h * H, h * H + H), gather(frw, at("stu", 32 * k + 16 * h, 32 * k + 16 * h + 16)))
-            due(0.08 * h - OPT["pra"] - OPT["sw"] * k)
-        for p in range(3):
-            lead = OPT["sw"] * (-k if p == 0 else (1 - k) * 0.4)
-            for e in range(2):
-                n = 2 if (p, e) in OPT["half"] else 1
-                for h in range(n):
-                    a, b, a0 = CH // n * h, CH // n * (h + 1), 2 * CH * (p % 2) + CH * e
-                    x = at(xs, (2 * p + e + 1) * CH + a, (2 * p + e + 1) * CH + b)
-                    tt(x, gather(frw, first(p, e, k, a // 16, b // 16)), at(xs, p * CH + a, p * CH + b), A.add)
-                    due(lead + 0.1 + 0.15 * (2 * p + e) + 0.07 * h)
-                    act(at(ab, a0 + a, a0 + b), x, F.Abs)
-                    due(lead + 0.2 + 0.15 * (2 * p + e) + 0.07 * h)
-            for q in range(8):
-                mm(at(pe, 64 * p + q, 64 * p + 64, 8), [(at(ab, 2 * CH * (p % 2) + q, 2 * CH * (p % 2 + 1), 8), at("bo"))])
-                due(lead + 0.45 + 0.3 * p)
-        hand(2, k, 192, lead + 1 + OPT["ea_"] if k < 1 else 5 + OPT["e3"])
+            due(0.16 * h - OPT["pra"])
+        for e in range(2):
+            n = 2 if (p, e) in OPT["half"] else 1
+            for h in range(n):
+                a, b = CH // n * h, CH // n * (h + 1)
+                x = at(xs, (2 * p + e + 1) * CH + a, (2 * p + e + 1) * CH + b)
+                tt(x, gather(frw, first(p, e, k, a // 16, b // 16)), at(xs, p * CH + a, p * CH + b), A.add)
+                due(0.18 + 0.32 * e + 0.16 * h)
+                act(at(ab, a0 + CH * e + a, a0 + CH * e + b), x, F.Abs)
+                due(0.34 + 0.32 * e + 0.16 * (h + 2 - n) + OPT["lag"])
+        for q in range(8):
+            mm(at(pe, o + q, o + 64, 8), [(at(ab, a0 + q, a0 + 2 * CH, 8), at("bo"))])
+            due(0.9 + OPT["lag"])
+        if p == 2:
+            hand(2, k, 192, 1 + OPT["ea_" if k < WIDE[-1] else "e3"])
 
     def look(t):
         n = OPT["lcut"]
         for h in range(n):
             move(OPT["look"][h % len(OPT["look"])], at("gl", CH // n * h, CH // n * (h + 1)), gather(axw, wl(t, r, 32 // n * h, 32 // n * (h + 1))))
+            ops[-1]["tau"] = 9 + OPT["tl1"] if t == 1 else 5 + 4 * t + r + OPT["tk"][h] if t >= OPT["tk0"] else None
         extract(at("pa", 0, 32), "gl", 0, CH, "m0")
         extract(at("pa", 32, 64), "gl", 0, CH, "m1")
         act(tri(t, 2, 96, 3), at("pa", 0, 32))
@@ -420,13 +437,17 @@ def record(g, r, T, topo):
         if t > 1:
             tt(tri(t, 0, 96, 3), nth("sc", 5, 4, 0, 1) if t == 3 and wide else at("pb", 32 * (t - 1), 32 * t), at("pb", 32 * t, 32 * t + 32), A.subtract)
         tt(tri(t, 1, 96, 3), at("pb", 32 * t, 32 * t + 32), tri(t, 2, 96, 3), A.subtract)
+        for i, op in enumerate(ops[-36:] if t >= OPT["tk0"] else []):
+            op["tau"] = 5 + 4 * t + r + OPT["tk"][2 if i < 32 else 3 if i < 34 else 4]
+        for i, op in enumerate(ops[-35:] if t == 1 else []):
+            op["tau"] = 9 + OPT["tl1"] + (0.3 if i < 32 else 0.9 if i < 34 else 1.3)
 
     def look2():
         for p in (1, 2):
-            move(OPT["lk2"][p - 1], at("gl", CH * p - CH, CH * p), gather(axw, first(p, 0, r)))
-            ops[-1]["tau"] = OPT["tl2"][r] + 0.3 * p
-        extract(at("pa", 0, 64), "gl", 0, 2 * CH, "m0")
-        extract(at("pa", 64, 128), "gl", 0, 2 * CH, "m1")
+            move(OPT["lk2"][p - 1], at("gx", CH * p - CH, CH * p), gather(axw, first(p, 0, r)))
+            ops[-1]["tau"] = 9 + OPT["tl2"][r] + 0.5 * p
+        extract(at("pa", 0, 64), "gx", 0, 2 * CH, "m0")
+        extract(at("pa", 64, 128), "gx", 0, 2 * CH, "m1")
         a1, a2, b1, b2 = [at("pa", 32 * i, 32 * i + 32) for i in range(4)]
         da, db = (lambda i: nth("da", 5, i, 0, 1)), (lambda l, i: nth("db", 5, i, l, l + 1))
         cp(db(1, 4), first(1, 0, r))
@@ -444,12 +465,14 @@ def record(g, r, T, topo):
     def decide2():
         for p in range(3):
             mm(at("pz", 64 * p, 64 * p + 64), [(view("ll", min(p, 1)), at("gq"))])
-        act(at("lz"), at("pz", 0, 192))
-        mm(at("pq", 0, 192), [(at("idf"), at("lz"))] + [(at("idf"), landed(2, k, r)) for k in [r] + ring[::OPT["rev"]]])
-        d = 0
-        due(d, 3)
+        act(at("lz"), at("pz", 0, 192), scale=-1.0)
+        d, late = 0, OPT["lw"][r]
         for h in range(2):
-            ts(view("lx", sl(1, 4), sl(None), h), at("pq", 0, 192), 0.0, A.is_gt, mk[h], A.mult)
+            mm(at(("pq", "pc")[h], 0, 192), [(at("idf"), at("lz")), (at("idb"), at("big", 192 * h, 192 * h + 192))]
+               + [(at("idf"), landed(2, k, r)) for k in [r] + [j for j in others if j != late]])
+            due(-OPT["t2"], 2)
+        for h in range(2):
+            tt(view("lx", sl(1, 4), sl(None), h), landed(2, late, r), at(("pq", "pc")[h], 0, 192), A.is_gt)
         mm(at("pc", 0, 320), [(view("lx", 1 + p), at("r%d" % p)) for p in range(3)])
         ts(at("cb"), at("pc", 0, 320), 1.0, A.min)
         scan(at("sa"), at("cb"), at("da"))
@@ -457,6 +480,7 @@ def record(g, r, T, topo):
         send(wl(3, r, 0, 64), wl(3, r, 0, 64), ring, "li2_%d" % r)
         due(d, 9)
         due(d + OPT["gap"], 4)
+        due(d + OPT["gap"] + OPT["gp2"], 3)
         turn[:] = 99, 0
         scan(at("sc"), at("cb"), at("db"))
         act(at("wv", 32, 64), nth("sc", 5, 4, 1, 2))
@@ -474,12 +498,17 @@ def record(g, r, T, topo):
         mm(at("pz", 0, 64), [(at("idn"), at("one"))] + [(x, at("de")) for x in bits(t)])
         tt(view("jj", t), at("pz", 0, 64), view("jj", t - 1), A.max)
         limit(t + 1)
+        for op in ops[-2:] if OPT["tll"] else []:
+            op["tau"] = 9 + 4 * t + r + OPT["tll"]
 
     def decide(t):
-        mm(at("pq", 0, 64), [(view("ll", t - 1), at("gq"))] + [(at("idf"), landed(t, k, r)) for k in [r] + ring[::OPT["rev"]]])
-        due(0, 3)
+        late = ring[OPT["lt"]]
         for h in range(2):
-            ts(view("lx", t + 3 * (t > 2), sl(None), h), at("pq", 0, 64), 0.0, A.is_gt, mk[h], A.mult)
+            mm(at(("pq", "pc")[h], 0, 64), [(view("ll", t - 1), at("gq")), (at("idb"), at("big", 192 * h, 192 * h + 64))]
+               + [(at("idf"), landed(t, k, r)) for k in [r] + [j for j in ring[::OPT["rev"]] if j != late]])
+            due(-OPT["th" if t > 1 else "t1"], 2)
+        for h in range(2):
+            tt(view("lx", t + 3 * (t > 2), sl(None), h), landed(t, late, r), at(("pq", "pc")[h], 0, 64), A.is_gt)
         n = 192 if t < NS else 384
         mm(at("pc", 0, n), [(bits(t)[0], at("rc", 0, n))])
         if t < NS:
@@ -487,20 +516,25 @@ def record(g, r, T, topo):
             cp(wl(t + 1, r, 0, 64), out(t, 2, 192, 3))
             send(wl(t + 1, r, 0, 64), wl(t + 1, r, 0, 64), ring, "li%d_%d" % (t, r))
             due(0, 6)
-            due(OPT["g1"], 3)
-            due(OPT["g2"], 2)
+            due(OPT["g1"][r if t > 2 else 4], 3)
+            due(OPT["g1"][r if t > 2 else 4] + OPT["g2"], 2)
         else:
             m = 3 * ends(r)[0][2]
             scan(at("s5", 0, m), at("pc", 0, m), at("d5", 0, m))
             cp(ends(r)[0], at("s5", 2, m, 3))
             send(ends(r)[0], ends(r)[0], ring, "li5_%d" % r, m / 1500 - 0.15)
             due(0, 6)
-            due(OPT["g1"], 3)
-            due(OPT["g2"], 2)
+            due(OPT["g1"][r], 3)
+            due(OPT["g1"][r] + OPT["g2"], 2)
             turn[:] = OPT["fin"], 0
-            scan(at("s5", m, 384), at("pc", m, 384), at("d5", m, 384))
-            if r >= OPT["mrg"]:
-                act(ends(r)[2], at("s5", m + 2, 384, 3))
+            if m < 384:
+                scan(at("s5", m, 384), at("pc", m, 384), at("d5", m, 384))
+            if m == 384:
+                pass
+            elif OPT["kind"][r] == "P":
+                cp(ends(r)[2], at("s5", m + 2, 384, 3))
+                for op in ops[-2:]:
+                    op["tau"] = 9 + 22 + r + OPT["dl"][r] + OPT["g1"][r] + (0.01 if op is ops[-2] else OPT["g2"] + 0.01)
                 send(ends(r)[2], ends(r)[2], ring, "ea%d" % r, 0.3)
             else:
                 cp(at("fin", 224 * r + 32, 224 * r + 128), at("s5", m + 2, 384, 3))
@@ -586,7 +620,7 @@ def record(g, r, T, topo):
         tt(nth("f0", 5, 1, 0, 5), at("pz", 0, 160), at("lvl"), A.is_equal)
         tt(nth("f0", 5, 4, 0, 5), at("pz", 0, 160), at("lvl"), A.is_le)
         act(nth("f1", 5, 0, 0, 5), at("pz", 160, 320), bias=2.0)
-        plain = r >= OPT["mrg"]
+        plain = OPT["kind"][r] == "P"
         unit = 16.0 if plain else 4.0
         act(nth("f1", 5, 3, 0, 4), cl)
         act(nth("v1", 3, 2, 0, 4), cl, scale=float(K))
@@ -595,15 +629,14 @@ def record(g, r, T, topo):
         act(nth("v1", 3, 1, 0, 4), ws(1, 5))
         tt(nth("v1", 3, 0, 1, 3), ws(3, 5), ws(2, 4), sub)
         scan(at("vo"), at("v0"), at("v1"))
-        for a, b, x in [(1, 3, 4.0), (3, 5, unit)] if plain else [(1, 5, 4.0)]:
-            ts(nth("f1", 5, 2, a, b), nth("vo", 3, 2, a - 1, b - 1), float(W), A.is_ge, -x * W, mul)
-            act(nth("f1", 5, 1, a, b), nth("vo", 3, 2, a - 1, b - 1), scale=x, bias=1.0)
-        ts(nth("f1", 5, 1, 0, 1), at("sti", 32 * r, 32 * r + 32), 4.0, mul, 1.0, plus)
+        ts(nth("f1", 5, 2, 1, 5), nth("vo", 3, 2, 0, 4), float(W), A.is_ge, -unit * W, mul)
+        act(nth("f1", 5, 1, 1, 5), nth("vo", 3, 2, 0, 4), scale=unit, bias=1.0)
+        ts(nth("f1", 5, 1, 0, 1), at("sti", 32 * r, 32 * r + 32), unit, mul, 1.0, plus)
         scan(at("fo"), at("f0"), at("f1"))
-        cp(at("fin", 224 * r + 128, 224 * r + 224), nth("fo", 5, 4, 0, 3))
-        if plain:
+        cp(ends(r)[1] if plain else at("fin", 224 * r + 128, 224 * r + 224), nth("fo", 5, 4, 0, 3))
+        if OPT["kind"][r] != "L":
             turn[0] = OPT["ea"]
-            send(ends(r)[1], ends(r)[1], ring, "fi%d" % r, 0.05)
+            send(ends(r)[1], ends(r)[1], ring, "fi%d" % r, 0.3 * plain)
             turn[0] = 99
         s3, s4 = nth("fo", 5, 4, 3, 4), nth("fo", 5, 4, 4, 5)
         e0, e1 = vv("e0"), d5(1, 1)
@@ -633,17 +666,20 @@ def record(g, r, T, topo):
     limit(1)
     limit(2)
     (look2 if wide else look)(*[1][wide:])
-    calls = [(x, t, k) for t, k, x in ORDER]
-    for t, k, x in ORDER:
+    calls = [(24 - len(TURNS) + i, t, k) for i, (t, k) in enumerate(TURNS)]
+    for t, k in ORDER:
         if k == r:
-            calls.append((OPT["d1"][r - 2] if t == 1 else OPT["d2"][r] if t == 2 else x + 2 + OPT["dl"][r], t, None))
+            calls.append((OPT["d1"][r - 2] if t == 1 else OPT["d2"][r] if t == 2 else 4 * t + k + 2 + OPT["dl"][r], t, None))
     for x, t, k in sorted(calls, key=lambda c: c[0] if c[2] is None else c[0] + 0.8):
         turn[:] = x, 0
         if k is not None:
-            (opening if t == 2 and k in WIDE else bulk)(*[t, k][t == 2 and k in WIDE:])
+            (opening if t < 1 else bulk)(abs(t), k)
             continue
         turn[1] = OPT["dec"]
+        n0 = len(ops)
         (decide2 if t == 2 and wide else decide)(*[t][t == 2 and wide:])
+        for op in ops[n0:] if (t, r) in OPT["free"] else []:
+            op["tau"] = None
         turn[:] = 99, OPT["lk"]
         if t < NS - 1:
             look(t + 1)
@@ -653,27 +689,36 @@ def record(g, r, T, topo):
     turn[:] = 99, 0
 
     def levels(k, h):
-        o = 192 * (k % 2) + 96 * h
-        a, b, d = at("fi", o, o + 96), at("ci2", o, o + 96), at("vo", o, o + 96)
+        o = 192 * k + 96 * h
+        a, b, d = at("ci1", o, o + 96), at("ci2", o, o + 96), at("f1", o, o + 96)
         cp(a, at("fin", 224 * k + 128 - 96 * h, 224 * k + 224 - 96 * h))
         ts(b, a, 2, A.arith_shift_right)
         ts(d, b, 12.0, A.mult, -1.0, A.add)
         tt(view("stb", sl(3 * h, 3 * h + 3), sl(32 * k, 32 * k + 32)), d, a, A.add)
+        for i, op in enumerate(ops[-4:]):
+            x = OPT["tc"][k - 2] - OPT["t0"] * (i == 0) if OPT["kind"][k] == "C" and h else OPT["tv"][k]
+            op["tau"] = 9 + max(x, 22.95 + r) + 0.01 * i + 0.001 * (2 * k + h)
     for k in range(NR):
-        levels(k, 0)
-    dma("Y", hbm(T.stk[:, 0:384]), view("stb", sl(0, 3)), "dk0", 196608)
+        if OPT["kind"][k] != "P":
+            levels(k, 0)
+        else:
+            act(view("stb", sl(0, 3), sl(32 * k, 32 * k + 32)), ends(k)[1])
+            ops[-1]["tau"] = 9 + max(OPT["tv"][k], 22.95 + r)
+    dma("Y", hbm(T.stk[:, 0:384]), view("stb", sl(0, 3)), "dk0", 196608, [line])
     for k in range(NR):
-        xs = at("xs%d" % k)
+        xs = at("xs%d" % k, 0, (13 if k in WIDE else 11) * CH)
         act(picked(k, 0, H), gather(xs, at("fin", 224 * k, 224 * k + 16)))
         cp(picked(k, H, CH), gather(xs, at("fin", 224 * k + 16, 224 * k + 32)))
         turn[0] = 24 + k
         due(0, 2)
         turn[0] = 99
         dma("Y", hbm(T.y[:, CH * k:CH * k + CH]), picked(k, 0, CH), "dy%d" % k, 2 ** 18)
-        if k >= OPT["mrg"]:
-            act(view("stb", sl(3, 6), sl(32 * k, 32 * k + 32)), ends(k)[2])
-        else:
+        if OPT["kind"][r] != "L" and k >= r - OPT["yw"]:
+            ops[-1]["rd"] += ends(r)[2 * (OPT["kind"][r] == "P")][1]
+        if OPT["kind"][k] != "P":
             levels(k, 1)
+        else:
+            act(view("stb", sl(3, 6), sl(32 * k, 32 * k + 32)), ends(k)[2])
     dma("S", hbm(T.stk[:, 384:768]), view("stb", sl(3, 6)), "dk1", 196608)
     return ops, arrivals, Q
 
@@ -773,7 +818,7 @@ def plan(recs):
                                                     for m, w in deps[n].items()])
 
         def release(n):
-            became[n] = max([0.0] + [end[m] if w else start[m] for m, w in deps[n].items()] + [land[x] for x in far[n]])
+            became[n] = max([PLAN["late"] * (turn[n] >= 18)] + [end[m] if w else start[m] for m, w in deps[n].items()] + [land[x] for x in far[n]])
             ready.setdefault((ops[n]["r"], ops[n]["q"]), []).append((became[n], n))
         for n in range(len(ops)):
             if not wait[n]:

import numpy as np
from concourse.bass import DstId, RemoteDMATransfer
from concourse.mybir import AluOpType as A, ActivationFunctionType as F

NR, CH, W, K, NS = 4, 512, 8192, 37, 5
AO = 48
f32, bf16, i32, u16 = "float32", "bfloat16", "int32", "uint16"

_SB = {"fr": ([8240], bf16), "ax": ([8240], bf16), "fi": ([512], i32), "hl": ([1024], bf16), "sti": ([128], i32),
       "stu": ([128], u16), "limi": ([8], i32), "limf": ([8], f32), "la": ([2, 8], f32), "lb": ([2, 8], f32),
       "gx": ([2048], bf16), "gl": ([512], bf16), "l0": ([768], u16), "ls": ([1024], u16), "lw": ([512], u16),
       "x64": ([128], f32), "r0": ([320], bf16), "r1": ([320], bf16), "r2": ([320], bf16), "pm": ([128], bf16),
       "pn": ([128], bf16), "lz": ([192], f32), "cb": ([320], bf16), "da": ([320], f32), "db": ([320], f32), "sa": ([320], f32),
       "sc": ([320], f32), "y0": ([160], bf16), "y1": ([160], f32), "fp": ([384], f32),
       "sb": ([1536], f32), "rv": ([1536], f32), "fin": ([896], u16), "ci1": ([768], i32), "ci2": ([768], i32), "stb": ([6, 128], f32),
       "pi": ([8], i32), "ci": ([8], i32), "cf": ([24], f32), "x144": ([144], f32), "x32": ([64], f32),
       "x16": ([32], f32), "bo": ([8], f32), "m0": ([144], bf16), "m1": ([144], bf16), "idf": ([128], f32), "idb": ([128], bf16),
       "idn": ([128], bf16), "gq": ([64], f32), "rc": ([384], bf16), "de": ([64], bf16), "dn": ([64], bf16), "dd": ([64], bf16),
       "one": ([64], bf16), "big": ([384], bf16), "rk": ([32, 9, 3], bf16), "ra": ([32, 2], bf16), "rb": ([32, 2], bf16),
       "lx": ([9, 8, 2, 8], bf16), "ll": ([5, 64, 2], f32), "jj": ([5, 64], bf16),
       "d1": ([384], f32), "d5": ([384], f32), "so": ([384], f32), "wv": ([160], f32), "s5": ([384], f32), "pb": ([160], f32),
       "sq": ([640], bf16), "rs": ([640], bf16), "ro": ([640], bf16), "h0": ([160], bf16), "h1": ([320], bf16),
       "ho": ([320], bf16), "xg": ([128], bf16), "c0": ([256], bf16), "co": ([256], bf16), "v0": ([384], bf16),
       "v1": ([384], f32), "vo": ([384], f32), "f0": ([800], bf16), "f1": ([800], f32), "fo": ([800], f32),
       "lvl": ([160], f32), "slc": ([128], bf16), "u": ([512], bf16), "v": ([1120], f32)}
for _k in range(NR):
    _SB.update({"xs%d" % _k: ([(13 if _k < 2 else 11) * CH], f32), "ab%d" % (_k % 2): ([4 * CH], f32)})
SCRATCH = {k: ("sbuf", [128] + n, d) for k, (n, d) in _SB.items()}
BANKS = ["pe0", "pe1", "pq", "pc", "pa", "px", "py", "pz"]
SCRATCH.update({k: ("psum", [128, 512], f32) for k in BANKS})

SEMAPHORES = (["qV", "qS", "qP", "qG", "sent", "dfi", "dst", "dlim", "dfa", "dfb", "dax", "day", "dk0", "dk1"] + ["fi%d" % k for k in range(NR)]
              + ["dy%d" % k for k in range(NR)] + ["sh%d_%d" % (t, k) for t in range(1, 6) for k in range(NR)]
              + ["li%d_%d" % (t, k) for t in range(1, 6) for k in range(NR)] + ["ea%d" % k for k in range(NR)])

PLAN = {"cyc": 0.9e-3, "gth": 1.2, "fix": 0.0, "pe": 0.45e-3, "sem": 0.35, "issue": 0.2, "start": 0.9, "rows": 0.5,
        "wake": 0.4, "dma": 1.3, "bw": 420e3, "first": 2.0, "hold": 1.5, "passes": 0, "keep": 1.2, "late": 28.0}
OPT = {"look": "SV", "WA": 5, "cut": 2, "dec": 4.0, "lk": 0.0, "bk": 0.5, "lcut": 2, "pcut": 0, "fin": 24,
       "kind": "LLPP", "pre": 0.8, "ev": 0.2, "ew": 0.7, "dl": (0.4, 0.4, 0.4, 0.4), "order": "VSP",
       "ring": (2, 1, 3), "rev": -1, "xz": "SVSS", "lk2": "SS", "pra": 1.1, "half": ((0, 0), (2, 1)), "ea_": 0.7,
       "d1": (7.4, 8.4), "d2": (10.4, 11.4, 12.2, 13.4), "txz": (3.95, 4.3), "tl2": (6.0, 7.0), "e1": 0.7, "e3": 0.2, "gap": 0.3,
       "lag": 0.0, "tw": 2.7, "tl1": 3.9, "g1": (0.32,) * 5, "g2": 0.14, "rd": 0.9, "h0": (0, 0, 0, 0), "el": 0.35, "th": 0.2, "t1": 0.6, "t2": 0.2, "lt": 0, "tv": (26.2, 26.2, 26.3, 26.6), "yw": 1, "a4": 1, "tk0": 2, "tk": (3.9, 5.05, 5.5, 5.9, 6.05), "tll": 4.7, "eo": 0.7, "tc": (26.6, 27.05), "t0": 0.0, "free": (), "fev": (), "lw": (2, 2), "gp2": 0.0, "dir": 0, "ea": 21.5}
WIDE = [0, 1]
TURNS = ([(1, 2), (1, 3), (0, 0), (0, 1), (-1, 0), (-2, 0), (-1, 1), (-2, 1), (2, 2), (2, 3)]
         + [(t, k) for t in (3, 4, 5) for k in range(NR)])
ORDER = [(1, 2), (1, 3)] + [(2, k) for k in range(NR)] + TURNS[-12:]
_cols = {}


def columns(name, ix):
    key = (name, repr(ix))
    if key not in _cols:
        shape = SCRATCH[name][1][1:]
        m = np.zeros(shape, bool)
        m[ix[1:]] = True
        _cols[key] = int.from_bytes(np.packbits(m.reshape(-1), bitorder="little").tobytes(), "little"), int(m.sum())
    return _cols[key]


def record(g, r, T, topo):
    cores = list(T.cores)
    others = [k for k in range(NR) if k != r]
    ring = [(r + i) % NR for i in OPT["ring"]]
    rest = lambda k: [j for j in range(NR) if j != k]
    Q = {"V": g.vector, "S": g.scalar, "P": g.tensor, "G": g, "Y": g.sync}
    V, S, P = g.vector, g.scalar, g.tensor
    ops, turn = [], [99, 0]
    cyc, GA, H, sl = PLAN["cyc"], PLAN["gth"], CH // 2, slice

    def view(name, *ix, part=sl(None)):
        ix = (part,) + ix
        bits, n = columns(name, ix)
        return T[name][ix if len(ix) > 1 else part], [(name, bits)], n, False

    def at(name, a=None, b=None, c=None):
        return view(name, sl(a, b, c)) if len(SCRATCH[name][1]) == 2 else view(name)

    def nth(name, n, i, a, b):
        return at(name, 32 * n * a + i, 32 * n * b, n)

    def gather(win, off):
        return win[0].indirect(off[0]), win[1] + off[1], 16 * off[2], True

    def add(q, fn, rd, wr, cost, sem=None, inc=16, to=None):
        rd = [x for a in rd if isinstance(a, tuple) for x in a[1]]
        wr = [x for a in wr for x in a[1]] + [x for x in rd if x[0] in BANKS]
        wr = [(n, 1) if n in BANKS else (n, m) for n, m in wr]
        ops.append({"q": q, "fn": fn, "rd": [x for x in rd if x[0] not in BANKS], "wr": wr, "cost": cost, "sem": sem,
                    "inc": inc, "to": to, "r": r, "turn": turn[0], "rush": turn[1], "tau": None})

    def cost(o, a, m=1.0):
        return 0.06 + o[2] * GA * cyc if a[3] else PLAN["fix"] + max(64, o[2] * m) * cyc

    def narrow(*x):
        return 0.5 if all(SCRATCH[a[1][0][0]][2] in (bf16, u16) for a in x) else 1.0

    ap = lambda x: x[0] if isinstance(x, tuple) else x

    def tt(o, a, b, op):
        m = 1.0 if a[1][0][0] in BANKS or b[1][0][0] in BANKS else 2.0
        add("V", lambda: V.tensor_tensor(o[0], a[0], b[0], op), [a, b], [o], cost(o, a, m))

    def ts(o, a, s1, op0, s2=None, op1=None):
        if op1 is None:
            add("V", lambda: V.tensor_scalar(o[0], a[0], ap(s1), None, op0), [a, s1], [o], cost(o, a, narrow(o, a)))
        else:
            add("V", lambda: V.tensor_scalar(o[0], a[0], ap(s1), ap(s2), op0, op1), [a, s1, s2], [o], cost(o, a, narrow(o, a)))

    def cp(o, a):
        add("V", lambda: V.tensor_copy(o[0], a[0]), [a], [o], cost(o, a, narrow(o, a)))

    def act(o, a, f=F.Copy, scale=1.0, bias=0.0):
        if f == F.Copy and (scale, bias) == (1.0, 0.0):
            add("S", lambda: S.activation(o[0], a[0], f), [a], [o], cost(o, a))
        else:
            f = F.Identity if f == F.Copy else f
            add("S", lambda: S.activation(o[0], a[0], f, bias=ap(bias), scale=ap(scale)), [a, scale, bias], [o], cost(o, a))

    def move(q, o, a):
        (cp if q == "V" else act)(o, a)

    def mm(o, terms):
        for i, (l, rh) in enumerate(terms):
            c = max(min(64, l[2]), rh[2]) * (4 if SCRATCH[l[1][0][0]][2] == f32 else 1) * PLAN["pe"]
            add("P", lambda l=l, rh=rh, i=i: P.matmul(o[0], l[0], rh[0], i == 0, i == len(terms) - 1), [l, rh], [o], c)

    def mset(o, c):
        add("V", lambda: V.memset(o[0], c), (), [o], cost(o, o, narrow(o)))

    def scan(o, d0, d1):
        add("V", lambda: V.tensor_tensor_scan(o[0], d0[0], d1[0], 0.0, A.mult, A.add), [d0, d1], [o], cost(o, o, narrow(o, d0, d1)))

    def iota(o, pat, base=0, cm=0):
        add("G", lambda: g.iota(o[0], pat, base, cm, allow_small_or_imprecise_dtypes=True), (), [o], 0.13 + 2 * o[2] * cyc)

    hbm = lambda x: (x, [], 0, False)
    lineb = (None, [("lineb", 1)], 0, False)
    line = (None, [("line", 1)], 0, False)

    def dma(q, o, a, sem, size, more=()):
        add(q, lambda: Q[q].dma_start(o[0], a[0]), [a], [o] + list(more), 0.3 + size / PLAN["bw"], sem=sem)

    def both(k, ranks):
        mask = -1
        for j in ranks:
            mask &= topo.mask(cores[k], cores[j])
        return mask

    def nin(k, ranks):
        return bin(both(k, ranks)).count("1")

    def send(o, a, ranks, sem, more=0.0):
        mask = both(r, ranks)
        ad = [topo.addr(cores[k]) for k in ranks]
        if len(ranks) == 1:
            fn = lambda: g.remote_dma(o[0], a[0], T.sem[sem], T.sem.sent, ad[0][1], ad[0][0], mask)
        else:
            fn = lambda: g.remote_dma_fused([RemoteDMATransfer(
                dst_ids=[DstId(rid=x[0], pnc=x[1]) for x in ad], dma_engine_mask=mask, remote_sem=T.sem[sem],
                src=a[0], dsts=[o[0]] * len(ranks))], local_sem=T.sem.sent)
        add("G", fn, [a], (), PLAN["rows"] + more, sem="sent", inc=nin(r, ranks), to=(ranks, sem))

    arrivals = []

    def landed(t, j, k):
        o, n = (192 * j, 192) if t == 2 and k in WIDE else (64 * (4 * (t - 1 if t < 3 else t) + j), 64)
        return at("rv", o, o + n)

    def leaving(t, k):
        o, n = (192 * k, 192) if t == 2 and k in WIDE else (128 * k + 64 * t + 64 if t < 3 else 64 * (4 * t + k), 64)
        return at("sb", o, o + n)

    def ends(k):
        if OPT["kind"][k] != "P":
            o = 224 * k + (32 if OPT["kind"][k] == "L" else 128)
            return at("fin", 224 * k, o), at("fin", o, 224 * k + 224)
        return at("fin", 224 * k, 224 * k + 32), at("fp", 192 * k - 384, 192 * k - 288), at("fp", 192 * k - 288, 192 * k - 192)
    for t, k in ORDER:
        o = ((t - 1) * 4 + k) * 64
        if k == r:
            arrivals += [(landed(t, j, r), "sh%d_%d" % (t, j), nin(j, [r])) for j in others]
        else:
            arrivals.append((at("ls", o, o + 64) if t < NS else ends(k)[0], "li%d_%d" % (t, k), nin(k, rest(k))))
    for k in others:
        arrivals.append((ends(k)[1], "fi%d" % k, nin(k, rest(k))))
        arrivals += [(x, "ea%d" % k, nin(k, rest(k))) for x in ends(k)[2:]]

    WA = OPT["WA"] * W // 8
    dma("Y", at("fi"), hbm(T.first[:]), "dfi", 2 ** 18, [line])
    dma("Y", at("sti"), hbm(T.start[:]), "dst", 2 ** 16, [line])
    dma("Y", at("fr", 0, WA), hbm(T.frag[:, 0:WA]), "dfa", 256 * WA, [line])
    dma("Y", at("fr", W, W + K), hbm(T.frag[:, 0:K]), "dfa", 2 ** 14, [line, at("fr", 0, 1)])
    dma("S", at("limi", 0, 5), hbm(T.lim[:]), "dlim", 2 ** 12)
    add("G", lambda: g.iota(T.pi[:, 0:1], [[0, 1]], 0, 1), (), [at("pi", 0, 1)], 0.13)
    iota(at("x144"), [[1, 144]])
    iota(at("x32"), [[0, 2], [1, 32]])
    iota(at("x16"), [[16, 32]])
    iota(at("s5"), [[0, 4], [1, 96]])
    iota(at("lvl"), [[-1, 5], [0, 32]], 4)

    mset(at("ax", 0, 2752), 0.0)
    act(at("ax", 2752, 5504), at("ax", 0, 2752))
    mset(at("ax", 5504, 8240), 0.0)
    cp(at("hl", 0, 512), at("fi"))
    tt(at("hl", 512, 1024), at("fi"), at("hl", 0, 512), A.subtract)
    for h in range(2):
        dma("Y", view("ax", sl(AO, AO + W), part=sl(h, None, 16)), at("hl", 512 * h, 512 * h + 512), "dax", 2 ** 17, [line, at("ax")])
    dma("Y", at("fr", WA, W), hbm(T.frag[:, WA:W]), "dfb", 256 * (W - WA), [line])
    cp(at("stu"), at("sti"))

    p0 = at("pi", 0, 1)
    for i, (sh, msk) in enumerate([(4, 7), (0, 15), (1, 7), (0, 1), (1, 31), (6, 1), (3, 1), (0, 7)]):
        ts(at("ci", i, i + 1), p0, sh, A.arith_shift_right, msk, A.bitwise_and)
    cp(at("cf", 0, 8), at("ci"))
    c = lambda i: at("cf", i, i + 1)
    cg, ci_, cpair, ch, cj, ce, ck, cq = [c(i) for i in range(8)]
    cp(c(8), p0)
    ts(c(9), cg, 16.0, A.mult, 15.0, A.add)
    ts(c(10), cpair, 0.0, A.is_equal)
    ts(c(11), cpair, 1.0, A.is_equal)
    ts(c(12), ch, -1.0, A.mult, 1.0, A.add)
    ts(c(13), ck, -1.0, A.mult, 1.0, A.add)
    ts(c(14), cg, 8.0, A.mult, cq, A.add)
    ts(c(15), cj, 3.0, A.mult, 2.0, A.add)
    ts(c(15), c(15), ce, A.subtract)
    ts(c(16), ce, 2.0, A.mult, -1.0, A.add)
    ts(c(17), ce, -1.0, A.add)
    mk, mk2 = [c(12), ch], [c(13), ck]
    ts(at("m0"), at("x144"), c(9), A.is_equal, c(10), A.mult)
    ts(at("m1"), at("x144"), c(9), A.is_equal, c(11), A.mult)
    ts(at("bo"), at("x144", 0, 8), cg, A.is_equal)
    ts(at("idf"), at("x144", 0, 128), c(8), A.is_equal, -1.0, A.mult)
    act(at("idb"), at("idf"), scale=-1.0)
    act(at("idn"), at("idf"))
    ts(at("gq"), at("x144", 0, 64), c(14), A.is_equal, -1.0, A.mult)
    mset(at("big"), 2.0 ** 26)
    for h in range(2):
        ts(at("big", 192 * h, 192 * h + 192), at("big", 192 * h, 192 * h + 192), mk[1 - h], A.mult)
    ts(at("rc"), at("s5"), c(15), A.is_equal)
    ts(at("de"), at("x32"), cj, A.is_equal)
    de = at("de", 0, 32)
    act(at("dn"), at("de"), scale=-1.0)
    act(at("dd", 0, 32), de, scale=c(16))
    act(at("dd", 32, 64), at("dd", 0, 32), scale=-1.0)
    mset(at("one"), 1.0)
    mset(at("rk"), 0.0)
    mset(at("rb"), 0.0)
    act(view("ra", sl(None), 0), de, scale=c(17))
    act(view("ra", sl(None), 1), view("ra", sl(None), 0), scale=-1.0)
    act(view("rb", sl(None), 0), view("ra", sl(None), 1))
    for u, k, x in [(4, 0, 1.0), (4, 1, 10.0), (5, 0, -1.0), (5, 1, 5.0)]:
        act(view("rk", sl(None), u, k), de, scale=x)
    act(view("rk", sl(None), 4, 2), view("ra", sl(None), 1), scale=0.5)
    cp(at("limf", 1, 6), at("limi", 0, 5))
    mset(at("limf", 0, 1), 0.0)
    for h in range(2):
        ts(view("lb", h, sl(0, 6)), at("limf", 0, 6), -1.0, A.mult, mk2[h], A.mult)
        tt(view("la", h, sl(1, 6)), view("lb", h, sl(0, 5)), view("lb", h, sl(1, 6)), A.subtract)
    ts(at("x16"), at("x16"), ci_, A.add)
    wide = r in WIDE
    tri = lambda t, a=0, b=192, c=None: at(["da", "db", "d1", "d1"][t - 1], a + 192 * (t == 4), b + 192 * (t == 4), c)
    out = lambda t, a=0, b=192, c=None: at(["sa", "sc", "so", "so"][t - 1], a + 192 * (t == 4), b + 192 * (t == 4), c)
    for t in range(3 if wide else 1, NS):
        if t != 3 or not wide:
            mset(tri(t, 96, 192, 3), -2.0 * CH)
        mset(tri(t, 97, 192, 3), 1.0 * CH)
        ts(tri(t, 98, 192, 3), at("x16"), 3.0 * CH if t == 3 and wide else 1.0 * CH, A.add)
    for l, x in enumerate([1.0, 2.0, 2.0 + 2 * wide, 2.0]):
        mset(at("slc", 32 * l, 32 * l + 32), x)
    mset(nth("y0", 5, 0, 0, 1), 0.0)
    if wide:
        for i, x in enumerate([1.0, 3.0, -2.0, 1.0]):
            mset(nth("da", 5, i, 1, 2), x * CH)
        ts(nth("da", 5, 4, 1, 2), at("x16"), 1.0 * CH, A.add)
        mset(at("db"), 0.0)
        iota(at("sc"), [[0, 2], [1, 160]])
        iota(at("x64"), [[0, 2], [1, 64]])
        ts(c(18), cj, -5.0, A.mult, -3.0, A.add)
        ts(c(19), cj, 5.0, A.mult, 4.0, A.add)
        ts(c(19), c(19), ce, A.subtract)
        ts(c(20), cj, 5.0, A.mult, 1.0, A.add)
        ts(c(21), ce, -1.0, A.mult, 1.0, A.add)
        ts(at("r1"), at("sc"), c(19), A.is_equal)
        ts(at("r2"), at("sc"), c(20), A.is_equal, c(21), A.mult)
        act(at("sa"), at("sc"), F.Abs, bias=c(18))
        ts(at("r0"), at("sa"), 1.0, A.is_le, c(21), A.mult)
        ts(at("pm"), at("x64"), c(8), A.is_equal)
        act(at("pn"), at("pm"), scale=-1.0)
    else:
        mset(tri(1, 0, 96, 3), 0.0)
    mset(view("jj", sl(0, 2)), 0.0)
    mset(view("lx", 0), 0.25)
    mset(at("sq", 0, 640, 4), 0.5)
    mset(at("sq", 0, 640, 20), -0.25)
    mset(at("rs"), 1.0)
    mset(at("rs", 0, 640, 20), 0.0)
    for name in ("h1", "xg", "c0", "v0"):
        mset(at(name), 0.0)
    mset(nth("h1", 5, 0, 0, 1), 2.0)
    mset(nth("v0", 3, 2, 0, 4), 1.0)
    mset(nth("v1", 3, 0, 0, 4), 0.0)
    mset(at("f0"), 1.0)
    mset(nth("f0", 5, 0, 0, 5), 0.0)
    mset(nth("f1", 5, 2, 0, 1), 0.0)
    mset(nth("f1", 5, 3, 4, 5), 0.0)
    mset(nth("f1", 5, 4, 0, 5), -1.0 * (OPT["kind"][r] == "P"))

    axw = at("ax", AO, AO + W)
    frw = at("fr", 0, W + K)

    def extract(o, src, n0, n, m):
        mm(o, [(at(m, 15 - i, 143 - i), at(src, n0 + i, n0 + n, 16)) for i in range(16)])

    for k in [(TURNS[0][1] + i) % NR for i in range(NR)]:
        move("SV"[k % 2], at("gx", CH * k, CH * k + CH), gather(axw, at("stu", 32 * k, 32 * k + 32)))
        ops[-1]["tau"] = 1.0
        if k % 2:
            extract(at("pa", 0, 64), "gx", CH * (k - 1), 2 * CH, "m0")
            cp(at("l0", 32 * k - 32, 32 * k + 32), at("pa", 0, 64))
            ts(at("l0", 96 + 32 * k, 160 + 32 * k), at("pa", 0, 64), float(K), A.add)
            for op in ops[-2:]:
                op["tau"] = 2.0 if k == 3 else 9 + OPT["tw"]
    for h in range(2):
        dma("Y", view("ax", sl(AO - K, AO - K + W), part=sl(2 + h, None, 16)), at("hl", 512 * h, 512 * h + 512), "day", 2 ** 17, [line, at("ax")])
        dma("Y", view("ax", sl(AO - K + W, AO + W), part=sl(2 + h, None, 16)),
            view("hl", sl(512 * h, 512 * h + K), part=sl(0, None, 16)), "day", 2 ** 10, [line, at("ax")])
    for k in WIDE:
        move(OPT["xz"][k], at("gx", CH * k, CH * k + CH), gather(axw, at("l0", 32 * k, 32 * k + 32)))
        ops[-1]["tau"] = 9 + OPT["txz"][k]
        if k % 2:
            o = 128 + 128 * k
            extract(at("px", 0, 64), "gx", CH * (k - 1), 2 * CH, "m0")
            extract(at("px", 64, 128), "gx", CH * (k - 1), 2 * CH, "m1")
            cp(at("l0", o, o + 128), at("px", 0, 128))
            ts(at("l0", o + 128, o + 256), at("px", 0, 128), float(K), A.add)

    def first(p, e, k, a=0, b=32):
        o = 128 * e + 32 * k if p == 0 else 256 + 256 * (k // 2) + 128 * e + 64 * (p - 1) + 32 * (k % 2)
        return at("l0", o + a, o + b)

    place = {}

    def vv(name, n=1, a=0, b=None, buf="v"):
        if name not in place:
            place[name] = sum(x[1] for x in place.values() if x[2] == buf), n, buf
        o, n, buf = place[name]
        return at(buf, 32 * (o + a), 32 * (o + (n if b is None else b)))

    uu = lambda name, n=1, a=0, b=None: vv(name, n, a, b, "u")

    def wl(t, k, a, b):
        o = ((t - 2) * 4 + k) * 64
        return at("ls", o + a, o + b) if t > 1 else first(0, 0, k, a, b)

    def limit(t):
        for h in range(2):
            act(view("ll", t - 1, sl(None), h), view("jj", t - 1), scale=view("la", h, sl(t, t + 1)), bias=view("lb", h, sl(t, t + 1)))

    def due(x, n=1):
        for op in ops[-n:]:
            op["tau"] = 9 + turn[0] + x

    picked = lambda k, a, b: at("ab%d" % (k % 2), (2 + k // 2) * CH + a, (2 + k // 2) * CH + b)

    def bulk(t, k):
        xs, ab, pe = "xs%d" % k, "ab%d" % (k % 2), "pe%d" % (k % 2)
        o1, x0 = ((t - 2) * 4 + k) * 32, (2 * t + (1 if k in WIDE else -1)) * CH
        n = OPT["cut"]
        w, lw = CH // n, 32 // n
        top = lambda h: picked(k, h * w, h * w + w) if t > 1 else at(xs, h * w, h * w + w)
        for h in range(n):
            if t == 1:
                act(top(h), gather(frw, at("stu", 32 * k + lw * h, 32 * k + lw * h + lw)))
            else:
                act(top(h), gather(at(xs, x0 - (5 if k in WIDE and t < NS else 3) * CH, x0), wl(t, k, 32 + lw * h, 32 + lw * h + lw)))
            due(0.16 * h - (OPT["pre"] if (k == r or t == 1) and (t, k) != (2, 2) else OPT["h0"][(k - r) % NR] * (h == 0 and t > 2)))
        if t > 1:
            ts(at("lw", o1, o1 + 32), wl(t, k, 0, 32), float(K), A.add)
            due(0.01)
        for e in range(2):
            for h in range(n):
                li = wl(t, k, lw * h, lw * h + lw)
                if e:
                    li = at("lw", o1 + lw * h, o1 + lw * h + lw) if t > 1 else first(0, 1, k, lw * h, lw * h + lw)
                x = at(xs, x0 + e * CH + h * w, x0 + e * CH + h * w + w)
                tt(x, gather(frw, li), top(h), A.add)
                due(0.18 + 0.16 * (2 * e + h))
                act(at(ab, e * CH + h * w, e * CH + h * w + w), x, F.Abs)
                due(0.34 + 0.16 * (2 * e + h))
        for a, b in ([(0, 96), (96, 128)] if OPT["pcut"] else [(0, 128)]):
            for q in range(8):
                mm(view(pe, sl(q, 64, 8), part=sl(a, b)), [(at(ab, 8 * a + q, 8 * b, 8), at("bo"))])
                due(OPT["rd"] if b == 128 else 0.75)
        hand(t, k, 64, 1 + (OPT["el"] if k == (r + 2) % NR and t > 2 else
                            OPT["e1" if (t, k) == (1, 3) else "eo" if k == r or t < 3 and (t == 1 or (k + 1) % NR == r) else "ew" if (k + 1) % NR == r else "ev"]))

    def hand(t, k, n, when):
        o = 64 + 192 * (k // 2) if n > 64 else 0
        act(leaving(t, k) if k != r else landed(t, r, r), at("pe%d" % (k % 2), o, o + n))
        due(when)
        if (t, k) in OPT["fev"]:
            ops[-1].update(tau=None, rush=4)
        if k != r:
            send(landed(t, r, k), leaving(t, k), [k], "sh%d_%d" % (t, r), 0.5 * (n > 64))
            due(when + 0.01)

    def opening(p, k):
        xs, ab, pe, o = "xs%d" % k, "ab%d" % (turn[0] % 2), "pe%d" % (k % 2), 64 + 192 * (k // 2) + 64 * p
        a0 = 2 * CH * ((turn[0] // 2 + OPT["a4"]) % 2) * (OPT["a4"] < 2)
        for h in range(2 * (p == 0)):
            act(at(xs, h * H, h * H + H), gather(frw, at("stu", 32 * k + 16 * h, 32 * k + 16 * h + 16)))
            due(0.16 * h - OPT["pra"])
        for e in range(2):
            n = 2 if (p, e) in OPT["half"] else 1
            for h in range(n):
                a, b = CH // n * h, CH // n * (h + 1)
                x = at(xs, (2 * p + e + 1) * CH + a, (2 * p + e + 1) * CH + b)
                tt(x, gather(frw, first(p, e, k, a // 16, b // 16)), at(xs, p * CH + a, p * CH + b), A.add)
                due(0.18 + 0.32 * e + 0.16 * h)
                act(at(ab, a0 + CH * e + a, a0 + CH * e + b), x, F.Abs)
                due(0.34 + 0.32 * e + 0.16 * (h + 2 - n) + OPT["lag"])
        for q in range(8):
            mm(at(pe, o + q, o + 64, 8), [(at(ab, a0 + q, a0 + 2 * CH, 8), at("bo"))])
            due(0.9 + OPT["lag"])
        if p == 2:
            hand(2, k, 192, 1 + OPT["ea_" if k < WIDE[-1] else "e3"])

    def look(t):
        n = OPT["lcut"]
        for h in range(n):
            move(OPT["look"][h % len(OPT["look"])], at("gl", CH // n * h, CH // n * (h + 1)), gather(axw, wl(t, r, 32 // n * h, 32 // n * (h + 1))))
            ops[-1]["tau"] = 9 + OPT["tl1"] if t == 1 else 5 + 4 * t + r + OPT["tk"][h] if t >= OPT["tk0"] else None
        extract(at("pa", 0, 32), "gl", 0, CH, "m0")
        extract(at("pa", 32, 64), "gl", 0, CH, "m1")
        act(tri(t, 2, 96, 3), at("pa", 0, 32))
        act(at("pb", 32 * t, 32 * t + 32), at("pa", 32, 64))
        if t > 1:
            tt(tri(t, 0, 96, 3), nth("sc", 5, 4, 0, 1) if t == 3 and wide else at("pb", 32 * (t - 1), 32 * t), at("pb", 32 * t, 32 * t + 32), A.subtract)
        tt(tri(t, 1, 96, 3), at("pb", 32 * t, 32 * t + 32), tri(t, 2, 96, 3), A.subtract)
        for i, op in enumerate(ops[-36:] if t >= OPT["tk0"] else []):
            op["tau"] = 5 + 4 * t + r + OPT["tk"][2 if i < 32 else 3 if i < 34 else 4]
        for i, op in enumerate(ops[-35:] if t == 1 else []):
            op["tau"] = 9 + OPT["tl1"] + (0.3 if i < 32 else 0.9 if i < 34 else 1.3)

    def look2():
        for p in (1, 2):
            move(OPT["lk2"][p - 1], at("gx", CH * p - CH, CH * p), gather(axw, first(p, 0, r)))
            ops[-1]["tau"] = 9 + OPT["tl2"][r] + 0.5 * p
        extract(at("pa", 0, 64), "gx", 0, 2 * CH, "m0")
        extract(at("pa", 64, 128), "gx", 0, 2 * CH, "m1")
        a1, a2, b1, b2 = [at("pa", 32 * i, 32 * i + 32) for i in range(4)]
        da, db = (lambda i: nth("da", 5, i, 0, 1)), (lambda l, i: nth("db", 5, i, l, l + 1))
        cp(db(1, 4), first(1, 0, r))
        cp(vv("z"), first(2, 0, r))
        tt(db(1, 1), vv("z"), db(1, 4), A.subtract)
        act(da(4), a1)
        act(vv("a2"), a2)
        act(db(0, 4), b1)
        tt(da(3), b1, da(4), A.subtract)
        tt(da(0), b2, vv("a2"), A.subtract)
        tt(db(0, 1), b2, db(0, 4), A.subtract)
        tt(da(2), vv("z"), db(0, 4), A.subtract)
        tt(da(1), vv("a2"), vv("z"), A.subtract)

    def decide2():
        for p in range(3):
            mm(at("pz", 64 * p, 64 * p + 64), [(view("ll", min(p, 1)), at("gq"))])
        act(at("lz"), at("pz", 0, 192), scale=-1.0)
        d, late = 0, OPT["lw"][r]
        for h in range(2):
            mm(at(("pq", "pc")[h], 0, 192), [(at("idf"), at("lz")), (at("idb"), at("big", 192 * h, 192 * h + 192))]
               + [(at("idf"), landed(2, k, r)) for k in [r] + [j for j in others if j != late]])
            due(-OPT["t2"], 2)
        for h in range(2):
            tt(view("lx", sl(1, 4), sl(None), h), landed(2, late, r), at(("pq", "pc")[h], 0, 192), A.is_gt)
        mm(at("pc", 0, 320), [(view("lx", 1 + p), at("r%d" % p)) for p in range(3)])
        ts(at("cb"), at("pc", 0, 320), 1.0, A.min)
        scan(at("sa"), at("cb"), at("da"))
        cp(wl(3, r, 0, 64), nth("sa", 5, 4, 0, 2))
        send(wl(3, r, 0, 64), wl(3, r, 0, 64), ring, "li2_%d" % r)
        due(d, 9)
        due(d + OPT["gap"], 4)
        due(d + OPT["gap"] + OPT["gp2"], 3)
        turn[:] = 99, 0
        scan(at("sc"), at("cb"), at("db"))
        act(at("wv", 32, 64), nth("sc", 5, 4, 1, 2))
        act(at("wv", 64, 96), nth("sa", 5, 4, 0, 1))
        act(at("d1", 96, 192, 3), nth("cb", 5, 2, 0, 1), scale=2.0 * CH, bias=-4.0 * CH)
        mm(at("py", 0, 128), [(at("idb"), view("lx", 2)), (at("pn"), view("lx", 1))])
        mm(at("py", 128, 256), [(at("idb"), view("lx", 3)), (at("pm"), view("lx", 1))])
        act(view("lx", 4), at("py", 0, 128), F.Relu)
        act(view("lx", 5), at("py", 128, 256), F.Relu, bias=-1.0)
        lost(2)

    bits = lambda s: [view("lx", 4), view("lx", 5)] if s == 2 and wide else [view("lx", s + 3 * (s > 2))]

    def lost(t):
        mm(at("pz", 0, 64), [(at("idn"), at("one"))] + [(x, at("de")) for x in bits(t)])
        tt(view("jj", t), at("pz", 0, 64), view("jj", t - 1), A.max)
        limit(t + 1)
        for op in ops[-2:] if OPT["tll"] else []:
            op["tau"] = 9 + 4 * t + r + OPT["tll"]

    def decide(t):
        late = ring[OPT["lt"]]
        for h in range(2):
            mm(at(("pq", "pc")[h], 0, 64), [(view("ll", t - 1), at("gq")), (at("idb"), at("big", 192 * h, 192 * h + 64))]
               + [(at("idf"), landed(t, k, r)) for k in [r] + [j for j in ring[::OPT["rev"]] if j != late]])
            due(-OPT["th" if t > 1 else "t1"], 2)
        for h in range(2):
            tt(view("lx", t + 3 * (t > 2), sl(None), h), landed(t, late, r), at(("pq", "pc")[h], 0, 64), A.is_gt)
        n = 192 if t < NS else 384
        mm(at("pc", 0, n), [(bits(t)[0], at("rc", 0, n))])
        if t < NS:
            scan(out(t), at("pc", 0, 192), tri(t))
            cp(wl(t + 1, r, 0, 64), out(t, 2, 192, 3))
            send(wl(t + 1, r, 0, 64), wl(t + 1, r, 0, 64), ring, "li%d_%d" % (t, r))
            due(0, 6)
            due(OPT["g1"][r if t > 2 else 4], 3)
            due(OPT["g1"][r if t > 2 else 4] + OPT["g2"], 2)
        else:
            m = 3 * ends(r)[0][2]
            scan(at("s5", 0, m), at("pc", 0, m), at("d5", 0, m))
            cp(ends(r)[0], at("s5", 2, m, 3))
            send(ends(r)[0], ends(r)[0], ring, "li5_%d" % r, m / 1500 - 0.15)
            due(0, 6)
            due(OPT["g1"][r], 3)
            due(OPT["g1"][r] + OPT["g2"], 2)
            turn[:] = OPT["fin"], 0
            if m < 384:
                scan(at("s5", m, 384), at("pc", m, 384), at("d5", m, 384))
            if m == 384:
                pass
            elif OPT["kind"][r] == "P":
                cp(ends(r)[2], at("s5", m + 2, 384, 3))
                for op in ops[-2:]:
                    op["tau"] = 9 + 22 + r + OPT["dl"][r] + OPT["g1"][r] + (0.01 if op is ops[-2] else OPT["g2"] + 0.01)
                send(ends(r)[2], ends(r)[2], ring, "ea%d" % r, 0.3)
            else:
                cp(at("fin", 224 * r + 32, 224 * r + 128), at("s5", m + 2, 384, 3))
                send(ends(r)[1], ends(r)[1], ring, "fi%d" % r, 0.3)
        turn[:] = 99, 0
        if t < NS:
            act(at("wv", 32 * t, 32 * t + 32), out(t, 2, 96, 3))
        if 1 < t < NS:
            lost(t)

    def books():
        al_, I, N = sl(None), at("idb"), at("idn")
        by = lambda s, x: [(b, x) for b in bits(s)]
        sub, mul, plus = A.subtract, A.mult, A.add
        mm(at("px", 0, 480), [x for s in range(5) for x in by(s, view("rk", al_, sl(4 - s, 9 - s)))])
        for k, b in enumerate([-1.0, -20.0, 0.0]):
            act(at("sq", 1 + k, 640, 4), at("px", k, 480, 3), F.Relu, bias=b)
        scan(at("ro"), at("rs"), at("sq"))
        ts(at("h0"), at("ro", 3, 640, 4), 4.0, A.is_gt)
        nc = lambda s: nth("h0", 5, s, 0, 1)
        rr = lambda s: nth("sq", 20, 4 * s + 1, 0, 1)
        for i, s, b in [(0, 1, 2.0), (0, 2, 8.0), (0, 3, 8.0), (1, 2, 6.0), (1, 3, 6.0)]:
            act(nth("h1", 5, s, i, i + 1), nth("ro", 20, 4 * s + 3 - i, 0, 1), F.Relu, scale=-2.0, bias=b)
        for i in range(2):
            scan(at("ho", 160 * i, 160 * i + 160), at("h0"), at("h1", 160 * i, 160 * i + 160))
        ts(uu("ge", 2), nth("ho", 5, 4, 0, 2), 3.0, A.is_ge)
        ts(uu("eq", 2), nth("ho", 5, 4, 0, 2), 3.0, A.is_equal)
        act(uu("mn"), nth("ho", 5, 4, 0, 1), F.Relu, scale=-1.0, bias=2.0)
        mm(at("pz", 0, 64), by(3, at("de")) + by(2, at("dd")) + by(1, at("dn")))
        act(nth("xg", 2, 1, 0, 2), at("pz", 0, 64), F.Relu, bias=-2.0)
        xa, xb = nth("xg", 2, 1, 0, 1), nth("xg", 2, 1, 1, 2)
        jc = lambda l: nth("c0", 2, 1, l - 1, l)
        act(jc(1), rr(2))
        tt(uu("r3"), rr(3), nc(3), A.is_gt)
        tt(jc(2), rr(2), rr(3), plus)
        tt(uu("r4"), rr(4), nc(4), A.is_gt)
        tt(jc(3), uu("r4"), jc(2), plus)
        tt(jc(4), uu("r4"), jc(2), plus)
        act(nth("v0", 3, 1, 1, 3), nth("c0", 2, 1, 0, 2))
        g3, g5 = uu("ge", 2, 0, 1), uu("ge", 2, 1, 2)
        mm(at("pz", 0, 32), [(N, xa), (N, xb), (I, rr(2))] + [(I, nc(s)) for s in range(1, 5)]
           + [(I, uu("r3")), (I, uu("r4")), (I, g3), (I, g5)])
        for l in range(1, 5):
            ts(nth("y0", 5, 5 - l, 0, 1), at("pz", 0, 32), 4.0 - l, A.is_le)
        for l in range(1, 5):
            mm(at("py", 64 * l - 64, 64 * l), by(l, at("ra")) + by(l + 1, at("rb")) * (l < 4)
               + [(I, at("xg", 0, 64)), (I, at("xg", 64, 128))] * (l == 1))
        scan(at("co"), at("c0"), at("py", 0, 256))
        cl = nth("co", 2, 1, 0, 4)
        slot = lambda l: [nth("co", 2, 1, l - 1, l)] + [jc(l - 1)] * 2 * (l in (2, 3)) + [jc(1), nth("cb", 5, 2, 0, 1)] * 2 * (l == 2 and wide)
        for l in range(4, 0, -1):
            mm(at("py", 260 - l, 416, 5), [(I, at("slc", 32 * l - 32, 32 * l))] + [(I, x) for x in slot(l)] + [(N, x) for x in slot(l - 1) if l > 1])
        mm(at("py", 260, 416, 5), [(I, nth("xg", 2, 0, 0, 1))])
        scan(at("y1"), at("y0"), at("py", 256, 416))
        for i in range(4):
            ts(vv("gg", 4, i, i + 1), nth("ro", 20, 19, 0, 1), 3.5 - 0.5 * i, A.is_le)
        al, g2, g3, g4 = [vv("gg", 4, i, i + 1) for i in range(4)]
        d5 = lambda l, j: nth("d5", 3, j, l, l + 1)
        gs, ka = vv("gs"), 9.0 + 2 * wide
        tt(gs, g4, at("pc", 1, 96, 3), A.is_gt)
        act(vv("m2"), al, scale=-1.0 * CH, bias=1.0 * CH)
        act(vv("n2"), al, scale=ka * CH)
        act(vv("n1"), g2, scale=(ka + 1) * CH)
        act(vv("g6"), gs, scale=3.0 * CH)
        act(vv("c3"), nth("co", 2, 1, 2, 3), scale=1.0 * CH, bias=(ka - 4) * CH)
        act(vv("gc", 3), vv("gg", 4, 0, 3), scale=1.0 * CH)
        tt(vv("m0", 2), vv("gc", 3, 0, 2), vv("gc", 3, 1, 3), sub)
        tt(vv("c3"), vv("c3"), g3, mul)
        tt(vv("g6"), vv("g6"), vv("n1"), sub)
        tt(vv("n1"), vv("n1"), vv("n2"), sub)
        tt(vv("n2"), vv("n2"), at("x16"), plus)
        tt(vv("c3"), vv("c3"), vv("g6"), plus)
        for j, m, n in [(0, vv("m0", 2, 1, 2), "c3"), (1, vv("m0", 2, 0, 1), "n1"), (2, vv("m2"), "n2")]:
            tt(vv("t%d" % j), m, nth("y1", 5, 4, 0, 1), mul)
            tt(d5(0, j), vv("t%d" % j), vv(n), plus)
        g3u = uu("ge", 2, 0, 1)
        mm(at("pz", 32, 64), [(N, uu("mn")), (N, uu("eq", 2, 0, 1)), (N, uu("eq", 2, 1, 2)), (N, nc(4)), (I, g3u)]
           + [(N, xa)] * 2 + [(N, xb)] * 3)
        act(uu("db", 2), at("pz", 0, 64))
        for l in range(5):
            mm(at("pz", 32 * l, 32 * l + 32), [(I, uu("db", 2, 0, 1))])
            mm(at("pz", 160 + 32 * l, 192 + 32 * l), [(I, uu("db", 2, 1, 2))])
        tt(nth("f0", 5, 1, 0, 5), at("pz", 0, 160), at("lvl"), A.is_equal)
        tt(nth("f0", 5, 4, 0, 5), at("pz", 0, 160), at("lvl"), A.is_le)
        act(nth("f1", 5, 0, 0, 5), at("pz", 160, 320), bias=2.0)
        plain = OPT["kind"][r] == "P"
        unit = 16.0 if plain else 4.0
        act(nth("f1", 5, 3, 0, 4), cl)
        act(nth("v1", 3, 2, 0, 4), cl, scale=float(K))
        ws = lambda a, b: at("wv", 32 * a - 32, 32 * b - 32)
        cp(ws(1, 2), first(0, 0, r))
        act(nth("v1", 3, 1, 0, 4), ws(1, 5))
        tt(nth("v1", 3, 0, 1, 3), ws(3, 5), ws(2, 4), sub)
        scan(at("vo"), at("v0"), at("v1"))
        ts(nth("f1", 5, 2, 1, 5), nth("vo", 3, 2, 0, 4), float(W), A.is_ge, -unit * W, mul)
        act(nth("f1", 5, 1, 1, 5), nth("vo", 3, 2, 0, 4), scale=unit, bias=1.0)
        ts(nth("f1", 5, 1, 0, 1), at("sti", 32 * r, 32 * r + 32), unit, mul, 1.0, plus)
        scan(at("fo"), at("f0"), at("f1"))
        cp(ends(r)[1] if plain else at("fin", 224 * r + 128, 224 * r + 224), nth("fo", 5, 4, 0, 3))
        if OPT["kind"][r] != "L":
            turn[0] = OPT["ea"]
            send(ends(r)[1], ends(r)[1], ring, "fi%d" % r, 0.3 * plain)
            turn[0] = 99
        s3, s4 = nth("fo", 5, 4, 3, 4), nth("fo", 5, 4, 4, 5)
        e0, e1 = vv("e0"), d5(1, 1)
        tt(e1, al, jc(3), mul)
        tt(e0, al, e1, sub)
        act(vv("wa"), ws(5, 6), scale=unit, bias=1.0)
        act(vv("wb", 2), ws(4, 6), scale=unit, bias=unit * K + 1.0)
        ts(vv("wt", 2), ws(4, 6), float(W - K), A.is_ge, unit * W, mul)
        tt(vv("wb", 2), vv("wb", 2), vv("wt", 2), sub)
        act(d5(1, 2), s3)
        tt(vv("p4"), g3, g4, plus)
        tt(d5(1, 0), vv("p4"), gs, sub)
        tt(vv("x0"), e0, vv("wa"), mul)
        tt(vv("xb"), g2, vv("wb", 2, 1, 2), mul)
        act(d5(3, 2), vv("x0"), bias=-1.0 * plain)
        tt(d5(3, 1), vv("xb"), vv("x0"), sub)
        act(d5(3, 0), vv("xb"), scale=-1.0)
        tt(vv("x1"), e1, vv("wa"), mul)
        tt(d5(2, 2), s4, vv("x1"), plus)
        tt(d5(2, 1), e0, vv("x1"), sub)
        act(vv("k5"), s4, bias=2.0 + plain)
        tt(vv("k5"), vv("k5"), g3, mul)
        tt(vv("sb"), vv("wb", 2, 0, 1), gs, mul)
        tt(vv("sb"), vv("sb"), g2, plus)
        tt(d5(2, 0), vv("sb"), vv("k5"), sub)

    limit(1)
    limit(2)
    (look2 if wide else look)(*[1][wide:])
    calls = [(24 - len(TURNS) + i, t, k) for i, (t, k) in enumerate(TURNS)]
    for t, k in ORDER:
        if k == r:
            calls.append((OPT["d1"][r - 2] if t == 1 else OPT["d2"][r] if t == 2 else 4 * t + k + 2 + OPT["dl"][r], t, None))
    for x, t, k in sorted(calls, key=lambda c: c[0] if c[2] is None else c[0] + 0.8):
        turn[:] = x, 0
        if k is not None:
            (opening if t < 1 else bulk)(abs(t), k)
            continue
        turn[1] = OPT["dec"]
        n0 = len(ops)
        (decide2 if t == 2 and wide else decide)(*[t][t == 2 and wide:])
        for op in ops[n0:] if (t, r) in OPT["free"] else []:
            op["tau"] = None
        turn[:] = 99, OPT["lk"]
        if t < NS - 1:
            look(t + 1)
        turn[1] = OPT["bk"]
        if t == NS - 1:
            books()
    turn[:] = 99, 0

    def levels(k, h):
        o = 192 * k + 96 * h
        a, b, d = at("ci1", o, o + 96), at("ci2", o, o + 96), at("f1", o, o + 96)
        cp(a, at("fin", 224 * k + 128 - 96 * h, 224 * k + 224 - 96 * h))
        ts(b, a, 2, A.arith_shift_right)
        ts(d, b, 12.0, A.mult, -1.0, A.add)
        tt(view("stb", sl(3 * h, 3 * h + 3), sl(32 * k, 32 * k + 32)), d, a, A.add)
        for i, op in enumerate(ops[-4:]):
            x = OPT["tc"][k - 2] - OPT["t0"] * (i == 0) if OPT["kind"][k] == "C" and h else OPT["tv"][k]
            op["tau"] = 9 + max(x, 22.95 + r) + 0.01 * i + 0.001 * (2 * k + h)
    for k in range(NR):
        if OPT["kind"][k] != "P":
            levels(k, 0)
        else:
            act(view("stb", sl(0, 3), sl(32 * k, 32 * k + 32)), ends(k)[1])
            ops[-1]["tau"] = 9 + max(OPT["tv"][k], 22.95 + r)
    dma("Y", hbm(T.stk[:, 0:384]), view("stb", sl(0, 3)), "dk0", 196608, [line])
    for k in range(NR):
        xs = at("xs%d" % k, 0, (13 if k in WIDE else 11) * CH)
        act(picked(k, 0, H), gather(xs, at("fin", 224 * k, 224 * k + 16)))
        cp(picked(k, H, CH), gather(xs, at("fin", 224 * k + 16, 224 * k + 32)))
        turn[0] = 24 + k
        due(0, 2)
        turn[0] = 99
        dma("Y", hbm(T.y[:, CH * k:CH * k + CH]), picked(k, 0, CH), "dy%d" % k, 2 ** 18)
        if OPT["kind"][r] != "L" and k >= r - OPT["yw"]:
            ops[-1]["rd"] += ends(r)[2 * (OPT["kind"][r] == "P")][1]
        if OPT["kind"][k] != "P":
            levels(k, 1)
        else:
            act(view("stb", sl(3, 6), sl(32 * k, 32 * k + 32)), ends(k)[2])
    dma("S", hbm(T.stk[:, 384:768]), view("stb", sl(3, 6)), "dk1", 196608)
    return ops, arrivals, Q


def links(ops, arrivals):
    seen, out, far = {}, [], []
    for a, sem, cnt in arrivals:
        seen.setdefault(a[1][0][0], []).append([a[1][0][1], (sem, cnt), True])
    for n, op in enumerate(ops):
        d, f = {}, set()
        for name, bits in op["rd"]:
            for m, who, wrote in seen.get(name, []):
                if wrote and m & bits:
                    if isinstance(who, tuple):
                        f.add(who)
                    else:
                        d[who] = True
        for name, bits in op["wr"]:
            for m, who, wrote in seen.get(name, []):
                if m & bits:
                    d[who] = d.get(who, False) or ops[who]["q"] != op["q"] or (name in _SB and op["q"] in "VS")
        if op["q"] == "P":
            d = {m: w and ops[m]["q"] != "P" for m, w in d.items()}
        out.append(d)
        far.append(f)
        for name, bits in op["rd"]:
            seen.setdefault(name, []).append([bits, n, False])
        for name, bits in op["wr"]:
            seen[name] = [[m & ~bits, who, wrote] for m, who, wrote in seen.get(name, []) if m & ~bits] + [[bits, n, True]]
    return out, far


def plan(recs):
    ops, deps, sends, waits = [], [], {}, []
    for rops, arrivals, _ in recs:
        base = len(ops)
        d, f = links(rops, arrivals)
        deps += [{m + base: w for m, w in x.items()} for x in d]
        waits += f
        ops += rops
    for n, op in enumerate(ops):
        for i, k in enumerate(op["to"][0] if op["to"] else []):
            sends.setdefault((k, op["to"][1]), []).append((n, i))
    far = [[x for s, _ in f for x in sends[(op["r"], s)]] for op, f in zip(ops, waits)]
    tau, behind = {}, {}
    while len(tau) < len(ops):
        for n in range(len(ops)):
            pre = list(deps[n]) + [x for x, _ in far[n]]
            if n not in tau and all(m in tau for m in pre):
                tau[n] = max([ops[n]["tau"] or 0.0] + [tau[m] + 1e-5 for m in pre])
    for n in sorted([n for n in range(len(ops)) if ops[n]["tau"] and ops[n]["q"] in OPT["order"]], key=lambda n: (tau[n], n)):
        key = ops[n]["r"], ops[n]["q"]
        if key in behind:
            deps[n].setdefault(behind[key], False)
        behind[key] = n
    succ, left = [[] for _ in ops], []
    for n in range(len(ops)):
        pre = set(deps[n]) | {m for m, _ in far[n]}
        left.append(len(pre))
        for m in pre:
            succ[m].append(n)
    order, todo, cnt = [], [n for n in range(len(ops)) if not left[n]], list(left)
    while todo:
        order.append(todo.pop())
        for m in succ[order[-1]]:
            cnt[m] -= 1
            if not cnt[m]:
                todo.append(m)
    prio = [0.0] * len(ops)
    for n in reversed(order):
        op = ops[n]
        more = PLAN["sem"] if op["sem"] is None else PLAN["issue"] + PLAN["start"] + op["cost"] if op["to"] else PLAN["dma"]
        prio[n] = op["cost"] + more + max([prio[m] for m in succ[n]] + [0.0])
    turn = [op["turn"] for op in ops]
    for n in reversed(order):
        turn[n] = min([turn[n]] + [turn[m] for m in succ[n] if ops[m]["r"] == ops[n]["r"]])
    prio = [(ops[n]["rush"] - turn[n], prio[n]) for n in range(len(ops))]

    def once(due):
        start, end, land, free, ready, became = {}, {}, {}, {}, {}, {}
        rings, first, out, wait = [0.0] * NR, [PLAN["first"]] * NR, [[] for _ in recs], list(left)
        coming = {}
        for n in sorted(due, key=due.get):
            coming.setdefault((ops[n]["r"], ops[n]["q"]), []).append(n)

        urgent = {}
        for n in sorted(range(len(ops)), key=tau.get):
            if ops[n]["tau"]:
                urgent.setdefault((ops[n]["r"], ops[n]["q"]), []).append(n)

        def guess(n, depth):
            if n in became:
                return became[n]
            if not depth or any(x not in land for x in far[n]):
                return 1e9
            return max([land[x] for x in far[n]] + [(end[m] if w else start[m]) if m in start else guess(m, depth - 1) + w * (ops[m]["cost"] + PLAN["sem"])
                                                    for m, w in deps[n].items()])

        def release(n):
            became[n] = max([PLAN["late"] * (turn[n] >= 18)] + [end[m] if w else start[m] for m, w in deps[n].items()] + [land[x] for x in far[n]])
            ready.setdefault((ops[n]["r"], ops[n]["q"]), []).append((became[n], n))
        for n in range(len(ops)):
            if not wait[n]:
                release(n)
        while len(start) < len(ops):
            t, key = min((max(free.get(key, 0.0), min(l)[0]), key) for key, l in ready.items() if l)
            x = max([x for x in ready[key] if x[0] <= t], key=lambda x: (prio[x[1]], -x[1]))
            n, op = x[1], ops[x[1]]
            span = op["cost"] * len(op["to"][0] if op["to"] else [0]) + max(0.0, rings[key[0]] - t - PLAN["start"])
            soon = [max(t, became.get(m, due[m])) for m in coming.get((key[0], "G"), []) if op["sem"] and turn[n] == 99
                    and ops[m]["to"] and m not in start and turn[m] < 99 and became.get(m, due[m]) < t + PLAN["hold"] * span]
            if soon:
                ready[key].remove(x)
                ready[key].append((min(soon) + 0.1, n))
                continue
            line = urgent[key] = [m for m in urgent.get(key, []) if m not in start]
            soon = [e for e in [guess(m, 4) for m in line[:1] if prio[m][0] > prio[n][0]] if t < e < t + PLAN["keep"] * op["cost"]]
            if soon and not op["sem"]:
                free[key] = min(soon)
                continue
            ready[key].remove(x)
            r = op["r"]
            start[n] = t
            if op["to"]:
                free[key] = t + PLAN["issue"]
                e = max(t + PLAN["issue"] + PLAN["start"] + first[r], rings[r])
                first[r] = 0.0
                for i in range(len(op["to"][0])):
                    e += op["cost"]
                    land[(n, i)] = e + PLAN["wake"]
                rings[r] = end[n] = e
            elif op["sem"]:
                free[key] = t + 0.1
                rings[r] = max(t + PLAN["dma"], rings[r]) + op["cost"]
                end[n] = rings[r] + 0.3
            else:
                free[key] = t + op["cost"]
                end[n] = t + op["cost"] + PLAN["sem"]
            out[r].append(op)
            for m in succ[n]:
                wait[m] -= 1
                if not wait[m]:
                    release(m)
        return max(end.values()), out, became

    best = last = once({})
    for _ in range(PLAN["passes"]):
        last = once(last[2])
        best = min(best, last, key=lambda x: x[0])
    return best[1]


def rank_program(g, core, T, topo):
    r = T.rank_of(core)
    if r is None:
        return
    recs = [record(g, k, T, topo) for k in range(NR)]
    ops, Q = plan(recs)[r], recs[r][2]
    known, count, tok, waits, need = {q: {} for q in Q}, {}, [], [], set()
    for n, (op, d, f) in enumerate(zip(ops, *links(ops, recs[r][1]))):
        q, w = op["q"], {}
        for t in [tok[m] for m in d if d[m]] + [x + ({}, None) for x in f]:
            if known[q].get(t[0], 0) < t[1] and w.get(t[0], (0, 0))[1] < t[1]:
                w[t[0]] = t
        for t in w.values():
            for s, c in list(t[2].items()) + [t[:2]]:
                known[q][s] = max(known[q].get(s, 0), c)
            need.add(t[3])
        waits.append(list(w.values()))
        s = op["sem"] or q
        count[s] = count.get(s, 0) + (op["inc"] if op["sem"] else 1)
        tok.append((s, count[s], dict(known[q]), None if op["sem"] else n))
    num, at = {}, {}
    for n, op in enumerate(ops):
        q = op["q"]
        for t in waits[n]:
            if t[3] is None:
                Q[q].wait_ge(T.sem[t[0]], t[1])
            else:
                Q[q].wait_ge(T.sem["q" + t[0]], at[t[3]])
        ins = op["fn"]()
        if op["sem"] is None:
            if n in need:
                num[q] = at[n] = num.get(q, 0) + 1
                ins.then_inc(T.sem["q" + q], 1)
        elif not op["to"]:
            ins.then_inc(T.sem[op["sem"]], op["inc"])
    for s in ["dk0", "dk1", "sent"] + ["dy%d" % k for k in range(NR)]:
        g.wait_ge(T.sem[s], count[s])
